import numpy as np, ml_dtypes
CORES = [13,21,141,149]
N = 4
BF = ml_dtypes.bfloat16
def gentries(a):
    return np.ascontiguousarray(a.reshape(8, 16, -1).transpose(0, 2, 1)).reshape(8, -1)
def gtable(e):
    e = np.asarray(e); return np.ascontiguousarray(e.reshape(8, -1, 16).transpose(0, 2, 1)).reshape(128, -1).astype(np.int32)
W, L, M, B, TS, CAP = 4096, 256, 8, 2, 4, 96
R = M * B
KAPPA = (3, 29, 71, 113, 151, 197, 233, 277)
def run(x, z, v):
    tr = []
    for b in range(B):
        u = np.add.reduce(z, axis=2)
        c = np.concatenate([((u * u >> 4) + k * u + v) & (W - 1) for k in KAPPA], axis=2)
        y = np.take_along_axis(x, c[:, :, None, :], 3).reshape(N, 8, 16, M, L)
        z = np.abs(np.maximum.reduce(y, axis=3) - z)
        tr.append(c)
    return z, np.concatenate(tr, axis=2)
def starts(z, h, fr):
    halt = (~fr) & (np.add.reduce((z >= h[..., None]).astype(np.int64), axis=2) >= 9)
    slot = np.add.accumulate(halt.astype(np.int64), axis=2) - halt
    return halt & (slot < CAP)
def parts(rng):
    return rng.integers(0, 256, (N, 8, 16, W)), rng.integers(0, 256, (N, 8, 16, L)), rng.integers(0, W, (N, 8, L))
def levels(rng, x, s, v, share):
    j = rng.integers(-24, 25, (N, 8, 16, TS)); z = run(x, s, v)[0]; th = np.zeros((N, 8, 16, TS), np.int64)
    for t in range(TS):
        k = np.sort(np.sort(z - j[..., t:t + 1], axis=2)[:, :, 7], axis=2)
        n = np.minimum(np.maximum((share[..., t] * L).astype(np.int64), 1), L)
        th[..., t] = np.take_along_axis(k, (L - n)[..., None], 2) + j[..., t]
    return np.minimum(np.maximum(th, 0), 255)
def pack(x, s, v, th):
    return {"x": x.reshape(N, 128, W).astype(np.float32).astype(BF), "sd": s.reshape(N, 128, L).astype(np.float32).astype(BF),
            "v0": np.stack([gtable(a) for a in v]), "th": np.ascontiguousarray(th.reshape(N, 128, TS)).astype(np.int32)}
def shares(rng):
    return rng.choice(np.array([0.1, 0.25, 0.4, 0.6]), (N, 8, TS))
def setup_inputs(rng):
    x, s, v = parts(rng)
    return pack(x, s, v, levels(rng, x, s, v, shares(rng)))
def setup_inputs_claims(rng):
    x, s, v = parts(rng); share = rng.choice(np.array([0.2, 0.35, 0.45]), (N, 8, TS)); th = levels(rng, x, s, v, share)
    z, c = run(x, s, v); go = starts(z, th[..., 0], np.zeros((N, 8, L), bool))
    for r in range(0, N, 2):
        for g in range(8):
            j = np.nonzero(go[r + 1, g])[0]
            if len(j) == 0: j = np.arange(L)
            e = rng.choice(np.array([0, R - 1, -1]), L); e = np.where(e < 0, rng.integers(0, R, L), e)
            v[r, g] = np.where(rng.random(L) < 0.6, c[r + 1, g, e * L + rng.choice(j, L)], v[r, g])
    th[0::2] = levels(rng, x, s, v, share)[0::2]
    th[1, :, :, 1] = 255; th[:, 5, :, 2] = 255; th[2, :, :, TS - 1] = 255
    return pack(x, s, v, th)
def setup_inputs_corners(rng):
    x, s, v = parts(rng); v = np.ascontiguousarray(np.argsort(rng.random((N, 8, W)), axis=-1)[..., :L])
    pm = np.ones((N, 8), bool); pm[2:, 6:] = False
    x = np.where(pm[:, :, None, None], 255, x)
    n = rng.choice(np.array([0, 1, CAP - 1, CAP, CAP + 1, L]), (N, 8)); n[0] = 0
    n[1] = np.array([CAP, CAP + 1, L, CAP, L, CAP + 1, CAP, L]); n[2] = np.array([CAP, CAP + 1, L, CAP - 1, 1, 0, CAP, CAP])
    hot = np.argsort(np.argsort(rng.random((N, 8, L)), axis=2), axis=2) < n[:, :, None]
    k = np.where(hot, np.where(rng.random((N, 8, L)) < 0.5, 9, rng.integers(9, 17, (N, 8, L))), np.where(rng.random((N, 8, L)) < 0.5, 8, rng.integers(0, 9, (N, 8, L))))
    up = np.argsort(np.argsort(rng.random((N, 8, 16, L)), axis=2), axis=2) < k[:, :, None, :]
    tb = rng.integers(1, 256, (N, 8, 16)); tb[:, 1] = 1; tb[:, 3] = 255; tb[:, 5] = rng.choice(np.array([1, 255]), (N, 16))
    b = tb[..., None]; near = rng.random(s.shape) < 0.5
    hi = np.where(near, b, b + ((256 - b) * rng.random(s.shape)).astype(np.int64)); lo = np.where(near, b - 1, (b * rng.random(s.shape)).astype(np.int64))
    s = np.where(pm[:, :, None, None], np.where(up, hi, lo), s)
    th = levels(rng, x, s, v, shares(rng)); th[..., 0] = np.where(pm[:, :, None], tb, th[..., 0])
    return pack(x, s, v, th)
def setup_inputs_ends(rng):
    x, s, v = parts(rng); one = 1.0
    for i in range(M.bit_length() - 1): one = one * 0.5
    a = rng.random((N, 8, 1, W)); x = np.where(a < 0.4 * one, 255, np.where(a < 1.2 * one, 255 * rng.integers(0, 2, x.shape), 0))
    a = rng.random((N, 8, 1, L)); s = np.where(a < 0.35, 255, np.where(a < 0.6, 0, 255 * rng.integers(0, 2, s.shape)))
    v = np.where(rng.random(v.shape) < 0.72, (W - 1) * rng.integers(0, 2, v.shape), v)
    x[:, 1::2, :, W - 1] = 255; x[:, 0::2, :, W - 1] = 0; x[:, :, :, 0] = 255 - x[:, :, :, W - 1]
    s[:, 1::2, :, L - 1] = 255; s[:, 0::2, :, L - 1] = 0; s[:, :, :, 0] = 255 - s[:, :, :, L - 1]; s[:, 1::2, :, 5] = 255; s[:, 1::2, :, L - 4] = 255
    v[:, :, L - 1] = W - 1; v[:, :, L - 4] = W - 1; v[:, :, 5] = W - 1; v[:, :, 0] = 0
    k = rng.choice(np.array([16, 16, 12, 10, 9, 8, 8, 7, 0]), (N, 8, 1, TS)); k[:, 7, :, 0] = 12; k[:, 6, :, 0] = 0; k[:, 0, :, TS - 1] = 9; k[:, 7, :, TS - 1] = 16
    th = np.where(np.argsort(np.argsort(rng.random((N, 8, 16, TS)), axis=2), axis=2) < k, 255, 0)
    return pack(x, s, v, th)
def setup_inputs_spread(rng):
    x, s, v = parts(rng)
    x = np.minimum((np.exp2(1 + 7 * rng.random((N, 8, 1, W))) * rng.random(x.shape)).astype(np.int64), 255)
    s = np.minimum((np.exp2(1 + 7 * rng.random((N, 8, 1, L))) * rng.random(s.shape)).astype(np.int64), 255)
    v = np.minimum((W * rng.random(v.shape) ** 3).astype(np.int64), W - 1)
    return pack(x, s, v, levels(rng, x, s, v, shares(rng)))
def setup_inputs_ties(rng):
    x, s, v = parts(rng); pool = rng.integers(0, W, (8, 12)); pool[:, 0] = 0; pool[:, 1] = W - 1; h = L // 2; q = L // 4
    v = np.stack([pool[g][rng.integers(0, 12, (N, L))] for g in range(8)], axis=1)
    s[..., h:] = s[..., :h]; v[..., h:] = np.where(rng.random((N, 8, h)) < 0.5, v[..., :h], v[..., h:])
    pl = [2, 4, 7]; x[:, 2] = 255; x[:, 4] = 0; x[:, 7] = 0
    s[:, pl] = rng.integers(0, 100, (N, 3, 16, L))
    for a in range(0, N, 2):
        b = a + 1
        k = int(rng.integers(1, 4)); p = int(v[b, 2, 0])
        s[b, 2, :, k * q:(k + 1) * q] = 255; v[b, 2, k * q:(k + 1) * q] = p
        s[a, 2, :, (k - 1) * q:k * q] = rng.integers(201, 256, (16, q))
        v[a, 2, (k - 1) * q:k * q] = np.where(rng.random(q) < 0.8, p, v[a, 2, (k - 1) * q:k * q]); v[a, 2, (k - 1) * q] = p
        ln = np.append(q + rng.permutation(3 * q - 1)[:3], L - 1); e = rng.integers(201, 252, 4); pv = 16 * rng.permutation(W // 16)[:4] + 1; u = 16 * e
        s[b, 4][:, ln] = e; v[b, 4][ln] = pv
        wr = rng.permutation(q)[:4 * M]; s[a, 4][:, wr] = rng.integers(201, 252, 4 * M); s[a, 4][5, wr] += 4
        v[a, 4][wr] = np.concatenate([((u * u >> 4) + m * u + pv) & (W - 1) for m in KAPPA])
        p = W - 2 if a == 0 else int(rng.integers(W // 2, W - 1))
        for l, c in ((0, p + 1), (h, p)):
            s[b, 7, :, l] = rng.integers(201, 256, 16); u = int(np.sum(s[b, 7, :, l])); v[b, 7, l] = (c - (u * u >> 4) - KAPPA[0] * u) & (W - 1)
        for l, c in ((3, p + 1), (L - 1, p)):
            s[a, 7, :, l] = rng.integers(201, 256, 16); v[a, 7, l] = c
    th = levels(rng, x, s, v, shares(rng)); th[..., 0][:, pl] = rng.integers(100, 201, (N, 3, 16))
    return pack(x, s, v, th)
def check_inputs(d):
    bad = []
    for k, lo, hi in (("x", 0, 255), ("sd", 0, 255), ("v0", 0, W - 1), ("th", 0, 255)):
        a = np.asarray(d[k]).astype(np.float64)
        if not (np.min(a) >= lo and np.max(a) <= hi): bad.append("range of " + k)
        elif np.any(np.floor(a) != a): bad.append("whole numbers in " + k)
    return bad
def reference(x, sd, v0, th):
    X = x.astype(np.float32).astype(np.int64).reshape(N, 8, 16, W); S = sd.astype(np.float32).astype(np.int64).reshape(N, 8, 16, L)
    H = th.astype(np.int64).reshape(N, 8, 16, TS); v = np.stack([gentries(a) for a in v0]).astype(np.int64)
    fr = np.zeros((N, 8, L), bool); tr = np.zeros((N, 8, R * L), np.int64); cl = np.arange(L) * 4 // L
    for t in range(TS):
        z, c = run(X, S, v)
        tr = np.where(np.tile(fr, (1, 1, R)), tr, c)
        go = starts(z, H[..., t], fr); fr = fr | go
        back = np.zeros((N, 8, L), bool); hurt = np.zeros((N, 8, L), bool); done = np.zeros((N, 1, 1), np.int64)
        for q in range(N):
            p = q ^ (1 + t % (N - 1))
            for g in range(8):
                ln = np.nonzero(go[p, g])[0]; w = v[p, g, ln]
                mark = np.full(W, 9); np.minimum.at(mark, tr[q, g], np.where(np.tile(fr[q, g], R), np.tile(cl, R), 9))
                ok = np.nonzero(mark[w] > cl[ln])[0]
                win = np.zeros(len(ln), bool); win[ok[np.unique(w[ok], return_index=True)[1]]] = True
                back[p, g, ln[~win]] = True; done[q, 0, 0] += np.count_nonzero(win)
                if t < TS - 1: X[q, g][:, w[win]] = z[p, g][:, ln[win]]
                hit = np.zeros(W, bool); hit[w[win]] = True
                hurt[q, g] = fr[q, g] & np.any(hit[tr[q, g]].reshape(R, L), axis=0)
        fr = fr & (~back) & (~hurt)
        v = np.where(fr, v, (((v & 4095) ** 2 >> 3) + 37 * v + done) & (W - 1))
    ys = np.concatenate([v, fr.astype(np.int64)], axis=2)
    return {"yt": np.stack([gtable(a) for a in tr]).astype(np.float32), "ys": np.stack([gtable(a) for a in ys]).astype(np.float32)}

@@ -1,0 +1,693 @@
+from concourse.bass import DstId
+from concourse.mybir import AluOpType as OP, AxisListType, ActivationFunctionType as AF
+
+KAP = (3, 29, 71, 113, 151, 197, 233, 277)
+STAGES, CAP = 4, 96
+NE = 8
+DUMP = 4112
+NV, NSC = 40, 88
+SENT = 8191 * 256
+
+_F, _B, _I, _U = "float32", "bfloat16", "int32", "uint16"
+
+
+def _sb(n, d):
+    return ("sbuf", [128, n], d)
+
+
+SCRATCH = {
+    "xt": _sb(4224, _B), "D": _sb(4224, _B), "Z0": _sb(256, _B), "Z1": _sb(256, _B), "Z2": _sb(256, _B),
+    "V0": _sb(16, _I), "THI": _sb(4, _I), "NTH": _sb(4, _F),
+    "GT": _sb(2048, _B), "HM": _sb(2048, _B), "SEG": _sb(1024, _B), "G2": _sb(4096, _B),
+    "CJ": _sb(128, _F), "GJ": _sb(128, _F), "GH": _sb(128, _F), "GM": _sb(128, _F), "TJ": _sb(128, _F),
+    "IS": _sb(96, _F), "K96": _sb(96, _F), "PI": _sb(1, _I), "PT": _sb(5, _I), "PC": _sb(5, _F), "DC": _sb(8, _F),
+    "BE": _sb(8, _F), "PQ": _sb(8, _F), "KROW": _sb(8, _F), "KEQ": _sb(8, _F), "KC": _sb(4, _F), "RI": _sb(16, _F),
+    "CLSR": _sb(256, _B), "DUMPP": _sb(128, _F), "DPT": _sb(128, _F),
+    "BO": _sb(128, _B), "BOK": _sb(128, _B), "WU0": _sb(128, _B), "WU1": _sb(128, _B), "ID": _sb(128, _B), "NI": _sb(128, _B),
+    "NF4": _sb(128, _B), "M1K": _sb(128, _B), "RK1": _sb(128, _B), "RK2": _sb(128, _B), "RT1": _sb(128, _B), "RT2": _sb(128, _B),
+    "PL": _sb(1024, _B), "LP": _sb(1024, _B), "HS0": _sb(128, _B), "HS1": _sb(128, _B), "RS": _sb(2048, _B),
+    "VS0": _sb(128, _B), "VS1": _sb(128, _B), "FLX": _sb(128, _B), "KR1": _sb(128, _B), "KR2": _sb(128, _B), "KR3": _sb(128, _B),
+    "ONE": _sb(256, _B), "ZER": _sb(128, _B), "DIAG": _sb(96, _F), "HOLD": _sb(96, _F), "RST": _sb(96, _F), "OB": _sb(96, _B),
+    "R0M": _sb(96, _F), "CODE": _sb(96, _B), "DMP6": _sb(6, _F), "W6": _sb(6, _F), "K8T": _sb(256, _F), "K2T": _sb(256, _F),
+    "YLI": _sb(32, _I), "YLU": _sb(32, _U),
+    "VH0": _sb(16, _B), "VL0": _sb(16, _B), "S0F": _sb(128, _F), "S0I": _sb(128, _I),
+    "CAT": _sb(384, _F), "CH": _sb(384, _B), "CL": _sb(384, _B), "U1": _sb(128, _F), "SQ": _sb(128, _F),
+    "TA": _sb(128, _I), "T1": _sb(128, _I), "TR": _sb(256, _I), "LU": _sb(256, _U), "VCI": _sb(128, _I), "VM": _sb(128, _F),
+    "VHI": _sb(128, _B), "VLO": _sb(128, _B), "GE": _sb(256, _B), "FL": _sb(128, _B), "INC": _sb(128, _B), "OFFP": _sb(128, _B),
+    "OL": _sb(16, _U), "XF": _sb(256, _F), "XW": _sb(1024, _I), "GO": _sb(128, _B), "FR": _sb(128, _B), "NF2": _sb(128, _B),
+    "P1": _sb(256, _I), "LG": _sb(256, _I), "LGU": _sb(256, _U), "WT": _sb(384, _F), "WI": _sb(128, _I), "ZS": _sb(128, _I),
+    "ZN": _sb(128, _I), "SEL": _sb(256, _F),
+    "XR": _sb(384, _I), "VO": _sb(96, _B), "MS": _sb(512, _I), "VWIN": _sb(1024, _B),
+    "E": _sb(336, _B), "FX": _sb(1152, _F), "N3": _sb(1024, _I), "DLU": _sb(12, _U), "DN": _sb(8, _B), "HB": _sb(256, _B),
+    "VROW": _sb(256, _B), "ACOL": _sb(4, _F), "UL": _sb(48, _F), "YO": _sb(256, _F), "YS": _sb(32, _F), "FIN": _sb(96, _F),
+}
+for _k in range(8):
+    SCRATCH["PB%d" % _k] = ("psum", [128, 512], "float32")
+
+SEMAPHORES = ["qv", "qs", "qp", "qg", "dx", "dsd", "dv0", "dth", "dyt", "dys"] + [n + str(t) for t in range(STAGES) for n in ("xin", "rin", "xl", "rl")]
+
+
+def _partner(r, t):
+    return r ^ (1 + t % 3)
+
+
+def _relay(c, T, topo):
+    r = T.rank_of(c)
+    far = [T.cores[_partner(r, t)] for t in range(STAGES)]
+    far = [d for d in far if not topo.may_write(c, d)]
+    if not far:
+        return None
+    ks = [k for k in topo.cores_of(c) if k not in T.cores and topo.may_write(c, k) and all(topo.may_write(k, d) for d in far)]
+    ks.sort(key=lambda k: (topo.die(k) != topo.die(c), k))
+    return ks[0]
+
+
+def _send(g, T, topo, src, dst, out, in_, rsem, lsem):
+    eng = [e for e in topo.engines(src, dst)][:NE]
+    m = 0
+    for e in eng:
+        m |= 1 << e
+    rid, pid = topo.addr(dst, src)
+    g.remote_dma(out, in_, remote_sem=T.sem[rsem], local_sem=T.sem[lsem], pid=pid, routing_id=rid, dma_engine_mask=m)
+
+
+def _relay_program(g, core, T, topo, c):
+    r = T.rank_of(c)
+    used = []
+    for t in range(STAGES):
+        d = T.cores[_partner(r, t)]
+        if topo.may_write(c, d):
+            continue
+        g.wait_ge(T.sem["xin%d" % t], NE)
+        _send(g, T, topo, core, d, T.XR[:, 96 * t:96 * t + 96], T.XR[:, 96 * t:96 * t + 96], "xin%d" % t, "xl%d" % t)
+        g.wait_ge(T.sem["rin%d" % t], NE)
+        _send(g, T, topo, core, d, T.VWIN[:, 0:96], T.G2[:, 96 * t:96 * t + 96], "rin%d" % t, "rl%d" % t)
+        used.append(t)
+    for t in used:
+        g.wait_ge(T.sem["xl%d" % t], NE)
+        g.wait_ge(T.sem["rl%d" % t], NE)
+
+
+def rank_program(g, core, T, topo):
+    rank = T.rank_of(core)
+    if rank is None:
+        for c in T.cores:
+            if core in topo.cores_of(c) and _relay(c, T, topo) == core:
+                _relay_program(g, core, T, topo, c)
+        return
+
+    Q = {"v": g.vector, "s": g.scalar, "p": g.tensor, "g": g, "y": g.sync}
+    CNT = {"v": 0, "s": 0, "p": 0, "g": 0}
+    clk = {q: {} for q in Q}
+    acc = {}
+    idx = [0]
+
+    def X(name, a=0, b=None, st=1):
+        n = SCRATCH[name][1][1]
+        b = n if b is None else b
+        return (T[name][:, a:b:st] if st != 1 else T[name][:, a:b], [(name, a, b)])
+
+    def IND(win, off):
+        return (win[0].indirect(off[0]), win[1], off[1])
+
+    def wait(q, rec):
+        if clk[q].get(rec["sem"], 0) >= rec["val"]:
+            return
+        Q[q].wait_ge(T.sem[rec["sem"]], rec["val"])
+        for k, n in rec["snap"].items():
+            if clk[q].get(k, 0) < n:
+                clk[q][k] = n
+        clk[q][rec["sem"]] = rec["val"]
+
+    def issue(q, fn, reads, writes, sem=None, val=None, waw=True):
+        lab = q if sem is None else "dma"
+        deps = []
+        for kind, regs in (("r", reads), ("w", writes)):
+            for (nm, lo, hi) in regs:
+                ps = nm[:2] == "PB"
+                for rec in acc.get(nm, []):
+                    if not ps and (rec["hi"] <= lo or rec["lo"] >= hi):
+                        continue
+                    if rec["q"] == lab and lab != "dma":
+                        if q == "p" and ps:
+                            continue
+                        if kind == "r" and not rec["w"]:
+                            continue
+                        if kind == "w" and not waw:
+                            continue
+                        if ps and (rec["hi"] <= lo or rec["lo"] >= hi):
+                            continue
+                        deps.append(rec)
+                    elif rec["w"] or kind == "w" or ps:
+                        deps.append(rec)
+        deps.sort(key=lambda r: -r["idx"])
+        for rec in deps:
+            wait(q, rec)
+        ins = fn()
+        if sem is None:
+            CNT[q] += 1
+            ins.then_inc(T.sem["q" + q], 1)
+            s, n = "q" + q, CNT[q]
+        else:
+            s, n = sem, val
+            if ins is not None and val == 16:
+                ins.then_inc(T.sem[sem], 16)
+        snap = dict(clk[q])
+        idx[0] += 1
+        for w, regs in ((False, reads), (True, writes)):
+            for (nm, lo, hi) in regs:
+                old = acc.get(nm, [])
+                if w:
+                    old = [r for r in old if not (lo <= r["lo"] and r["hi"] <= hi)]
+                else:
+                    old = [r for r in old if r["w"] or not (r["q"] == lab and lab != "dma" and lo <= r["lo"] and r["hi"] <= hi)]
+                old.append({"lo": lo, "hi": hi, "w": w, "q": lab, "sem": s, "val": n, "snap": snap, "idx": idx[0]})
+                acc[nm] = old
+
+    def arrive(name, a, b, sem, val):
+        idx[0] += 1
+        acc.setdefault(name, []).append({"lo": a, "hi": b, "w": True, "q": "dma", "sem": sem, "val": val, "snap": {}, "idx": idx[0]})
+
+    def rd(*vs):
+        out = []
+        for v in vs:
+            if isinstance(v, tuple):
+                out += v[1]
+                if len(v) == 3:
+                    out += v[2]
+        return out
+
+    def ap(v):
+        return v[0] if isinstance(v, tuple) else v
+
+    def outs(o):
+        return o[1], (o[2] if len(o) == 3 else [])
+
+    def tt(o, a, b, op, waw=True):
+        w, r = outs(o)
+        issue("v", lambda: g.vector.tensor_tensor(ap(o), ap(a), ap(b), op), rd(a, b) + r, w, waw=waw)
+
+    def ts(o, a, s1, op0, s2=None, op1=None, waw=True):
+        def f():
+            if op1 is None:
+                return g.vector.tensor_scalar(ap(o), ap(a), ap(s1), None, op0)
+            return g.vector.tensor_scalar(ap(o), ap(a), ap(s1), ap(s2), op0, op1)
+        issue("v", f, rd(a, s1, s2), o[1], waw=waw)
+
+    def tc(o, a):
+        w, r = outs(o)
+        issue("v", lambda: g.vector.tensor_copy(ap(o), ap(a)), rd(a) + r, w)
+
+    def ms(o, c):
+        issue("v", lambda: g.vector.memset(ap(o), c), [], o[1], waw=True)
+
+    def scan(o, d0, d1, op0, op1):
+        issue("v", lambda: g.vector.tensor_tensor_scan(ap(o), ap(d0), ap(d1), 0.0, op0, op1), rd(d0, d1), o[1])
+
+    def red(o, a):
+        issue("v", lambda: g.vector.tensor_reduce(ap(o), ap(a), AxisListType.X, OP.add), rd(a), o[1])
+
+    def act(o, a, func, bias=0.0, scale=1.0):
+        issue("s", lambda: g.scalar.activation(ap(o), ap(a), func, bias=ap(bias), scale=ap(scale)), rd(a, bias, scale), o[1])
+
+    def mm(o, l, r, start, stop):
+        issue("p", lambda: g.tensor.matmul(ap(o), ap(l), ap(r), start, stop), rd(l, r), o[1])
+
+    def iota(o, pat, base=0, cm=0):
+        def f():
+            if SCRATCH[o[1][0][0]][2] == "int32":
+                return g.iota(ap(o), pat, base, cm)
+            return g.iota(ap(o), pat, base, cm, allow_small_or_imprecise_dtypes=True)
+        issue("g", f, [], o[1])
+
+    def load(q, name, a, b, src, sem):
+        v = X(name, a, b)
+        issue(q, lambda: Q[q].dma_start(v[0], src), [], v[1], sem=sem, val=16)
+
+    def store(q, dst, v, sem):
+        issue(q, lambda: Q[q].dma_start(dst, v[0]), v[1], [], sem=sem, val=16)
+
+    def col(name, j):
+        return X(name, j, j + 1)
+
+    load("s", "Z0", 0, 256, T.sd[:, :], "dsd")
+    load("y", "V0", 0, 16, T.v0[:, :], "dv0")
+    load("y", "xt", 0, 4096, T.x[:, :], "dx")
+    load("s", "THI", 0, 4, T.th[:, :], "dth")
+
+    iota(X("PI"), [[0, 1]], 0, 1)
+    iota(X("GH"), [[8, 16], [0, 8]])
+    iota(X("IS"), [[0, 6], [1, 16]])
+    iota(X("TJ"), [[16, 8], [1, 2], [0, 8]])
+    iota(X("PQ"), [[-2, 8]], 0, 1)
+    iota(X("CJ"), [[1, 128]])
+    iota(X("GJ"), [[16, 8], [0, 16]])
+    iota(X("GM"), [[16, 8], [0, 2], [1, 8]])
+    iota(X("BE"), [[2, 8]])
+    iota(X("DPT", 0, 64), [[4, 64]], 256)
+    iota(X("DPT", 64, 128), [[8, 64]], 512)
+    iota(X("CLSR"), [[1, 4], [0, 64]])
+    iota(X("K96"), [[16, 6], [0, 16]], DUMP)
+    iota(X("HM", 0, 1024), [[0, 128], [1, 8]])
+    iota(X("VWIN", 96, 1024), [[0, 928]])
+    iota(X("D"), [[0, 4224]])
+
+    for m in range(8):
+        ms(col("KROW", m), float(KAP[m]))
+    ms(X("xt", 4096, 4224), 0.0)
+    P, I16, M8, H2, G16 = [col("PC", j) for j in range(5)]
+    tc(col("PT", 0), X("PI"))
+    ts(col("PT", 1), X("PI"), 15, OP.bitwise_and)
+    ts(col("PT", 2), X("PI"), 7, OP.bitwise_and)
+    ts(col("PT", 3), X("PI"), 3, OP.logical_shift_right, 1, OP.bitwise_and)
+    ts(col("PT", 4), X("PI"), 112, OP.bitwise_and)
+    tc(X("PC"), X("PT"))
+    ts(col("DC", 0), G16, 8.0, OP.add)
+    ts(X("WU0"), X("GH"), G16, OP.is_equal)
+    ts(X("WU1"), X("GH"), col("DC", 0), OP.is_equal)
+    ts(X("KEQ"), X("IS", 0, 8), M8, OP.is_equal)
+    tt(X("KEQ"), X("KEQ"), X("KROW"), OP.mult)
+    red(col("KC", 0), X("KEQ"))
+    ts(col("KC", 1), col("KC", 0), 2.0, OP.mult)
+    tt(col("KC", 2), col("KC", 1), col("KC", 1), OP.mult)
+    ts(col("KC", 2), col("KC", 2), -1.0, OP.mult, -0.25, OP.add)
+    K2, KM = col("KC", 1), col("KC", 2)
+    for e in range(8):
+        ts(X("LP", 128 * e, 128 * e + 128), X("TJ"), col("PQ", e), OP.is_equal)
+    tc(X("VH0"), X("V0"))
+    tt(X("VL0"), X("V0"), X("VH0"), OP.subtract)
+
+    mm(X("PB0", 0, 128), X("WU0"), X("Z0", 0, 256, 2), True, False)
+    mm(X("PB0", 0, 128), X("WU1"), X("Z0", 1, 256, 2), False, True)
+    act(X("S0F"), X("PB0", 0, 128), AF.Square, bias=K2, scale=0.25)
+    act(X("CAT", 0, 128), X("PB0", 0, 128), AF.Copy)
+    act(X("SEG"), X("HM", 0, 1024), AF.Sign)
+    for e in range(8):
+        mm(X("PB1", e, 128, 8), X("LP", 128 * e, 128 * e + 128), X("VH0"), True, False)
+        mm(X("PB1", e, 128, 8), X("LP", 128 * e, 128 * e + 128), X("VL0"), False, True)
+    ts(X("S0I"), X("S0F"), KM, OP.add)
+    tc(X("VCI"), X("PB1", 0, 128))
+    tt(X("TA"), X("S0I"), X("VCI"), OP.add)
+    ts(X("TR", 0, 128), X("TA"), 4095, OP.bitwise_and)
+    tc(X("LU", 0, 128), X("TR", 0, 128))
+    ts(X("ID"), X("CJ"), P, OP.is_equal)
+    ts(X("NI"), X("CJ"), P, OP.is_equal, -1.0, OP.mult)
+    tc(X("CAT", 256, 384), X("VCI"))
+    ts(X("NTH"), X("THI"), -1.0, OP.mult, 0.5, OP.add)
+
+    ts(X("BO"), X("GJ"), G16, OP.is_equal)
+    tt(col("DC", 1), G16, M8, OP.add)
+    ts(col("DC", 2), M8, 0.0, OP.is_equal)
+    tt(col("DC", 3), G16, H2, OP.add)
+    ts(col("DC", 4), H2, -1.0, OP.mult, 1.0, OP.add)
+    ts(col("DC", 5), H2, -1.0, OP.mult)
+    ts(col("DC", 6), col("DC", 2), col("DC", 4), OP.mult, 256.0, OP.mult)
+    ts(col("DC", 7), col("DC", 2), H2, OP.mult, 256.0, OP.mult)
+    ts(X("RK1"), X("GM"), col("DC", 1), OP.is_equal)
+    act(X("RT1"), X("RK1"), AF.Identity, scale=col("DC", 5))
+    act(X("RT2"), X("NI"), AF.Identity, scale=col("DC", 4))
+    act(X("M1K"), X("NI"), AF.Copy, scale=1024.0)
+    act(X("HS0"), X("BO"), AF.Identity, scale=col("DC", 6))
+    act(X("HS1"), X("BO"), AF.Identity, scale=col("DC", 7))
+    ts(X("RI"), X("IS", 0, 16), I16, OP.is_equal)
+    ms(X("KR1"), 8.0)
+    ms(X("KR2"), 16384.0)
+    ms(X("KR3"), 2.0)
+    ms(X("ONE"), 1.0)
+    ms(X("ZER"), 0.0)
+    ts(X("BE"), X("BE"), col("DC", 3), OP.add)
+    for e in range(8):
+        ts(X("PL", 128 * e, 128 * e + 128), X("CJ"), col("BE", e), OP.is_equal, col("DC", 2), OP.mult)
+    ts(col("ACOL", 1), H2, 2.0, OP.mult)
+    ts(col("ACOL", 2), H2, 4.0, OP.mult)
+    ts(X("DUMPP", 0, 64), X("DPT", 0, 64), col("ACOL", 1), OP.add)
+    ts(X("DUMPP", 64, 128), X("DPT", 64, 128), col("ACOL", 2), OP.add)
+    ms(X("XW", 0, 96), SENT)
+    tt(X("RK2"), X("RT1"), X("RT2"), OP.add)
+
+    def consts_verdict():
+        ts(X("DIAG"), X("IS"), I16, OP.is_equal)
+        ts(X("HOLD"), X("IS"), 0.0, OP.is_gt)
+        act(X("OB"), X("DIAG"), AF.Copy, bias=57344.0, scale=-65536.0)
+        act(X("BOK"), X("BO"), AF.Copy, scale=8192.0)
+        ts(X("R0M"), X("IS"), 0.0, OP.is_equal)
+        ts(X("RST"), X("K96"), I16, OP.add)
+        tc(X("DMP6"), X("RST", 0, 96, 16))
+        tt(X("RST"), X("RST"), X("R0M"), OP.mult)
+        for k in range(6):
+            act(X("CODE", 16 * k, 16 * k + 16), X("DIAG", 16 * k, 16 * k + 16), AF.Copy, scale=float(16 ** k))
+            ms(col("W6", k), float(2 * 16 ** k))
+        ms(X("FX", 900, 948, 4), 8192.0)
+
+    def consts_back():
+        for i in range(16):
+            act(X("RS", 128 * i, 128 * i + 128), X("BO"), AF.Identity, scale=col("RI", i))
+        act(X("VS0"), X("WU0"), AF.Identity, scale=col("RI", 0))
+        act(X("VS1"), X("WU1"), AF.Identity, scale=col("RI", 0))
+
+    def consts_out():
+        for e in range(16):
+            act(X("K8T", 16 * e, 16 * e + 16), X("IS", 0, 16), AF.Copy, bias=float(8 * KAP[e % 8]), scale=0.0)
+        act(X("K2T"), X("K8T"), AF.Square, scale=0.25)
+        act(X("K2T"), X("K2T"), AF.Copy, bias=-0.25, scale=-1.0)
+        ms(X("YLI"), 0)
+        ts(X("YLI", 0, 8), X("YLI", 0, 8), I16, OP.add)
+        ts(X("YLI", 8, 16), X("YLI", 8, 16), I16, OP.add, 16.0, OP.add)
+        ts(X("YLI", 16, 32), X("YLI", 16, 32), I16, OP.add)
+        tc(X("YLU"), X("YLI"))
+
+    def gs(b, bt):
+        l0 = 128 * bt
+        c0 = 128 * b + l0 // 2
+        act(X("GT", 8 * l0, 8 * (l0 + NSC)), IND(X("xt"), X("LU", c0, c0 + NSC // 2)), AF.Copy)
+
+    def gv(b, bt):
+        l0 = 128 * bt + NSC
+        c0 = 128 * b + l0 // 2
+        tc(X("GT", 8 * l0, 8 * (l0 + NV)), IND(X("xt"), X("LU", c0, c0 + NV // 2)))
+
+    def smax(bt):
+        a = 1024 * bt
+        scan(X("HM", a, a + 1024), X("SEG"), X("GT", a, a + 1024), OP.mult, OP.max)
+
+    def diff(bt, zin):
+        l0 = 128 * bt
+        pb = "PB%d" % bt
+        mm(X(pb, 0, 128), X("NI"), X(zin, l0, l0 + 128), True, False)
+        mm(X(pb, 0, 128), X("ID"), X("HM", 8 * l0 + 7, 8 * l0 + 1024, 8), False, True)
+
+    def absz(bt, zout):
+        l0 = 128 * bt
+        act(X(zout, l0, l0 + 128), X("PB%d" % bt, 0, 128), AF.Abs)
+
+    def usum(bt):
+        l0, c0 = 128 * bt, 64 * bt
+        pb = "PB%d" % bt
+        mm(X(pb, 128, 192), X("WU0"), X("Z1", l0, l0 + 128, 2), True, False)
+        mm(X(pb, 128, 192), X("WU1"), X("Z1", l0 + 1, l0 + 128, 2), False, True)
+        act(X("SQ", c0, c0 + 64), X(pb, 128, 192), AF.Square, bias=K2, scale=0.25)
+        act(X("U1", c0, c0 + 64), X(pb, 128, 192), AF.Copy)
+
+    def list1(bt):
+        c0 = 64 * bt
+        tt(X("T1", c0, c0 + 64), X("SQ", c0, c0 + 64), X("VM", c0, c0 + 64), OP.add)
+        ts(X("TR", 128 + c0, 192 + c0), X("T1", c0, c0 + 64), 4095, OP.bitwise_and)
+        tc(X("LU", 128 + c0, 192 + c0), X("TR", 128 + c0, 192 + c0))
+
+    def newv():
+        ts(X("TA"), X("WI"), col("ACOL", 0), OP.add)
+        ts(X("VCI"), X("TA"), 4095, OP.bitwise_and)
+
+    def hurt(step):
+        if step == 0:
+            tt(X("FX", 960, 966), X("DN", 0, 6), X("W6"), OP.mult)
+        elif step == 1:
+            red(col("FX", 966), X("FX", 960, 966))
+        elif step == 2:
+            ts(col("FX", 967), col("FX", 966), float(0x111111), OP.add)
+        elif step == 3:
+            ts(X("MS", 0, 256), X("N3", 512, 768), col("FX", 967), OP.add)
+        elif step == 4:
+            ts(X("MS", 256, 512), X("MS", 0, 256), 0x444444, OP.bitwise_and)
+        else:
+            ts(X("HB"), X("MS", 256, 512), 0.0, OP.is_gt)
+
+    def back(t):
+        arrive("VWIN", 0, 96, "rin%d" % t, NE)
+        act(X("VROW"), IND(X("VWIN"), X("OL")), AF.Copy)
+
+    def thaw1():
+        mm(X("PB7", 128, 256), X("ID"), X("NF2"), True, False)
+        for cl in range(4):
+            for h in range(2):
+                mm(X("PB7", 128 + 32 * cl, 160 + 32 * cl), X("WU%d" % h), X("HB", 4 * h + cl, 256, 8), False, False)
+
+    def thaw2():
+        mm(X("PB7", 128, 256), X("VS0"), X("VROW", 0, 256, 2), False, False)
+        mm(X("PB7", 128, 256), X("VS1"), X("VROW", 1, 256, 2), False, True)
+
+    def verdict_row(t, hop):
+        for i in range(16):
+            mm(X("PB7", i, 96, 16), X("RS", 128 * i, 128 * i + 128), X("DN", 0, 6), True, True)
+        act(X("VO"), X("PB7", 0, 96), AF.Copy, bias=1.0, scale=-1.0)
+        out = T.VWIN[:, 0:96] if hop in T.cores else T.G2[:, 96 * t:96 * t + 96]
+        dv = X("VO")
+        issue("g", lambda: _send(g, T, topo, core, hop, out, dv[0], "rin%d" % t, "rl%d" % t), dv[1], [], sem="rl%d" % t, val=NE)
+
+    V = X("CAT", 256, 384)
+    S6 = X("FX", 207, 288, 16)
+
+    for t in range(STAGES):
+        dst = T.cores[_partner(rank, t)]
+        hop = dst if topo.may_write(core, dst) else _relay(core, T, topo)
+        if t:
+            ts(X("TA"), X("ZN"), col("ACOL", 0), OP.add)
+            tc(IND(X("xt"), X("DLU", 6, 12)), X("N3", 896, 992))
+            ts(X("TR", 0, 128), X("TA"), 4095, OP.bitwise_and)
+            tc(X("LU", 0, 128), X("TR", 0, 128))
+        gs(0, 0)
+        gv(0, 0)
+        gs(0, 1)
+        if t:
+            ts(X("TA"), X("WI"), col("ACOL", 0), OP.add)
+            hurt(0)
+            ts(X("VCI"), X("TA"), 4095, OP.bitwise_and)
+            hurt(1)
+        ts(X("VM"), X("VCI"), KM, OP.add)
+        if t:
+            hurt(2)
+        tc(X("VHI"), X("VCI"))
+        mm(X("PB3", 0, 256), X("KR2"), X("CLSR"), True, False)
+        mm(X("PB3", 0, 256), X("KR3"), X("ONE"), False, False)
+        smax(0)
+        diff(0, "Z0")
+        absz(0, "Z1")
+        usum(0)
+        tt(X("VLO"), X("VCI"), X("VHI"), OP.subtract)
+        for h in range(2):
+            mm(X("PB3", h, 256, 2), X("HS%d" % h), X("VHI"), False, False)
+            mm(X("PB3", h, 256, 2), X("HS%d" % h), X("VLO"), False, False)
+        if t:
+            hurt(3)
+        gv(0, 1)
+        if t:
+            hurt(4)
+        smax(1)
+        diff(1, "Z0")
+        absz(1, "Z1")
+        usum(1)
+        tt(X("T1", 0, 64), X("SQ", 0, 64), X("VM", 0, 64), OP.add)
+        if t:
+            hurt(5)
+        ts(X("TR", 128, 192), X("T1", 0, 64), 4095, OP.bitwise_and)
+        tc(X("LU", 128, 192), X("TR", 128, 192))
+        gs(1, 0)
+        gv(1, 0)
+        list1(1)
+        gs(1, 1)
+        smax(0)
+        diff(0, "Z1")
+        gv(1, 1)
+        absz(0, "Z2")
+        act(X("GE", 0, 128), X("Z2", 0, 128), AF.Sign, bias=col("NTH", t))
+        if t:
+            thaw1()
+        smax(1)
+        diff(1, "Z1")
+        absz(1, "Z2")
+        act(X("GE", 128, 256), X("Z2", 128, 256), AF.Sign, bias=col("NTH", t))
+        mm(X("PB2", 0, 128), X("WU0"), X("GE", 0, 256, 2), True, False)
+        mm(X("PB2", 0, 128), X("WU1"), X("GE", 1, 256, 2), False, True)
+        if t:
+            back(t - 1)
+            thaw2()
+            ts(X("FLX"), X("PB2", 0, 128), 1.0, OP.is_lt, 65536.0, OP.mult)
+            tt(X("FL"), X("PB7", 128, 256), X("FLX"), OP.is_gt)
+        else:
+            ts(X("FL"), X("PB2", 0, 128), 1.0, OP.is_ge)
+        mm(X("PB3", 0, 128), X("ID"), X("Z2", 0, 128), False, False)
+        mm(X("PB3", 128, 256), X("ID"), X("Z2", 128, 256), False, True)
+        act(X("XF"), X("PB3", 0, 256), AF.Copy)
+        scan(X("INC"), X("FL"), X("ZER"), OP.add, OP.add)
+        mm(X("PB2", 128, 256), X("KR1"), X("ONE", 0, 128), True, False)
+        mm(X("PB2", 128, 256), X("RK2"), X("FL"), False, False)
+        mm(X("PB2", 128, 256), X("M1K"), X("FL"), False, False)
+        mm(X("PB2", 128, 256), X("RK1"), X("INC"), False, True)
+        if t:
+            ts(X("FR"), X("PB7", 128, 256), 0.0, OP.is_equal)
+        tt(X("OFFP"), X("PB2", 128, 256), X("DUMPP"), OP.min)
+        if t:
+            ts(X("NF4"), X("PB7", 128, 256), 0.0, OP.is_gt, 4096.0, OP.mult)
+        for e in range(8):
+            mm(X("PB2", 256, 272), X("PL", 128 * e, 128 * e + 128), X("OFFP", e, 128, 8), e == 0, e == 7)
+        tc(X("OL"), X("PB2", 256, 272))
+        tc(IND(X("XW"), X("OL")), X("XF"))
+        sv = X("XW", 0, 96)
+        issue("g", lambda: _send(g, T, topo, core, hop, T.XR[:, 96 * t:96 * t + 96], sv[0], "xin%d" % t, "xl%d" % t),
+              sv[1], [], sem="xl%d" % t, val=NE)
+        if t == 0:
+            consts_verdict()
+        ts(X("GO"), X("OFFP"), 95.5, OP.is_ge, 4096.0, OP.mult)
+        if t == 0:
+            for b in range(2):
+                tt(X("LG", 128 * b, 128 * b + 128), X("TR", 128 * b, 128 * b + 128), X("GO"), OP.add)
+            ts(X("NF2"), X("GO"), 1.0, OP.mult)
+        else:
+            for b in range(2):
+                tt(X("LG", 128 * b, 128 * b + 128), X("LG", 128 * b, 128 * b + 128), X("NF4"), OP.add)
+                tt(X("P1", 128 * b, 128 * b + 128), X("TR", 128 * b, 128 * b + 128), X("GO"), OP.add)
+            tt(X("SEL", 0, 128), V, X("VCI"), OP.subtract)
+            tt(X("LG"), X("LG"), X("P1"), OP.min)
+            tt(X("SEL", 0, 128), X("SEL", 0, 128), X("FR"), OP.mult)
+            tt(X("NF2"), X("GO"), X("NF4"), OP.min)
+        ts(X("LGU"), X("LG"), 4096.0, OP.min)
+        if t:
+            tt(V, X("SEL", 0, 128), X("VCI"), OP.add)
+            tt(X("SEL", 128, 256), X("CAT", 128, 256), X("U1"), OP.subtract)
+            tc(IND(X("D"), X("DLU", 0, 6)), X("ZER", 0, 96))
+            tt(X("SEL", 128, 256), X("SEL", 128, 256), X("FR"), OP.mult)
+            if t < STAGES - 1:
+                ms(X("XW", 0, 96), SENT)
+            tt(X("CAT", 128, 256), X("SEL", 128, 256), X("U1"), OP.add)
+        else:
+            act(X("CAT", 128, 256), X("U1"), AF.Copy)
+            ms(X("XW", 0, 96), SENT)
+        act(X("WT", 0, 128), V, AF.Square)
+        act(X("WT", 128, 256), V, AF.Copy, scale=37.0)
+        act(X("WT", 0, 128), X("WT", 0, 128), AF.Copy, bias=-0.25, scale=0.125)
+        tt(X("WI"), X("WT", 0, 128), X("WT", 128, 256), OP.add)
+        if t < STAGES - 1:
+            tt(X("ZS"), X("WI"), X("S0I"), OP.add)
+            ts(X("ZN"), X("ZS"), 4095, OP.bitwise_and)
+        if t == 0:
+            consts_back()
+            consts_out()
+        arrive("XR", 96 * t, 96 * t + 96, "xin%d" % t, NE)
+        XR = X("XR", 96 * t, 96 * t + 96)
+        Y1 = X("N3", 800, 896)
+        ts(Y1, XR, 8, OP.logical_shift_right, 8191, OP.bitwise_and)
+        tt(X("FX", 0, 96), Y1, X("DIAG"), OP.mult)
+        scan(X("FX", 96, 192), X("HOLD"), X("FX", 0, 96), OP.mult, OP.add)
+        pos = []
+        o = 96
+        for k in range(5):
+            n = 80 - 16 * k
+            ts(X("E", o, o + n), X("N3", 816 + 16 * k, 896), col("FX", 96 + 16 * k + 15), OP.is_equal)
+            pos.append((o, n))
+            o += n
+        tt(X("E", 0, 96), Y1, X("FX", 96, 192), OP.is_equal)
+        mm(X("PB4", 0, 96), X("ID"), X("OB"), True, False)
+        for (o, n) in pos:
+            mm(X("PB4", 96 - n, 96), X("BOK"), X("E", o, o + n), False, False)
+        mm(X("PB4", 0, 96), X("BOK"), X("E", 0, 96), False, True)
+        tt(X("FX", 0, 96), X("PB4", 0, 96), Y1, OP.add)
+        scan(X("FX", 192, 288), X("RST"), X("FX", 0, 96), OP.max, OP.min)
+        ts(X("DLU", 0, 6), S6, -1.0, OP.add)
+        tc(IND(X("D"), X("DLU", 0, 6)), X("CODE"))
+
+        def piece(q, b, k0, k1):
+            o, i = X("G2", 2048 * b + 512 * k0, 2048 * b + 512 * k1), IND(X("D"), X("LGU", 128 * b + 32 * k0, 128 * b + 32 * k1))
+            if q == "v":
+                tc(o, i)
+            else:
+                act(o, i, AF.Copy)
+
+        def sums(b, k0, k1):
+            for cl in range(k0, k1):
+                for m in range(8):
+                    o = X("PB7", 0, 64) if b and cl == 3 else X("PB%d" % (5 + b), cl, 256, 4)
+                    mm(o, X("ID"), X("G2", 2048 * b + 512 * cl + m, 2048 * b + 512 * cl + 512, 8), m == 0, m == 7)
+
+        mm(X("PB6", 3, 256, 4), X("ID"), X("ZER", 0, 64), True, True)
+        piece("v", 0, 0, 2)
+        piece("s", 0, 2, 4)
+        piece("v", 1, 0, 1)
+        piece("s", 1, 1, 3)
+        piece("s", 1, 3, 4)
+        sums(0, 0, 2)
+        sums(0, 2, 4)
+        sums(1, 0, 1)
+        sums(1, 1, 3)
+        sums(1, 3, 4)
+        ts(X("MS", 0, 96), XR, 21, OP.logical_shift_right)
+        tt(X("FX", 0, 96), X("MS", 0, 96), X("DIAG"), OP.mult)
+        scan(X("FX", 96, 192), X("HOLD"), X("FX", 0, 96), OP.mult, OP.add)
+        for cl in range(1, 4):
+            for p in (0, 4):
+                ts(X("FX", 900 + p + cl, 948, 8), X("FX", 111, 192, 16), float(cl), OP.is_ge, 8192.0, OP.mult, waw=False)
+        ts(X("FX", 990, 996), S6, 4100.0, OP.is_ge, -1.0, OP.mult)
+        ts(X("N3", 896, 992), XR, 255, OP.bitwise_and)
+        for b in range(2):
+            ts(X("MS", 256 * b, 256 * b + 256), X("PB%d" % (5 + b), 0, 256), float(0x777777), OP.add)
+            ts(X("N3", 256 * b, 256 * b + 256), X("MS", 256 * b, 256 * b + 256), 0x888888, OP.bitwise_and, 3, OP.logical_shift_right)
+        tt(X("N3", 512, 768), X("N3", 0, 256), X("N3", 256, 512), OP.add)
+        ts(X("P1", 0, 64), X("PB7", 0, 64), float(0x777777), OP.add)
+        tt(X("MS", 0, 128), X("N3", 512, 640), X("N3", 640, 768), OP.add)
+        ts(X("P1", 64, 128), X("P1", 0, 64), 0x888888, OP.bitwise_and, 3, OP.logical_shift_right)
+        tt(X("MS", 128, 192), X("MS", 0, 64), X("MS", 64, 128), OP.add)
+        tt(X("P1", 128, 160), X("P1", 64, 96), X("P1", 96, 128), OP.add)
+        tt(X("P1", 160, 176), X("P1", 128, 144), X("P1", 144, 160), OP.add)
+        tt(X("MS", 131, 192, 4), X("MS", 131, 192, 4), X("P1", 160, 176), OP.add)
+        ts(X("MS", 192, 256), X("MS", 128, 192), float(0x777777), OP.add)
+        ts(X("MS", 256, 320), X("MS", 192, 256), 0x888888, OP.bitwise_and, 3, OP.logical_shift_right)
+        tt(X("MS", 320, 352), X("MS", 256, 288), X("MS", 288, 320), OP.add)
+        tt(X("MS", 352, 368), X("MS", 320, 336), X("MS", 336, 352), OP.add)
+        tt(X("MS", 368, 376), X("MS", 352, 360), X("MS", 360, 368), OP.add)
+        for k in range(6):
+            ts(X("MS", 384 + 8 * k, 392 + 8 * k), X("MS", 368, 376), 4 * k, OP.logical_shift_right, 15, OP.bitwise_and)
+        tt(X("FX", 1000, 1048), X("MS", 384, 432), X("FX", 900, 948), OP.mult)
+        scan(X("FX", 1048, 1096), X("SEG", 0, 48), X("FX", 1000, 1048), OP.mult, OP.add)
+        vet = X("FX", 1055, 1096, 8)
+        tt(X("DN", 0, 6), vet, X("FX", 990, 996), OP.is_equal)
+        if t < STAGES - 1:
+            tt(X("FX", 972, 978), vet, S6, OP.add)
+        mm(X("PB4", 128, 134), X("ONE", 0, 128), X("DN", 0, 6), True, True)
+        if t < STAGES - 1:
+            tt(X("FX", 980, 986), X("FX", 972, 978), X("DMP6"), OP.min)
+        red(col("ACOL", 0), X("PB4", 128, 134))
+        if t < STAGES - 1:
+            ts(X("DLU", 6, 12), X("FX", 980, 986), -1.0, OP.add)
+        verdict_row(t, hop)
+        tt(X("N3", 515, 768, 4), X("N3", 515, 768, 4), X("P1", 64, 128), OP.add)
+
+    newv()
+    tc(X("VHI"), X("VCI"))
+    tt(X("VLO"), X("VCI"), X("VHI"), OP.subtract)
+    for e in range(8):
+        mm(X("PB3", 0, 16), X("PL", 128 * e, 128 * e + 128), X("VHI", e, 128, 8), e == 0, False)
+        mm(X("PB3", 0, 16), X("PL", 128 * e, 128 * e + 128), X("VLO", e, 128, 8), False, e == 7)
+    for k in range(6):
+        hurt(k)
+    thaw1()
+    tc(X("FIN", 0, 16), X("PB3", 0, 16))
+    tc(X("CH"), X("CAT"))
+    tt(X("CL"), X("CAT"), X("CH"), OP.subtract)
+    for e in range(8):
+        mm(X("PB6", 256, 304), X("PL", 128 * e, 128 * e + 128), X("CH", e, 384, 8), e == 0, False)
+        mm(X("PB6", 256, 304), X("PL", 128 * e, 128 * e + 128), X("CL", e, 384, 8), False, e == 7)
+    tc(X("UL"), X("PB6", 256, 304))
+    tt(X("FX", 288, 544), IND(X("UL", 0, 32), X("YLU", 0, 16)), X("K8T"), OP.add)
+    act(X("FX", 544, 800), X("FX", 288, 544), AF.Square, scale=0.25)
+    tt(X("FIN", 16, 32), X("UL", 32, 48), X("FIN", 0, 16), OP.subtract)
+    tt(X("FX", 288, 544), X("FX", 544, 800), X("K2T"), OP.add)
+    tt(X("MS", 0, 256), IND(X("UL", 32, 48), X("YLU", 16, 32)), X("FX", 288, 544), OP.add)
+    ts(X("MS", 256, 512), X("MS", 0, 256), 4095, OP.bitwise_and)
+    tc(X("YO"), X("MS", 256, 512))
+    store("y", T.yt[:, :], X("YO"), "dyt")
+    back(STAGES - 1)
+    thaw2()
+    ts(X("FR"), X("PB7", 128, 256), 0.0, OP.is_equal)
+    for e in range(8):
+        mm(X("PB2", 0, 16), X("PL", 128 * e, 128 * e + 128), X("FR", e, 128, 8), e == 0, e == 7)
+    tc(X("YS", 16, 32), X("PB2", 0, 16))
+    tt(X("FIN", 32, 48), X("FIN", 16, 32), X("YS", 16, 32), OP.mult)
+    tt(X("YS", 0, 16), X("FIN", 32, 48), X("FIN", 0, 16), OP.add)
+    store("y", T.ys[:, :], X("YS"), "dys")
+
+    for n, v in [("dx", 16), ("dsd", 16), ("dv0", 16), ("dth", 16), ("dyt", 16), ("dys", 16)]:
+        g.wait_ge(T.sem[n], v)
+    for q in "vspg":
+        g.wait_ge(T.sem["q" + q], CNT[q])
+    for t in range(STAGES):
+        for n in ("xin", "rin", "xl", "rl"):
+            g.wait_ge(T.sem[n + str(t)], NE)

@@ -1,12 +1,13 @@
-from concourse.bass import DstId
 from concourse.mybir import AluOpType as OP, AxisListType, ActivationFunctionType as AF
 
 KAP = (3, 29, 71, 113, 151, 197, 233, 277)
 STAGES, CAP = 4, 96
 NE = 8
 DUMP = 4112
-NV, NSC = 40, 88
-SENT = 8191 * 256
+WIN = 4352
+SENT = 1 << 23
+MAGIC = 1.5 * 2 ** 23
+NORM = (float(0x777777), 0x888888)
 
 _F, _B, _I, _U = "float32", "bfloat16", "int32", "uint16"
 
@@ -15,36 +16,41 @@ def _sb(n, d):
     return ("sbuf", [128, n], d)
 
 
+def _twos(n):
+    return 0 if n % 2 else 1 + _twos(n // 2)
+
+
+REP = [0] + [4096 >> max(_twos(KAP[m] - KAP[j]) for j in range(m)) for m in range(1, 8)]
+
 SCRATCH = {
-    "xt": _sb(4224, _B), "D": _sb(4224, _B), "Z0": _sb(256, _B), "Z1": _sb(256, _B), "Z2": _sb(256, _B),
+    "xt": _sb(WIN, _B), "D": _sb(WIN, _B), "Z0": _sb(256, _B), "Z1": _sb(256, _B), "Z2": _sb(256, _B),
     "V0": _sb(16, _I), "THI": _sb(4, _I), "NTH": _sb(4, _F),
-    "GT": _sb(2048, _B), "HM": _sb(2048, _B), "SEG": _sb(1024, _B), "G2": _sb(4096, _B),
-    "CJ": _sb(128, _F), "GJ": _sb(128, _F), "GH": _sb(128, _F), "GM": _sb(128, _F), "TJ": _sb(128, _F),
-    "IS": _sb(96, _F), "K96": _sb(96, _F), "PI": _sb(1, _I), "PT": _sb(5, _I), "PC": _sb(5, _F), "DC": _sb(8, _F),
-    "BE": _sb(8, _F), "PQ": _sb(8, _F), "KROW": _sb(8, _F), "KEQ": _sb(8, _F), "KC": _sb(4, _F), "RI": _sb(16, _F),
-    "CLSR": _sb(256, _B), "DUMPP": _sb(128, _F), "DPT": _sb(128, _F),
-    "BO": _sb(128, _B), "BOK": _sb(128, _B), "WU0": _sb(128, _B), "WU1": _sb(128, _B), "ID": _sb(128, _B), "NI": _sb(128, _B),
-    "NF4": _sb(128, _B), "M1K": _sb(128, _B), "RK1": _sb(128, _B), "RK2": _sb(128, _B), "RT1": _sb(128, _B), "RT2": _sb(128, _B),
-    "PL": _sb(1024, _B), "LP": _sb(1024, _B), "HS0": _sb(128, _B), "HS1": _sb(128, _B), "RS": _sb(2048, _B),
-    "VS0": _sb(128, _B), "VS1": _sb(128, _B), "FLX": _sb(128, _B), "KR1": _sb(128, _B), "KR2": _sb(128, _B), "KR3": _sb(128, _B),
-    "ONE": _sb(256, _B), "ZER": _sb(128, _B), "DIAG": _sb(96, _F), "HOLD": _sb(96, _F), "RST": _sb(96, _F), "OB": _sb(96, _B),
-    "R0M": _sb(96, _F), "CODE": _sb(96, _B), "DMP6": _sb(6, _F), "W6": _sb(6, _F), "K8T": _sb(256, _F), "K2T": _sb(256, _F),
-    "YLI": _sb(32, _I), "YLU": _sb(32, _U),
-    "VH0": _sb(16, _B), "VL0": _sb(16, _B), "S0F": _sb(128, _F), "S0I": _sb(128, _I),
-    "CAT": _sb(384, _F), "CH": _sb(384, _B), "CL": _sb(384, _B), "U1": _sb(128, _F), "SQ": _sb(128, _F),
-    "TA": _sb(128, _I), "T1": _sb(128, _I), "TR": _sb(256, _I), "LU": _sb(256, _U), "VCI": _sb(128, _I), "VM": _sb(128, _F),
-    "VHI": _sb(128, _B), "VLO": _sb(128, _B), "GE": _sb(256, _B), "FL": _sb(128, _B), "INC": _sb(128, _B), "OFFP": _sb(128, _B),
-    "OL": _sb(16, _U), "XF": _sb(256, _F), "XW": _sb(1024, _I), "GO": _sb(128, _B), "FR": _sb(128, _B), "NF2": _sb(128, _B),
-    "P1": _sb(256, _I), "LG": _sb(256, _I), "LGU": _sb(256, _U), "WT": _sb(384, _F), "WI": _sb(128, _I), "ZS": _sb(128, _I),
-    "ZN": _sb(128, _I), "SEL": _sb(256, _F),
-    "XR": _sb(384, _I), "VO": _sb(96, _B), "MS": _sb(512, _I), "VWIN": _sb(1024, _B),
-    "E": _sb(336, _B), "FX": _sb(1152, _F), "N3": _sb(1024, _I), "DLU": _sb(12, _U), "DN": _sb(8, _B), "HB": _sb(256, _B),
-    "VROW": _sb(256, _B), "ACOL": _sb(4, _F), "UL": _sb(48, _F), "YO": _sb(256, _F), "YS": _sb(32, _F), "FIN": _sb(96, _F),
+    "GT": _sb(2048, _B), "HM": _sb(2048, _B), "SEGM": _sb(512, _B), "G2": _sb(4096, _B),
+    "PI": _sb(1, _I), "PT": _sb(7, _I), "PC": _sb(7, _F), "DC": _sb(8, _F), "KC": _sb(8, _F), "KROW": _sb(24, _F), "KEQ": _sb(24, _F),
+    "GH": _sb(128, _F), "C8": _sb(128, _F), "TJ": _sb(128, _F), "CJ": _sb(128, _F), "GM": _sb(128, _F), "GJ": _sb(128, _F),
+    "IS": _sb(256, _F), "MK8": _sb(24, _F), "MC": _sb(8, _F), "VHL": _sb(32, _B), "VS": _sb(256, _B),
+    "WU0": _sb(128, _B), "WU1": _sb(128, _B), "WP": _sb(128, _B), "ID": _sb(128, _B), "NI": _sb(128, _B), "K4": _sb(128, _B),
+    "BO": _sb(128, _B), "BOK": _sb(128, _B), "RK1": _sb(128, _B), "RKA": _sb(128, _B), "RKF": _sb(128, _B), "OBM": _sb(128, _B),
+    "PM": _sb(128, _B), "PL": _sb(1024, _F), "HS0": _sb(128, _F), "HS1": _sb(128, _F), "KR2": _sb(128, _B), "CLSR": _sb(256, _B),
+    "ONE": _sb(128, _B), "ZER": _sb(128, _B), "RSTP": _sb(128, _F),
+    "DG": _sb(96, _F), "RS96": _sb(96, _F), "OB": _sb(96, _B), "RST": _sb(96, _F), "CODE": _sb(96, _B), "MK": _sb(112, _B),
+    "POW": _sb(6, _F), "H16": _sb(18, _F), "H7": _sb(7, _F), "SM": _sb(64, _F), "SEG4": _sb(192, _B), "SEG7": _sb(64, _B),
+    "OBL": _sb(256, _B), "RSL": _sb(256, _F),
+    "S0F": _sb(128, _F), "S0I": _sb(128, _I), "DUP0": _sb(128, _B), "DUP1": _sb(128, _B), "DT": _sb(256, _F),
+    "SQ": _sb(128, _F), "TA": _sb(128, _I), "T1": _sb(128, _I), "TR": _sb(384, _I), "LU": _sb(256, _U), "VM": _sb(128, _F),
+    "GE": _sb(256, _B), "FL": _sb(128, _B), "INC": _sb(128, _B), "OS": _sb(128, _F), "OL": _sb(16, _U),
+    "XF": _sb(256, _F), "XW": _sb(640, _I), "GO": _sb(128, _B), "FR": _sb(128, _B), "NF": _sb(128, _B), "NF32": _sb(128, _F),
+    "OC": _sb(16, _B), "OI": _sb(32, _I), "ML": _sb(32, _U), "MG": _sb(256, _B), "PR": _sb(256, _B), "HB": _sb(256, _B),
+    "LG": _sb(768, _F), "LGU": _sb(256, _U), "WS": _sb(128, _F), "WI": _sb(128, _I), "WM": _sb(128, _I), "ZS": _sb(128, _I),
+    "XR": _sb(384, _I), "VWIN": _sb(16, _B), "DNB": _sb(16, _B),
+    "Y1": _sb(96, _I), "CI": _sb(96, _I), "ZV": _sb(96, _I), "E": _sb(336, _B), "FX": _sb(640, _F), "MS": _sb(512, _I),
+    "CM": _sb(36, _F), "FD": _sb(12, _F), "SML": _sb(32, _F), "TI": _sb(12, _I), "DLU": _sb(12, _U), "ACOL": _sb(1, _F),
+    "UL": _sb(64, _F), "YQ": _sb(256, _F), "YV": _sb(256, _F), "YO": _sb(256, _F), "YS": _sb(32, _F), "FIN": _sb(48, _F),
 }
 for _k in range(8):
-    SCRATCH["PB%d" % _k] = ("psum", [128, 512], "float32")
+    SCRATCH["PB%d" % _k] = ("psum", [128, 32, 2, 8] if _k in (3, 6) else [128, 512], "float32")
 
-SEMAPHORES = ["qv", "qs", "qp", "qg", "dx", "dsd", "dv0", "dth", "dyt", "dys"] + [n + str(t) for t in range(STAGES) for n in ("xin", "rin", "xl", "rl")]
+SEMAPHORES = ["qv", "qs", "qp", "qg", "dx", "dsd", "dv0", "dth", "dz", "dyt", "dys"] + [n + str(t) for t in range(STAGES) for n in ("xin", "rin", "xl", "rl")]
 
 
 def _partner(r, t):
@@ -81,7 +87,7 @@ def _relay_program(g, core, T, topo, c):
         g.wait_ge(T.sem["xin%d" % t], NE)
         _send(g, T, topo, core, d, T.XR[:, 96 * t:96 * t + 96], T.XR[:, 96 * t:96 * t + 96], "xin%d" % t, "xl%d" % t)
         g.wait_ge(T.sem["rin%d" % t], NE)
-        _send(g, T, topo, core, d, T.VWIN[:, 0:96], T.G2[:, 96 * t:96 * t + 96], "rin%d" % t, "rl%d" % t)
+        _send(g, T, topo, core, d, T.VWIN[:, 0:16], T.G2[:, 16 * t:16 * t + 16], "rin%d" % t, "rl%d" % t)
         used.append(t)
     for t in used:
         g.wait_ge(T.sem["xl%d" % t], NE)
@@ -102,10 +108,16 @@ def rank_program(g, core, T, topo):
     acc = {}
     idx = [0]
 
+    def bits(a, b, st=1):
+        return (1 << b) - (1 << a) if st == 1 else sum(1 << j for j in range(a, b, st))
+
     def X(name, a=0, b=None, st=1):
         n = SCRATCH[name][1][1]
         b = n if b is None else b
-        return (T[name][:, a:b:st] if st != 1 else T[name][:, a:b], [(name, a, b)])
+        return (T[name][:, a:b:st] if st != 1 else T[name][:, a:b], [(name, bits(a, b, st))])
+
+    def X4(name, k0, k1, h=None):
+        return (T[name][:, k0:k1] if h is None else T[name][:, k0:k1, h, :], [(name, bits(16 * k0, 16 * k1))])
 
     def IND(win, off):
         return (win[0].indirect(off[0]), win[1], off[1])
@@ -119,26 +131,18 @@ def rank_program(g, core, T, topo):
                 clk[q][k] = n
         clk[q][rec["sem"]] = rec["val"]
 
-    def issue(q, fn, reads, writes, sem=None, val=None, waw=True):
+    def issue(q, fn, reads, writes, sem=None, val=None, inc=0):
         lab = q if sem is None else "dma"
         deps = []
         for kind, regs in (("r", reads), ("w", writes)):
-            for (nm, lo, hi) in regs:
+            for (nm, cols) in regs:
                 ps = nm[:2] == "PB"
                 for rec in acc.get(nm, []):
-                    if not ps and (rec["hi"] <= lo or rec["lo"] >= hi):
-                        continue
+                    clash = rec["cols"] & cols and (rec["w"] or kind == "w")
                     if rec["q"] == lab and lab != "dma":
-                        if q == "p" and ps:
-                            continue
-                        if kind == "r" and not rec["w"]:
-                            continue
-                        if kind == "w" and not waw:
-                            continue
-                        if ps and (rec["hi"] <= lo or rec["lo"] >= hi):
-                            continue
-                        deps.append(rec)
-                    elif rec["w"] or kind == "w" or ps:
+                        if clash and not (ps and q == "p"):
+                            deps.append(rec)
+                    elif ps or clash:
                         deps.append(rec)
         deps.sort(key=lambda r: -r["idx"])
         for rec in deps:
@@ -150,23 +154,23 @@ def rank_program(g, core, T, topo):
             s, n = "q" + q, CNT[q]
         else:
             s, n = sem, val
-            if ins is not None and val == 16:
-                ins.then_inc(T.sem[sem], 16)
+            if inc:
+                ins.then_inc(T.sem[sem], inc)
         snap = dict(clk[q])
         idx[0] += 1
         for w, regs in ((False, reads), (True, writes)):
-            for (nm, lo, hi) in regs:
+            for (nm, cols) in regs:
                 old = acc.get(nm, [])
                 if w:
-                    old = [r for r in old if not (lo <= r["lo"] and r["hi"] <= hi)]
+                    old = [r for r in old if r["cols"] & ~cols]
                 else:
-                    old = [r for r in old if r["w"] or not (r["q"] == lab and lab != "dma" and lo <= r["lo"] and r["hi"] <= hi)]
-                old.append({"lo": lo, "hi": hi, "w": w, "q": lab, "sem": s, "val": n, "snap": snap, "idx": idx[0]})
+                    old = [r for r in old if r["w"] or r["q"] != lab or lab == "dma" or r["cols"] & ~cols]
+                old.append({"cols": cols, "w": w, "q": lab, "sem": s, "val": n, "snap": snap, "idx": idx[0]})
                 acc[nm] = old
 
     def arrive(name, a, b, sem, val):
         idx[0] += 1
-        acc.setdefault(name, []).append({"lo": a, "hi": b, "w": True, "q": "dma", "sem": sem, "val": val, "snap": {}, "idx": idx[0]})
+        acc.setdefault(name, []).append({"cols": bits(a, b), "w": True, "q": "dma", "sem": sem, "val": val, "snap": {}, "idx": idx[0]})
 
     def rd(*vs):
         out = []
@@ -183,35 +187,38 @@ def rank_program(g, core, T, topo):
     def outs(o):
         return o[1], (o[2] if len(o) == 3 else [])
 
-    def tt(o, a, b, op, waw=True):
-        w, r = outs(o)
-        issue("v", lambda: g.vector.tensor_tensor(ap(o), ap(a), ap(b), op), rd(a, b) + r, w, waw=waw)
+    def tt(o, a, b, op):
+        issue("v", lambda: g.vector.tensor_tensor(ap(o), ap(a), ap(b), op), rd(a, b), o[1])
 
-    def ts(o, a, s1, op0, s2=None, op1=None, waw=True):
+    def ts(o, a, s1, op0, s2=None, op1=None):
         def f():
             if op1 is None:
                 return g.vector.tensor_scalar(ap(o), ap(a), ap(s1), None, op0)
             return g.vector.tensor_scalar(ap(o), ap(a), ap(s1), ap(s2), op0, op1)
-        issue("v", f, rd(a, s1, s2), o[1], waw=waw)
+        issue("v", f, rd(a, s1, s2), o[1])
 
     def tc(o, a):
         w, r = outs(o)
         issue("v", lambda: g.vector.tensor_copy(ap(o), ap(a)), rd(a) + r, w)
 
     def ms(o, c):
-        issue("v", lambda: g.vector.memset(ap(o), c), [], o[1], waw=True)
+        issue("v", lambda: g.vector.memset(ap(o), c), [], o[1])
 
-    def scan(o, d0, d1, op0, op1):
-        issue("v", lambda: g.vector.tensor_tensor_scan(ap(o), ap(d0), ap(d1), 0.0, op0, op1), rd(d0, d1), o[1])
+    def scan(o, d0, d1, op0, op1, init=0.0):
+        issue("v", lambda: g.vector.tensor_tensor_scan(ap(o), ap(d0), ap(d1), ap(init), op0, op1), rd(d0, d1, init), o[1])
 
     def red(o, a):
         issue("v", lambda: g.vector.tensor_reduce(ap(o), ap(a), AxisListType.X, OP.add), rd(a), o[1])
 
-    def act(o, a, func, bias=0.0, scale=1.0):
+    def act(o, a, func=AF.Copy, bias=0.0, scale=1.0):
         issue("s", lambda: g.scalar.activation(ap(o), ap(a), func, bias=ap(bias), scale=ap(scale)), rd(a, bias, scale), o[1])
 
     def mm(o, l, r, start, stop):
         issue("p", lambda: g.tensor.matmul(ap(o), ap(l), ap(r), start, stop), rd(l, r), o[1])
+
+    def msum(o, pairs):
+        for j, (l, r) in enumerate(pairs):
+            mm(o, l, r, j == 0, j == len(pairs) - 1)
 
     def iota(o, pat, base=0, cm=0):
         def f():
@@ -220,15 +227,18 @@ def rank_program(g, core, T, topo):
             return g.iota(ap(o), pat, base, cm, allow_small_or_imprecise_dtypes=True)
         issue("g", f, [], o[1])
 
+    def dma(q, out, in_, reads, writes, sem, val=16):
+        issue(q, lambda: Q[q].dma_start(out, in_), reads, writes, sem=sem, val=val, inc=16)
+
     def load(q, name, a, b, src, sem):
         v = X(name, a, b)
-        issue(q, lambda: Q[q].dma_start(v[0], src), [], v[1], sem=sem, val=16)
-
-    def store(q, dst, v, sem):
-        issue(q, lambda: Q[q].dma_start(dst, v[0]), v[1], [], sem=sem, val=16)
+        dma(q, v[0], src, [], v[1], sem)
 
     def col(name, j):
         return X(name, j, j + 1)
+
+    def const(o, c):
+        act(o, col("GH", 0), AF.Copy, bias=float(c), scale=0.0)
 
     load("s", "Z0", 0, 256, T.sd[:, :], "dsd")
     load("y", "V0", 0, 16, T.v0[:, :], "dv0")
@@ -237,454 +247,482 @@ def rank_program(g, core, T, topo):
 
     iota(X("PI"), [[0, 1]], 0, 1)
     iota(X("GH"), [[8, 16], [0, 8]])
-    iota(X("IS"), [[0, 6], [1, 16]])
+    iota(X("C8"), [[0, 16], [1, 8]])
     iota(X("TJ"), [[16, 8], [1, 2], [0, 8]])
-    iota(X("PQ"), [[-2, 8]], 0, 1)
     iota(X("CJ"), [[1, 128]])
+    iota(X("SEGM"), [[0, 64], [256, 8]])
     iota(X("GJ"), [[16, 8], [0, 16]])
     iota(X("GM"), [[16, 8], [0, 2], [1, 8]])
-    iota(X("BE"), [[2, 8]])
-    iota(X("DPT", 0, 64), [[4, 64]], 256)
-    iota(X("DPT", 64, 128), [[8, 64]], 512)
     iota(X("CLSR"), [[1, 4], [0, 64]])
-    iota(X("K96"), [[16, 6], [0, 16]], DUMP)
-    iota(X("HM", 0, 1024), [[0, 128], [1, 8]])
-    iota(X("VWIN", 96, 1024), [[0, 928]])
-    iota(X("D"), [[0, 4224]])
+    iota(X("RSTP"), [[0, 128]])
+    iota(X("RSTP", 0, 128, 8), [[16, 16]], 256, 1)
+    iota(X("D", 0, WIN // 8), [[0, WIN // 8]])
 
-    for m in range(8):
-        ms(col("KROW", m), float(KAP[m]))
-    ms(X("xt", 4096, 4224), 0.0)
-    P, I16, M8, H2, G16 = [col("PC", j) for j in range(5)]
-    tc(col("PT", 0), X("PI"))
-    ts(col("PT", 1), X("PI"), 15, OP.bitwise_and)
-    ts(col("PT", 2), X("PI"), 7, OP.bitwise_and)
-    ts(col("PT", 3), X("PI"), 3, OP.logical_shift_right, 1, OP.bitwise_and)
-    ts(col("PT", 4), X("PI"), 112, OP.bitwise_and)
-    tc(X("PC"), X("PT"))
-    ts(col("DC", 0), G16, 8.0, OP.add)
-    ts(X("WU0"), X("GH"), G16, OP.is_equal)
-    ts(X("WU1"), X("GH"), col("DC", 0), OP.is_equal)
-    ts(X("KEQ"), X("IS", 0, 8), M8, OP.is_equal)
-    tt(X("KEQ"), X("KEQ"), X("KROW"), OP.mult)
-    red(col("KC", 0), X("KEQ"))
-    ts(col("KC", 1), col("KC", 0), 2.0, OP.mult)
-    tt(col("KC", 2), col("KC", 1), col("KC", 1), OP.mult)
-    ts(col("KC", 2), col("KC", 2), -1.0, OP.mult, -0.25, OP.add)
-    K2, KM = col("KC", 1), col("KC", 2)
-    for e in range(8):
-        ts(X("LP", 128 * e, 128 * e + 128), X("TJ"), col("PQ", e), OP.is_equal)
-    tc(X("VH0"), X("V0"))
-    tt(X("VL0"), X("V0"), X("VH0"), OP.subtract)
-
-    mm(X("PB0", 0, 128), X("WU0"), X("Z0", 0, 256, 2), True, False)
-    mm(X("PB0", 0, 128), X("WU1"), X("Z0", 1, 256, 2), False, True)
-    act(X("S0F"), X("PB0", 0, 128), AF.Square, bias=K2, scale=0.25)
-    act(X("CAT", 0, 128), X("PB0", 0, 128), AF.Copy)
-    act(X("SEG"), X("HM", 0, 1024), AF.Sign)
-    for e in range(8):
-        mm(X("PB1", e, 128, 8), X("LP", 128 * e, 128 * e + 128), X("VH0"), True, False)
-        mm(X("PB1", e, 128, 8), X("LP", 128 * e, 128 * e + 128), X("VL0"), False, True)
-    ts(X("S0I"), X("S0F"), KM, OP.add)
-    tc(X("VCI"), X("PB1", 0, 128))
-    tt(X("TA"), X("S0I"), X("VCI"), OP.add)
-    ts(X("TR", 0, 128), X("TA"), 4095, OP.bitwise_and)
-    tc(X("LU", 0, 128), X("TR", 0, 128))
-    ts(X("ID"), X("CJ"), P, OP.is_equal)
-    ts(X("NI"), X("CJ"), P, OP.is_equal, -1.0, OP.mult)
-    tc(X("CAT", 256, 384), X("VCI"))
-    ts(X("NTH"), X("THI"), -1.0, OP.mult, 0.5, OP.add)
-
-    ts(X("BO"), X("GJ"), G16, OP.is_equal)
-    tt(col("DC", 1), G16, M8, OP.add)
-    ts(col("DC", 2), M8, 0.0, OP.is_equal)
-    tt(col("DC", 3), G16, H2, OP.add)
-    ts(col("DC", 4), H2, -1.0, OP.mult, 1.0, OP.add)
-    ts(col("DC", 5), H2, -1.0, OP.mult)
-    ts(col("DC", 6), col("DC", 2), col("DC", 4), OP.mult, 256.0, OP.mult)
-    ts(col("DC", 7), col("DC", 2), H2, OP.mult, 256.0, OP.mult)
-    ts(X("RK1"), X("GM"), col("DC", 1), OP.is_equal)
-    act(X("RT1"), X("RK1"), AF.Identity, scale=col("DC", 5))
-    act(X("RT2"), X("NI"), AF.Identity, scale=col("DC", 4))
-    act(X("M1K"), X("NI"), AF.Copy, scale=1024.0)
-    act(X("HS0"), X("BO"), AF.Identity, scale=col("DC", 6))
-    act(X("HS1"), X("BO"), AF.Identity, scale=col("DC", 7))
-    ts(X("RI"), X("IS", 0, 16), I16, OP.is_equal)
-    ms(X("KR1"), 8.0)
-    ms(X("KR2"), 16384.0)
-    ms(X("KR3"), 2.0)
-    ms(X("ONE"), 1.0)
+    ms(X("xt", 4096, WIN), 0.0)
     ms(X("ZER"), 0.0)
-    ts(X("BE"), X("BE"), col("DC", 3), OP.add)
-    for e in range(8):
-        ts(X("PL", 128 * e, 128 * e + 128), X("CJ"), col("BE", e), OP.is_equal, col("DC", 2), OP.mult)
-    ts(col("ACOL", 1), H2, 2.0, OP.mult)
-    ts(col("ACOL", 2), H2, 4.0, OP.mult)
-    ts(X("DUMPP", 0, 64), X("DPT", 0, 64), col("ACOL", 1), OP.add)
-    ts(X("DUMPP", 64, 128), X("DPT", 64, 128), col("ACOL", 2), OP.add)
+    ms(X("ONE"), 1.0)
+    ms(X("KR2"), 16384.0)
     ms(X("XW", 0, 96), SENT)
-    tt(X("RK2"), X("RT1"), X("RT2"), OP.add)
+    P, I16, M8, H2, G16, IH, IO = [col("PC", j) for j in range(7)]
+    for j, (sh, mk) in enumerate(((0, 127), (0, 15), (0, 7), (3, 1), (0, 112), (1, 7), (0, 1))):
+        ts(col("PT", j), X("PI"), sh, OP.logical_shift_right, mk, OP.bitwise_and)
+    tc(X("PC"), X("PT"))
+    for m in range(8):
+        const(col("KROW", m), 2 * KAP[m])
+    ts(X("WU0"), X("GH"), G16, OP.is_equal)
+    ts(X("WU1"), X("GH"), G16, OP.subtract, 8.0, OP.is_equal)
+    ts(X("MK8"), X("C8", 0, 24), M8, OP.is_equal)
+    ts(X("MC"), X("C8", 0, 8), IH, OP.is_equal)
+    tt(X("KEQ", 0, 8), X("MK8", 0, 8), X("KROW", 0, 8), OP.mult)
+    ts(X("WP"), X("TJ"), G16, OP.subtract, IO, OP.is_equal)
+    K2, KM, RA, RB, RC = [col("KC", j) for j in range(5)]
+    red(K2, X("KEQ", 0, 8))
+    ts(X("ID"), X("CJ"), P, OP.is_equal)
+    ts(col("KC", 5), K2, K2, OP.mult)
+    ts(X("NI"), X("CJ"), P, OP.is_equal, -1.0, OP.mult)
+    ts(KM, col("KC", 5), -1.0, OP.mult, -0.25, OP.add)
+    for m in range(8):
+        const(col("KROW", 8 + m), 1.0 / REP[m] if m else 0.0)
+        const(col("KROW", 16 + m), REP[m])
+
+    tc(X("VHL", 0, 16), X("V0"))
+    msum(X("PB0", 0, 128), [(X("WU%d" % h), X("Z0", h, 256, 2)) for h in range(2)])
+    tt(X("VHL", 16, 32), X("V0"), X("VHL", 0, 16), OP.subtract)
+    act(X("S0F"), X("PB0", 0, 128), AF.Square, bias=K2, scale=0.25)
+    act(X("LG", 512, 640), X("PB0", 0, 128))
+    for e in range(8):
+        ts(X("VS", e, 256, 8), X("VHL"), col("MC", e), OP.mult)
+    msum(X("PB1", 0, 128), [(X("WP"), X("VS", 128 * j, 128 * j + 128)) for j in range(2)])
+    ts(X("S0I"), X("S0F"), KM, OP.add)
+    tt(X("TA"), X("S0I"), X("PB1", 0, 128), OP.add)
+    ts(X("VM"), X("PB1", 0, 128), KM, OP.add)
+    ts(X("TR", 0, 128), X("TA"), 4095, OP.bitwise_and)
+    tc(X("TR", 256, 384), X("PB1", 0, 128))
+    tc(X("LU", 0, 128), X("TR", 0, 128))
+    for j in range(1, 8):
+        a = X("D", j * (WIN // 8), (j + 1) * (WIN // 8))
+        z = X("D", 0, WIN // 8)
+        dma("y", a[0], z[0], z[1], a[1], "dz", 7 * 16)
+
+    ts(X("NTH"), X("THI"), -1.0, OP.mult, 0.5, OP.add)
+    ts(X("BO"), X("GJ"), G16, OP.is_equal)
+    ts(X("DC", 0, 2), X("GH", 0, 16, 8), I16, OP.is_equal, 256.0, OP.mult)
+    ts(col("DC", 2), H2, -1.0, OP.mult)
+    ts(X("RK1"), X("GM"), G16, OP.subtract, M8, OP.is_equal)
+    ts(X("RKA"), X("CJ"), 8.0, OP.add, P, OP.is_equal)
+    ts(X("OBM"), X("C8"), M8, OP.not_equal, 2048.0, OP.mult)
+    for h in range(2):
+        act(X("HS%d" % h), X("BO"), AF.Identity, scale=col("DC", h))
+    act(X("RKA"), X("RKA"), AF.Identity, scale=col("DC", 2))
+    act(X("OBM"), X("OBM"), bias=1024.0)
+    act(X("K4"), X("ID"), scale=4096.0)
+    a, b = X("RKF"), X("RKA")
+    issue("g", lambda: g.affine_select(a[0], b[0], [[-1, 128]], OP.not_equal, -1024.0, 0, 1), b[1], a[1])
+    iota(X("IS"), [[0, 16], [1, 16]])
+    iota(X("RST"), [[0, 96]])
+    iota(X("RST", 0, 96, 16), [[16, 6]], DUMP, 1)
+    DMP6 = X("RST", 0, 96, 16)
+
+    def repeats(out, u):
+        act(X("DT", 0, 128), u, AF.Identity, bias=MAGIC, scale=RA)
+        act(X("DT", 128, 256), X("DT", 0, 128), AF.Identity, bias=RC, scale=RB)
+        tt(out, X("DT", 128, 256), u, OP.is_equal)
 
     def consts_verdict():
-        ts(X("DIAG"), X("IS"), I16, OP.is_equal)
-        ts(X("HOLD"), X("IS"), 0.0, OP.is_gt)
-        act(X("OB"), X("DIAG"), AF.Copy, bias=57344.0, scale=-65536.0)
-        act(X("BOK"), X("BO"), AF.Copy, scale=8192.0)
-        ts(X("R0M"), X("IS"), 0.0, OP.is_equal)
-        ts(X("RST"), X("K96"), I16, OP.add)
-        tc(X("DMP6"), X("RST", 0, 96, 16))
-        tt(X("RST"), X("RST"), X("R0M"), OP.mult)
+        tt(X("KEQ", 8, 24), X("MK8", 8, 24), X("KROW", 8, 24), OP.mult)
+        ts(col("DC", 3), M8, 2.0, OP.mult, G16, OP.add)
+        red(RA, X("KEQ", 8, 16))
+        red(RB, X("KEQ", 16, 24))
+        ts(X("PM"), X("CJ"), col("DC", 3), OP.subtract, H2, OP.is_equal)
+        ts(RC, RB, -MAGIC, OP.mult, col("MK8", 0), OP.subtract)
+        ts(X("DG"), X("IS", 0, 96), I16, OP.is_equal, 65536.0, OP.mult)
+        repeats(X("DUP0"), X("LG", 512, 640))
+        act(X("DG"), X("DG"), bias=-1.0)
+        act(X("OB"), X("DG"), bias=57343.0, scale=-1.0)
+        act(X("BOK"), X("BO"), scale=8192.0)
+        act(X("MK", 0, 96), X("DG"), bias=-0.25, scale=-0.25)
         for k in range(6):
-            act(X("CODE", 16 * k, 16 * k + 16), X("DIAG", 16 * k, 16 * k + 16), AF.Copy, scale=float(16 ** k))
-            ms(col("W6", k), float(2 * 16 ** k))
-        ms(X("FX", 900, 948, 4), 8192.0)
-
-    def consts_back():
-        for i in range(16):
-            act(X("RS", 128 * i, 128 * i + 128), X("BO"), AF.Identity, scale=col("RI", i))
-        act(X("VS0"), X("WU0"), AF.Identity, scale=col("RI", 0))
-        act(X("VS1"), X("WU1"), AF.Identity, scale=col("RI", 0))
+            s = 16.0 ** (5 - k) / 65536
+            act(X("CODE", 16 * k, 16 * k + 16), X("DG", 16 * k, 16 * k + 16), bias=s, scale=s)
+            const(col("POW", k), 16.0 ** (k - 5))
+        ms(X("NF"), 16384.0)
+        ms(X("MK", 96, 112), 0.0)
+        ms(X("RS96"), 65536.0)
+        ms(X("H16"), 16.0)
+        ms(X("H7"), 16.0)
+        ms(X("SM"), 0.0)
+        ms(X("SEG4"), 1.0)
+        ms(X("SEG7"), 1.0)
+        ms(X("DNB"), 0.0)
+        ms(X("RS96", 0, 96, 16), -1.0)
+        ms(X("H16", 0, 18, 6), 0.0)
+        ms(col("H7", 6), 3.0)
+        ms(X("SM", 6, 14, 7), NORM[0])
+        ms(col("SM", 15), NORM[0])
+        ms(X("SEG4", 0, 192, 4), 0.0)
+        for j in (0, 7, 14):
+            ms(X("SEG7", j, 64, 16), 0.0)
+        tc(X("FD", 1, 12, 2), DMP6)
 
     def consts_out():
-        for e in range(16):
-            act(X("K8T", 16 * e, 16 * e + 16), X("IS", 0, 16), AF.Copy, bias=float(8 * KAP[e % 8]), scale=0.0)
-        act(X("K2T"), X("K8T"), AF.Square, scale=0.25)
-        act(X("K2T"), X("K2T"), AF.Copy, bias=-0.25, scale=-1.0)
-        ms(X("YLI"), 0)
-        ts(X("YLI", 0, 8), X("YLI", 0, 8), I16, OP.add)
-        ts(X("YLI", 8, 16), X("YLI", 8, 16), I16, OP.add, 16.0, OP.add)
-        ts(X("YLI", 16, 32), X("YLI", 16, 32), I16, OP.add)
-        tc(X("YLU"), X("YLI"))
+        for e in range(8):
+            act(X("PL", 128 * e, 128 * e + 128), X("PM"), AF.Identity, scale=col("MK8", e))
+        ts(X("OBL"), X("IS"), I16, OP.not_equal)
+        ms(X("RSL"), 0.0)
+        ms(X("RSL", 0, 256, 16), 1.0)
 
-    def gs(b, bt):
-        l0 = 128 * bt
-        c0 = 128 * b + l0 // 2
-        act(X("GT", 8 * l0, 8 * (l0 + NSC)), IND(X("xt"), X("LU", c0, c0 + NSC // 2)), AF.Copy)
+    def gat(q, b, l0, l1):
+        o, i = X("GT", 8 * l0, 8 * l1), IND(X("xt"), X("LU", 128 * b + l0 // 2, 128 * b + l1 // 2))
+        if q == "v":
+            tc(o, i)
+        else:
+            act(o, i)
 
-    def gv(b, bt):
-        l0 = 128 * bt + NSC
-        c0 = 128 * b + l0 // 2
-        tc(X("GT", 8 * l0, 8 * (l0 + NV)), IND(X("xt"), X("LU", c0, c0 + NV // 2)))
+    def smax(l0, l1):
+        scan(X("HM", 8 * l0, 8 * l1), X("SEGM", 0, 8 * (l1 - l0)), X("GT", 8 * l0, 8 * l1), OP.min, OP.max)
 
-    def smax(bt):
-        a = 1024 * bt
-        scan(X("HM", a, a + 1024), X("SEG"), X("GT", a, a + 1024), OP.mult, OP.max)
+    def diff(pb, zin, l0, l1):
+        msum(X(pb, 0, l1 - l0), [(X("NI"), X(zin, l0, l1)), (X("ID"), X("HM", 8 * l0 + 7, 8 * l1, 8))])
 
-    def diff(bt, zin):
-        l0 = 128 * bt
-        pb = "PB%d" % bt
-        mm(X(pb, 0, 128), X("NI"), X(zin, l0, l0 + 128), True, False)
-        mm(X(pb, 0, 128), X("ID"), X("HM", 8 * l0 + 7, 8 * l0 + 1024, 8), False, True)
+    def absz(pb, zout, l0, l1):
+        act(X(zout, l0, l1), X(pb, 0, l1 - l0), AF.Abs)
 
-    def absz(bt, zout):
-        l0 = 128 * bt
-        act(X(zout, l0, l0 + 128), X("PB%d" % bt, 0, 128), AF.Abs)
+    def usum(pb, l0, l1):
+        msum(X(pb, 128, 128 + (l1 - l0) // 2), [(X("WU%d" % h), X("Z1", l0 + h, l1, 2)) for h in range(2)])
 
-    def usum(bt):
-        l0, c0 = 128 * bt, 64 * bt
-        pb = "PB%d" % bt
-        mm(X(pb, 128, 192), X("WU0"), X("Z1", l0, l0 + 128, 2), True, False)
-        mm(X(pb, 128, 192), X("WU1"), X("Z1", l0 + 1, l0 + 128, 2), False, True)
-        act(X("SQ", c0, c0 + 64), X(pb, 128, 192), AF.Square, bias=K2, scale=0.25)
-        act(X("U1", c0, c0 + 64), X(pb, 128, 192), AF.Copy)
+    def sq(pb, l0, l1):
+        act(X("SQ", l0 // 2, l1 // 2), X(pb, 128, 128 + (l1 - l0) // 2), AF.Square, bias=K2, scale=0.25)
 
-    def list1(bt):
-        c0 = 64 * bt
-        tt(X("T1", c0, c0 + 64), X("SQ", c0, c0 + 64), X("VM", c0, c0 + 64), OP.add)
-        ts(X("TR", 128 + c0, 192 + c0), X("T1", c0, c0 + 64), 4095, OP.bitwise_and)
-        tc(X("LU", 128 + c0, 192 + c0), X("TR", 128 + c0, 192 + c0))
+    def list0(step, l0, l1):
+        c0, c1 = l0 // 2, l1 // 2
+        if step == 0:
+            ts(X("TA", c0, c1), X("ZS", c0, c1), X("ACOL"), OP.add)
+        elif step == 1:
+            ts(X("TR", c0, c1), X("TA", c0, c1), 4095, OP.bitwise_and)
+        else:
+            tc(X("LU", c0, c1), X("TR", c0, c1))
 
-    def newv():
-        ts(X("TA"), X("WI"), col("ACOL", 0), OP.add)
-        ts(X("VCI"), X("TA"), 4095, OP.bitwise_and)
+    def list1(step, l0, l1):
+        c0, c1 = l0 // 2, l1 // 2
+        if step == 0:
+            tt(X("T1", c0, c1), X("SQ", c0, c1), X("VM", c0, c1), OP.add)
+        elif step == 1:
+            ts(X("TR", 128 + c0, 128 + c1), X("T1", c0, c1), 4095, OP.bitwise_and)
+        else:
+            tc(X("LU", 128 + c0, 128 + c1), X("TR", 128 + c0, 128 + c1))
 
     def hurt(step):
         if step == 0:
-            tt(X("FX", 960, 966), X("DN", 0, 6), X("W6"), OP.mult)
+            scan(X("SML", 0, 7), X("H7"), X("DNB", 1, 14, 2), OP.mult, OP.add)
         elif step == 1:
-            red(col("FX", 966), X("FX", 960, 966))
+            ts(X("MS", 0, 192), X("PB5", 0, 192), col("SML", 6), OP.add)
+            ts(X("MS", 192, 256), X("PB2", 256, 320), col("SML", 6), OP.add)
         elif step == 2:
-            ts(col("FX", 967), col("FX", 966), float(0x111111), OP.add)
-        elif step == 3:
-            ts(X("MS", 0, 256), X("N3", 512, 768), col("FX", 967), OP.add)
-        elif step == 4:
             ts(X("MS", 256, 512), X("MS", 0, 256), 0x444444, OP.bitwise_and)
         else:
             ts(X("HB"), X("MS", 256, 512), 0.0, OP.is_gt)
 
     def back(t):
-        arrive("VWIN", 0, 96, "rin%d" % t, NE)
-        act(X("VROW"), IND(X("VWIN"), X("OL")), AF.Copy)
+        arrive("VWIN", 0, 16, "rin%d" % t, NE)
+        tt(X("PR"), IND(X("VWIN"), X("ML", 16, 32)), X("MG"), OP.mult)
 
-    def thaw1():
-        mm(X("PB7", 128, 256), X("ID"), X("NF2"), True, False)
-        for cl in range(4):
+    def thaw(step):
+        o = X("PB7", 0, 128)
+        if step == 0:
+            mm(o, X("ID"), X("NF"), True, False)
             for h in range(2):
-                mm(X("PB7", 128 + 32 * cl, 160 + 32 * cl), X("WU%d" % h), X("HB", 4 * h + cl, 256, 8), False, False)
+                mm(o, X("WU%d" % h), X("HB", h, 256, 2), False, False)
+        elif step == 1:
+            for h in range(2):
+                mm(o, X("WU%d" % h), X("PR", h, 256, 2), False, h == 1)
+        else:
+            act(X("FR"), o, AF.Relu, bias=8192.0, scale=-8192.0)
+            act(X("NF"), X("FR"), bias=16384.0, scale=-2.0)
 
-    def thaw2():
-        mm(X("PB7", 128, 256), X("VS0"), X("VROW", 0, 256, 2), False, False)
-        mm(X("PB7", 128, 256), X("VS1"), X("VROW", 1, 256, 2), False, True)
+    def word(pb, step, l0, l1):
+        k0, k1 = l0 // 16, l1 // 16
+        if step == 0:
+            mm(X4(pb, k0, k1), X("KR2"), X("CLSR", l0, l1), True, False)
+            for h in range(2):
+                mm(X4(pb, k0, k1, h), X("HS%d" % h), X("VM", l0 // 2, l1 // 2), False, False)
+        elif step == 1:
+            for h in range(2):
+                mm(X4(pb, k0, k1, h), X("ID"), X("Z2", l0 + h, l1, 2), False, h == 1)
+        else:
+            act(X("XF", l0, l1), X4(pb, k0, k1), bias=256.0 * (4 * KAP[0] ** 2 + 0.25))
 
-    def verdict_row(t, hop):
-        for i in range(16):
-            mm(X("PB7", i, 96, 16), X("RS", 128 * i, 128 * i + 128), X("DN", 0, 6), True, True)
-        act(X("VO"), X("PB7", 0, 96), AF.Copy, bias=1.0, scale=-1.0)
-        out = T.VWIN[:, 0:96] if hop in T.cores else T.G2[:, 96 * t:96 * t + 96]
-        dv = X("VO")
-        issue("g", lambda: _send(g, T, topo, core, hop, out, dv[0], "rin%d" % t, "rl%d" % t), dv[1], [], sem="rl%d" % t, val=NE)
+    def halt(t, step, l0, l1):
+        c0, c1 = l0 // 2, l1 // 2
+        if step == 0:
+            act(X("GE", l0, l1), X("Z2", l0, l1), AF.Sign, bias=col("NTH", t))
+        elif step == 1:
+            msum(X("PB2", c0, c1), [(X("NI"), X("FR", c0, c1))] * (t > 0) + [(X("WU%d" % h), X("GE", l0 + h, l1, 2)) for h in range(2)])
+        elif step == 2:
+            ts(X("FL", c0, c1), X("PB2", c0, c1), 1.0, OP.is_ge)
+        elif step == 3:
+            scan(X("INC", c0, c1), X("FL", c0, c1), X("ZER", c0, c1), OP.add, OP.add, col("INC", c0 - 1) if c0 else -0.5)
+        elif step == 4:
+            msum(X("PB4", 128 + c0, 128 + c1), [(X("ID"), X("OBM", c0, c1)), (X("RKF"), X("FL", c0, c1)), (X("RK1"), X("INC", c0, c1))])
+        elif step == 5:
+            scan(X("OS", c0, c1), X("RSTP", c0, c1), X("PB4", 128 + c0, 128 + c1), OP.max, OP.min)
+        elif step == 6:
+            tc(X("OL", l0 // 16, l1 // 16), X("OS", c0 + 7, c1, 8))
+        else:
+            tc(IND(X("XW"), X("OL", l0 // 16, l1 // 16)), X("XF", l0, l1))
 
-    V = X("CAT", 256, 384)
+    V = X("LG", 256, 384)
     S6 = X("FX", 207, 288, 16)
+    DN = X("DNB", 1, 12, 2)
 
     for t in range(STAGES):
+        last = t == STAGES - 1
         dst = T.cores[_partner(rank, t)]
         hop = dst if topo.may_write(core, dst) else _relay(core, T, topo)
+        gat("s", 0, 0, 64)
         if t:
-            ts(X("TA"), X("ZN"), col("ACOL", 0), OP.add)
-            tc(IND(X("xt"), X("DLU", 6, 12)), X("N3", 896, 992))
-            ts(X("TR", 0, 128), X("TA"), 4095, OP.bitwise_and)
-            tc(X("LU", 0, 128), X("TR", 0, 128))
-        gs(0, 0)
-        gv(0, 0)
-        gs(0, 1)
+            for j in range(3):
+                list0(j, 128, 256)
+                if j == 0:
+                    hurt(0)
+        gat("v", 0, 64, 128)
+        gat("s", 0, 128, 192)
         if t:
-            ts(X("TA"), X("WI"), col("ACOL", 0), OP.add)
-            hurt(0)
-            ts(X("VCI"), X("TA"), 4095, OP.bitwise_and)
+            ts(X("VM"), X("WM"), X("ACOL"), OP.add, KM, OP.add)
+        smax(0, 64)
+        smax(64, 128)
+        diff("PB0", "Z0", 0, 128)
+        gat("s", 0, 192, 224)
+        absz("PB0", "Z1", 0, 128)
+        usum("PB0", 0, 128)
+        gat("s", 0, 224, 256)
+        sq("PB0", 0, 128)
+        if t:
             hurt(1)
-        ts(X("VM"), X("VCI"), KM, OP.add)
+        smax(128, 192)
+        list1(0, 0, 128)
+        smax(192, 256)
+        diff("PB1", "Z0", 128, 256)
+        list1(1, 0, 128)
         if t:
             hurt(2)
-        tc(X("VHI"), X("VCI"))
-        mm(X("PB3", 0, 256), X("KR2"), X("CLSR"), True, False)
-        mm(X("PB3", 0, 256), X("KR3"), X("ONE"), False, False)
-        smax(0)
-        diff(0, "Z0")
-        absz(0, "Z1")
-        usum(0)
-        tt(X("VLO"), X("VCI"), X("VHI"), OP.subtract)
-        for h in range(2):
-            mm(X("PB3", h, 256, 2), X("HS%d" % h), X("VHI"), False, False)
-            mm(X("PB3", h, 256, 2), X("HS%d" % h), X("VLO"), False, False)
+        list1(2, 0, 128)
+        absz("PB1", "Z1", 128, 256)
+        usum("PB1", 128, 256)
+        gat("s", 1, 0, 32)
+        sq("PB1", 128, 256)
+        gat("s", 1, 32, 64)
+        word("PB3", 0, 0, 192)
+        gat("v", 1, 64, 96)
+        list1(0, 128, 256)
         if t:
             hurt(3)
-        gv(0, 1)
-        if t:
-            hurt(4)
-        smax(1)
-        diff(1, "Z0")
-        absz(1, "Z1")
-        usum(1)
-        tt(X("T1", 0, 64), X("SQ", 0, 64), X("VM", 0, 64), OP.add)
-        if t:
-            hurt(5)
-        ts(X("TR", 128, 192), X("T1", 0, 64), 4095, OP.bitwise_and)
-        tc(X("LU", 128, 192), X("TR", 128, 192))
-        gs(1, 0)
-        gv(1, 0)
-        list1(1)
-        gs(1, 1)
-        smax(0)
-        diff(0, "Z1")
-        gv(1, 1)
-        absz(0, "Z2")
-        act(X("GE", 0, 128), X("Z2", 0, 128), AF.Sign, bias=col("NTH", t))
-        if t:
-            thaw1()
-        smax(1)
-        diff(1, "Z1")
-        absz(1, "Z2")
-        act(X("GE", 128, 256), X("Z2", 128, 256), AF.Sign, bias=col("NTH", t))
-        mm(X("PB2", 0, 128), X("WU0"), X("GE", 0, 256, 2), True, False)
-        mm(X("PB2", 0, 128), X("WU1"), X("GE", 1, 256, 2), False, True)
+            thaw(0)
+        list1(1, 128, 256)
+        smax(0, 64)
+        list1(2, 128, 256)
+        gat("s", 1, 96, 128)
+        gat("s", 1, 128, 192)
+        word("PB6", 0, 192, 256)
         if t:
             back(t - 1)
-            thaw2()
-            ts(X("FLX"), X("PB2", 0, 128), 1.0, OP.is_lt, 65536.0, OP.mult)
-            tt(X("FL"), X("PB7", 128, 256), X("FLX"), OP.is_gt)
-        else:
-            ts(X("FL"), X("PB2", 0, 128), 1.0, OP.is_ge)
-        mm(X("PB3", 0, 128), X("ID"), X("Z2", 0, 128), False, False)
-        mm(X("PB3", 128, 256), X("ID"), X("Z2", 128, 256), False, True)
-        act(X("XF"), X("PB3", 0, 256), AF.Copy)
-        scan(X("INC"), X("FL"), X("ZER"), OP.add, OP.add)
-        mm(X("PB2", 128, 256), X("KR1"), X("ONE", 0, 128), True, False)
-        mm(X("PB2", 128, 256), X("RK2"), X("FL"), False, False)
-        mm(X("PB2", 128, 256), X("M1K"), X("FL"), False, False)
-        mm(X("PB2", 128, 256), X("RK1"), X("INC"), False, True)
-        if t:
-            ts(X("FR"), X("PB7", 128, 256), 0.0, OP.is_equal)
-        tt(X("OFFP"), X("PB2", 128, 256), X("DUMPP"), OP.min)
-        if t:
-            ts(X("NF4"), X("PB7", 128, 256), 0.0, OP.is_gt, 4096.0, OP.mult)
-        for e in range(8):
-            mm(X("PB2", 256, 272), X("PL", 128 * e, 128 * e + 128), X("OFFP", e, 128, 8), e == 0, e == 7)
-        tc(X("OL"), X("PB2", 256, 272))
-        tc(IND(X("XW"), X("OL")), X("XF"))
+            thaw(1)
+            thaw(2)
+        smax(64, 128)
+        diff("PB0", "Z1", 0, 128)
+        absz("PB0", "Z2", 0, 128)
+        gat("s", 1, 192, 232)
+        gat("v", 1, 232, 256)
+        smax(128, 192)
+        diff("PB1", "Z1", 128, 192)
+        absz("PB1", "Z2", 128, 192)
+        halt(t, 0, 0, 192)
+        halt(t, 1, 0, 192)
+        word("PB3", 1, 0, 192)
+        smax(192, 256)
+        diff("PB0", "Z1", 192, 256)
+        absz("PB0", "Z2", 192, 256)
+        halt(t, 0, 192, 256)
+        word("PB3", 2, 0, 192)
+        halt(t, 2, 0, 192)
+        halt(t, 3, 0, 192)
+        halt(t, 4, 0, 192)
+        halt(t, 1, 192, 256)
+        word("PB6", 1, 192, 256)
+        word("PB6", 2, 192, 256)
+        halt(t, 5, 0, 192)
+        halt(t, 2, 192, 256)
+        halt(t, 6, 0, 192)
+        halt(t, 3, 192, 256)
+        halt(t, 4, 192, 256)
+        halt(t, 7, 0, 192)
+        for j in (5, 6, 7):
+            halt(t, j, 192, 256)
         sv = X("XW", 0, 96)
         issue("g", lambda: _send(g, T, topo, core, hop, T.XR[:, 96 * t:96 * t + 96], sv[0], "xin%d" % t, "xl%d" % t),
               sv[1], [], sem="xl%d" % t, val=NE)
         if t == 0:
             consts_verdict()
-        ts(X("GO"), X("OFFP"), 95.5, OP.is_ge, 4096.0, OP.mult)
-        if t == 0:
-            for b in range(2):
-                tt(X("LG", 128 * b, 128 * b + 128), X("TR", 128 * b, 128 * b + 128), X("GO"), OP.add)
-            ts(X("NF2"), X("GO"), 1.0, OP.mult)
-        else:
-            for b in range(2):
-                tt(X("LG", 128 * b, 128 * b + 128), X("LG", 128 * b, 128 * b + 128), X("NF4"), OP.add)
-                tt(X("P1", 128 * b, 128 * b + 128), X("TR", 128 * b, 128 * b + 128), X("GO"), OP.add)
-            tt(X("SEL", 0, 128), V, X("VCI"), OP.subtract)
-            tt(X("LG"), X("LG"), X("P1"), OP.min)
-            tt(X("SEL", 0, 128), X("SEL", 0, 128), X("FR"), OP.mult)
-            tt(X("NF2"), X("GO"), X("NF4"), OP.min)
-        ts(X("LGU"), X("LG"), 4096.0, OP.min)
+        msum(X("PB2", 128, 256), [(X("RKF"), X("FL")), (X("RK1"), X("INC"))])
+        fr = [(X("ID"), X("FR"))] * (t > 0)
+        msum(X("PB5", 256, 384), [(X("WU%d" % h), X("Z1", h, 256, 2)) for h in range(2)] + fr)
+        ts(X("OC"), X("OS", 7, 128, 8), 96.0, OP.min)
+        ts(X("GO"), X("PB2", 128, 256), -928.5, OP.is_ge, 8192.0, OP.mult)
         if t:
-            tt(V, X("SEL", 0, 128), X("VCI"), OP.add)
-            tt(X("SEL", 128, 256), X("CAT", 128, 256), X("U1"), OP.subtract)
+            for j in range(4):
+                mm(X("PB1", 128 * j, 128 * j + 128), X("ID"), X("NF"), True, True)
+            ts(X("TA"), X("WM"), X("ACOL"), OP.add)
+        repeats(X("DUP1"), X("PB5", 256, 384))
+        mm(X("PB7", 128, 144), X("PM"), X("OC"), True, True)
+        for b in range(2):
+            msum(X("PB0", 128 * b, 128 * b + 128), [(X("ID"), X("GO")), (X("K4"), X("DUP%d" % b))])
+        if t:
+            mm(X("PB0", 256, 384), X("ID"), X("FR"), True, True)
+            ts(X("TR", 256, 384), X("TA"), 4095, OP.bitwise_and)
+            tt(X("LG", 0, 512), X("LG", 0, 512), X("PB1"), OP.add)
             tc(IND(X("D"), X("DLU", 0, 6)), X("ZER", 0, 96))
-            tt(X("SEL", 128, 256), X("SEL", 128, 256), X("FR"), OP.mult)
-            if t < STAGES - 1:
-                ms(X("XW", 0, 96), SENT)
-            tt(X("CAT", 128, 256), X("SEL", 128, 256), X("U1"), OP.add)
+            tt(X("PB0", 0, 384), X("TR"), X("PB0", 0, 384), OP.add)
+            tt(X("LG", 384, 512), X("LG", 384, 512), X("PB5", 256, 384), OP.min)
+            tt(X("LG", 0, 384), X("LG", 0, 384), X("PB0", 0, 384), OP.min)
         else:
-            act(X("CAT", 128, 256), X("U1"), AF.Copy)
-            ms(X("XW", 0, 96), SENT)
-        act(X("WT", 0, 128), V, AF.Square)
-        act(X("WT", 128, 256), V, AF.Copy, scale=37.0)
-        act(X("WT", 0, 128), X("WT", 0, 128), AF.Copy, bias=-0.25, scale=0.125)
-        tt(X("WI"), X("WT", 0, 128), X("WT", 128, 256), OP.add)
-        if t < STAGES - 1:
+            tc(V, X("TR", 256, 384))
+            act(X("LG", 384, 512), X("PB5", 256, 384))
+            tt(X("LG", 0, 256), X("TR", 0, 256), X("PB0", 0, 256), OP.add)
+        act(X("WS"), V, AF.Square, bias=37.0, scale=0.25)
+        tc(X("ML", 0, 16), X("PB7", 128, 144))
+        tc(X("OI", 0, 16), X("PB7", 128, 144))
+        ts(X("LGU"), X("LG", 0, 256), 4096.0, OP.min)
+        act(X("MG"), IND(X("MK"), X("ML", 0, 16)))
+        ts(X("OI", 16, 32), X("OI", 0, 16), 4, OP.logical_shift_right)
+        ts(X("WI"), X("WS"), 2.0, OP.mult, -2738.25, OP.add)
+        ts(X("ML", 16, 32), X("OI", 16, 32), 2.0, OP.mult, 1.0, OP.add)
+        ts(X("WM"), X("WI"), 4095, OP.bitwise_and)
+        if last:
+            act(X("NF32"), X("NF"), scale=1.0 / 256)
+            tc(X("LG", 640, 768), X("WM"))
+            msum(X("PB7", 256, 320), [(X("PL", 128 * e, 128 * e + 128), X("LG", 256 + e, 768, 8)) for e in range(8)])
+        else:
             tt(X("ZS"), X("WI"), X("S0I"), OP.add)
-            ts(X("ZN"), X("ZS"), 4095, OP.bitwise_and)
-        if t == 0:
-            consts_back()
+        if t == 1:
             consts_out()
         arrive("XR", 96 * t, 96 * t + 96, "xin%d" % t, NE)
         XR = X("XR", 96 * t, 96 * t + 96)
-        Y1 = X("N3", 800, 896)
-        ts(Y1, XR, 8, OP.logical_shift_right, 8191, OP.bitwise_and)
-        tt(X("FX", 0, 96), Y1, X("DIAG"), OP.mult)
-        scan(X("FX", 96, 192), X("HOLD"), X("FX", 0, 96), OP.mult, OP.add)
+        ts(X("Y1"), XR, 8, OP.logical_shift_right, 0x8FFF, OP.bitwise_and)
+        ts(X("CI"), XR, 21, OP.logical_shift_right)
+        tt(X("FX", 0, 96), X("Y1"), X("DG"), OP.min)
+        scan(X("FX", 96, 192), X("RS96"), X("FX", 0, 96), OP.min, OP.max)
+        tt(X("FX", 288, 384), X("CI"), X("DG"), OP.min)
         pos = []
         o = 96
         for k in range(5):
             n = 80 - 16 * k
-            ts(X("E", o, o + n), X("N3", 816 + 16 * k, 896), col("FX", 96 + 16 * k + 15), OP.is_equal)
+            ts(X("E", o, o + n), X("Y1", 16 + 16 * k, 96), col("FX", 96 + 16 * k + 15), OP.is_equal)
             pos.append((o, n))
             o += n
-        tt(X("E", 0, 96), Y1, X("FX", 96, 192), OP.is_equal)
+        tt(X("E", 0, 96), X("Y1"), X("FX", 96, 192), OP.is_equal)
         mm(X("PB4", 0, 96), X("ID"), X("OB"), True, False)
         for (o, n) in pos:
             mm(X("PB4", 96 - n, 96), X("BOK"), X("E", o, o + n), False, False)
         mm(X("PB4", 0, 96), X("BOK"), X("E", 0, 96), False, True)
-        tt(X("FX", 0, 96), X("PB4", 0, 96), Y1, OP.add)
+        scan(X("FX", 384, 480), X("RS96"), X("FX", 288, 384), OP.min, OP.max)
+        tt(X("FX", 0, 96), X("PB4", 0, 96), X("Y1"), OP.add)
+        ts(X("CM", 0, 6), X("FX", 399, 480, 16), 1.0, OP.is_ge, 7.0, OP.mult)
         scan(X("FX", 192, 288), X("RST"), X("FX", 0, 96), OP.max, OP.min)
-        ts(X("DLU", 0, 6), S6, -1.0, OP.add)
+        ts(X("CM", 6, 12), X("FX", 399, 480, 16), 2.0, OP.is_ge, 7.0, OP.mult)
+        tc(X("DLU", 0, 6), S6)
+        ts(X("CM", 12, 18), X("FX", 399, 480, 16), 3.0, OP.is_ge, 7.0, OP.mult)
         tc(IND(X("D"), X("DLU", 0, 6)), X("CODE"))
 
-        def piece(q, b, k0, k1):
-            o, i = X("G2", 2048 * b + 512 * k0, 2048 * b + 512 * k1), IND(X("D"), X("LGU", 128 * b + 32 * k0, 128 * b + 32 * k1))
+        def piece(q, cl, b, l0=0, l1=64):
+            a, c = 1024 * cl + 512 * b, 128 * b + 32 * cl
+            o, i = X("G2", a + 8 * l0, a + 8 * l1), IND(X("D"), X("LGU", c + l0 // 2, c + l1 // 2))
             if q == "v":
                 tc(o, i)
             else:
-                act(o, i, AF.Copy)
+                act(o, i)
 
-        def sums(b, k0, k1):
-            for cl in range(k0, k1):
-                for m in range(8):
-                    o = X("PB7", 0, 64) if b and cl == 3 else X("PB%d" % (5 + b), cl, 256, 4)
-                    mm(o, X("ID"), X("G2", 2048 * b + 512 * cl + m, 2048 * b + 512 * cl + 512, 8), m == 0, m == 7)
+        def sums(cl, b):
+            o = X("PB2", 256, 320) if cl == 3 else X("PB5", 64 * cl, 64 * cl + 64)
+            a = 1024 * cl + 512 * b
+            for m in range(8):
+                mm(o, X("ID"), X("G2", a + m, a + 512, 8), b == 0 and m == 0, b == 1 and m == 7)
 
-        mm(X("PB6", 3, 256, 4), X("ID"), X("ZER", 0, 64), True, True)
-        piece("v", 0, 0, 2)
-        piece("s", 0, 2, 4)
-        piece("v", 1, 0, 1)
-        piece("s", 1, 1, 3)
-        piece("s", 1, 3, 4)
-        sums(0, 0, 2)
-        sums(0, 2, 4)
-        sums(1, 0, 1)
-        sums(1, 1, 3)
-        sums(1, 3, 4)
-        ts(X("MS", 0, 96), XR, 21, OP.logical_shift_right)
-        tt(X("FX", 0, 96), X("MS", 0, 96), X("DIAG"), OP.mult)
-        scan(X("FX", 96, 192), X("HOLD"), X("FX", 0, 96), OP.mult, OP.add)
-        for cl in range(1, 4):
-            for p in (0, 4):
-                ts(X("FX", 900 + p + cl, 948, 8), X("FX", 111, 192, 16), float(cl), OP.is_ge, 8192.0, OP.mult, waw=False)
-        ts(X("FX", 990, 996), S6, 4100.0, OP.is_ge, -1.0, OP.mult)
-        ts(X("N3", 896, 992), XR, 255, OP.bitwise_and)
-        for b in range(2):
-            ts(X("MS", 256 * b, 256 * b + 256), X("PB%d" % (5 + b), 0, 256), float(0x777777), OP.add)
-            ts(X("N3", 256 * b, 256 * b + 256), X("MS", 256 * b, 256 * b + 256), 0x888888, OP.bitwise_and, 3, OP.logical_shift_right)
-        tt(X("N3", 512, 768), X("N3", 0, 256), X("N3", 256, 512), OP.add)
-        ts(X("P1", 0, 64), X("PB7", 0, 64), float(0x777777), OP.add)
-        tt(X("MS", 0, 128), X("N3", 512, 640), X("N3", 640, 768), OP.add)
-        ts(X("P1", 64, 128), X("P1", 0, 64), 0x888888, OP.bitwise_and, 3, OP.logical_shift_right)
-        tt(X("MS", 128, 192), X("MS", 0, 64), X("MS", 64, 128), OP.add)
-        tt(X("P1", 128, 160), X("P1", 64, 96), X("P1", 96, 128), OP.add)
-        tt(X("P1", 160, 176), X("P1", 128, 144), X("P1", 144, 160), OP.add)
-        tt(X("MS", 131, 192, 4), X("MS", 131, 192, 4), X("P1", 160, 176), OP.add)
-        ts(X("MS", 192, 256), X("MS", 128, 192), float(0x777777), OP.add)
-        ts(X("MS", 256, 320), X("MS", 192, 256), 0x888888, OP.bitwise_and, 3, OP.logical_shift_right)
-        tt(X("MS", 320, 352), X("MS", 256, 288), X("MS", 288, 320), OP.add)
-        tt(X("MS", 352, 368), X("MS", 320, 336), X("MS", 336, 352), OP.add)
-        tt(X("MS", 368, 376), X("MS", 352, 360), X("MS", 360, 368), OP.add)
-        for k in range(6):
-            ts(X("MS", 384 + 8 * k, 392 + 8 * k), X("MS", 368, 376), 4 * k, OP.logical_shift_right, 15, OP.bitwise_and)
-        tt(X("FX", 1000, 1048), X("MS", 384, 432), X("FX", 900, 948), OP.mult)
-        scan(X("FX", 1048, 1096), X("SEG", 0, 48), X("FX", 1000, 1048), OP.mult, OP.add)
-        vet = X("FX", 1055, 1096, 8)
-        tt(X("DN", 0, 6), vet, X("FX", 990, 996), OP.is_equal)
-        if t < STAGES - 1:
-            tt(X("FX", 972, 978), vet, S6, OP.add)
-        mm(X("PB4", 128, 134), X("ONE", 0, 128), X("DN", 0, 6), True, True)
-        if t < STAGES - 1:
-            tt(X("FX", 980, 986), X("FX", 972, 978), X("DMP6"), OP.min)
-        red(col("ACOL", 0), X("PB4", 128, 134))
-        if t < STAGES - 1:
-            ts(X("DLU", 6, 12), X("FX", 980, 986), -1.0, OP.add)
-        verdict_row(t, hop)
-        tt(X("N3", 515, 768, 4), X("N3", 515, 768, 4), X("P1", 64, 128), OP.add)
+        for cl, b in ((0, 0), (0, 1), (1, 0), (1, 1)):
+            piece("v", cl, b, 0, 32)
+            piece("s", cl, b, 32, 64)
+            sums(cl, b)
+        for cl in (2, 3):
+            piece("v", cl, 0)
+            piece("s", cl, 1)
+            sums(cl, 0)
+            sums(cl, 1)
+        if last:
+            act(X("UL"), X("PB7", 256, 320))
+            for e in range(16):
+                k = KAP[e % 8]
+                act(X("YQ", 16 * e, 16 * e + 16), X("UL", 32 - 16 * (e // 8), 48 - 16 * (e // 8)), AF.Square, bias=2.0 * k, scale=0.25)
+                act(X("YV", 16 * e, 16 * e + 16), X("UL", 0, 16), bias=-4.0 * k * k - 0.25)
+        scan(X("CM", 18, 36), X("H16"), X("CM", 0, 18), OP.mult, OP.add)
+        ts(X("SML", 8, 14), S6, 4096.0, OP.is_lt, 10.0, OP.mult)
+        for j in (6, 13, 15):
+            tc(X("SM", 16 + j, 64, 16), X("CM", 23, 36, 6))
+        if not last:
+            tt(X("FD", 0, 12, 2), S6, DMP6, OP.subtract)
+            ts(X("ZV"), XR, 255, OP.bitwise_and)
+        scan(X("FX", 288, 480), X("SEG4"), X("PB5", 0, 192), OP.mult, OP.add)
+        if not last:
+            ms(X("XW", 0, 96), SENT)
+        ts(X("MS", 0, 48), X("FX", 291, 480, 4), NORM[0], OP.add)
+        scan(X("FX", 480, 544), X("SEG4", 0, 64), X("PB2", 256, 320), OP.mult, OP.add)
+        ts(X("MS", 48, 64), X("FX", 483, 544, 4), NORM[0], OP.add)
+        ts(X("MS", 64, 128), X("MS", 0, 64), NORM[1], OP.bitwise_and, 3, OP.logical_shift_right)
+        scan(X("FX", 0, 64), X("SEG7"), X("MS", 64, 128), OP.mult, OP.add)
+        tt(X("MS", 128, 192), X("FX", 0, 64), X("SM"), OP.add)
+        ts(X("MS", 192, 256), X("MS", 128, 192), NORM[1], OP.bitwise_and, 3, OP.logical_shift_right)
+        scan(X("FX", 64, 128), X("MS", 192, 256), X("ZER", 0, 64), OP.add, OP.add, -float(0x666666))
+        ts(X("TI", 0, 6), X("POW"), col("FX", 127), OP.mult)
+        ts(X("TI", 6, 12), X("TI", 0, 6), 15, OP.bitwise_and)
+        tt(DN, X("TI", 6, 12), X("SML", 8, 14), OP.is_equal)
+        out = T.VWIN[:, 0:16] if hop in T.cores else T.G2[:, 16 * t:16 * t + 16]
+        dv = X("DNB")
+        issue("g", lambda: _send(g, T, topo, core, hop, out, dv[0], "rin%d" % t, "rl%d" % t), dv[1], [], sem="rl%d" % t, val=NE)
+        mm(X("PB4", 256, 262), X("ONE"), DN, True, True)
+        if not last:
+            scan(X("SML", 16, 28), X("DNB", 0, 12), X("FD"), OP.mult, OP.add)
+            tc(X("DLU", 6, 12), X("SML", 17, 28, 2))
+        red(X("ACOL"), X("PB4", 256, 262))
+        if not last:
+            list0(0, 0, 128)
+            tc(IND(X("xt"), X("DLU", 6, 12)), X("ZV"))
+            list0(1, 0, 128)
+            list0(2, 0, 128)
 
-    newv()
-    tc(X("VHI"), X("VCI"))
-    tt(X("VLO"), X("VCI"), X("VHI"), OP.subtract)
-    for e in range(8):
-        mm(X("PB3", 0, 16), X("PL", 128 * e, 128 * e + 128), X("VHI", e, 128, 8), e == 0, False)
-        mm(X("PB3", 0, 16), X("PL", 128 * e, 128 * e + 128), X("VLO", e, 128, 8), False, e == 7)
-    for k in range(6):
-        hurt(k)
-    thaw1()
-    tc(X("FIN", 0, 16), X("PB3", 0, 16))
-    tc(X("CH"), X("CAT"))
-    tt(X("CL"), X("CAT"), X("CH"), OP.subtract)
-    for e in range(8):
-        mm(X("PB6", 256, 304), X("PL", 128 * e, 128 * e + 128), X("CH", e, 384, 8), e == 0, False)
-        mm(X("PB6", 256, 304), X("PL", 128 * e, 128 * e + 128), X("CL", e, 384, 8), False, e == 7)
-    tc(X("UL"), X("PB6", 256, 304))
-    tt(X("FX", 288, 544), IND(X("UL", 0, 32), X("YLU", 0, 16)), X("K8T"), OP.add)
-    act(X("FX", 544, 800), X("FX", 288, 544), AF.Square, scale=0.25)
-    tt(X("FIN", 16, 32), X("UL", 32, 48), X("FIN", 0, 16), OP.subtract)
-    tt(X("FX", 288, 544), X("FX", 544, 800), X("K2T"), OP.add)
-    tt(X("MS", 0, 256), IND(X("UL", 32, 48), X("YLU", 16, 32)), X("FX", 288, 544), OP.add)
-    ts(X("MS", 256, 512), X("MS", 0, 256), 4095, OP.bitwise_and)
-    tc(X("YO"), X("MS", 256, 512))
-    store("y", T.yt[:, :], X("YO"), "dyt")
+    hurt(0)
+    tt(X("TR", 0, 256), X("YQ"), X("YV"), OP.add)
+    hurt(1)
+    ts(X("OI", 16, 32), X("UL", 48, 64), X("ACOL"), OP.add)
+    hurt(2)
+    hurt(3)
+    ts(X("MS", 0, 256), X("TR", 0, 256), 4095, OP.bitwise_and)
+    ts(X("OI", 0, 16), X("OI", 16, 32), 4095, OP.bitwise_and)
+    tc(X("YO"), X("MS", 0, 256))
+    v = X("YO")
+    dma("y", T.yt[:, :], v[0], v[1], [], "dyt")
+    tt(X("FIN", 0, 16), X("UL", 0, 16), X("OI", 0, 16), OP.subtract)
+    o = X("PB2", 0, 256)
+    mm(o, X("ID"), X("OBL"), True, False)
+    mm(o, X("BO"), X("HB"), False, False)
+    for h in range(2):
+        mm(X("PB2", h, 256, 2), X("HS%d" % h), X("NF32"), False, False)
     back(STAGES - 1)
-    thaw2()
-    ts(X("FR"), X("PB7", 128, 256), 0.0, OP.is_equal)
-    for e in range(8):
-        mm(X("PB2", 0, 16), X("PL", 128 * e, 128 * e + 128), X("FR", e, 128, 8), e == 0, e == 7)
-    tc(X("YS", 16, 32), X("PB2", 0, 16))
-    tt(X("FIN", 32, 48), X("FIN", 16, 32), X("YS", 16, 32), OP.mult)
-    tt(X("YS", 0, 16), X("FIN", 32, 48), X("FIN", 0, 16), OP.add)
-    store("y", T.ys[:, :], X("YS"), "dys")
+    mm(o, X("BO"), X("PR"), False, True)
+    scan(X("FX", 0, 256), X("RSL"), o, OP.max, OP.min)
+    ts(X("YS", 16, 32), X("FX", 15, 256, 16), 0.0, OP.is_equal)
+    tt(X("FIN", 16, 32), X("FIN", 0, 16), X("YS", 16, 32), OP.mult)
+    tt(X("YS", 0, 16), X("FIN", 16, 32), X("OI", 0, 16), OP.add)
+    v = X("YS")
+    dma("y", T.ys[:, :], v[0], v[1], [], "dys")
 
-    for n, v in [("dx", 16), ("dsd", 16), ("dv0", 16), ("dth", 16), ("dyt", 16), ("dys", 16)]:
+    for n, v in [("dx", 16), ("dsd", 16), ("dv0", 16), ("dth", 16), ("dz", 7 * 16), ("dyt", 16), ("dys", 16)]:
         g.wait_ge(T.sem[n], v)
     for q in "vspg":
         g.wait_ge(T.sem["q" + q], CNT[q])

@@ -8,6 +8,12 @@ WIN = 4352
 SENT = 1 << 23
 MAGIC = 1.5 * 2 ** 23
 NORM = (float(0x777777), 0x888888)
+CYCLE, WAKE, ISSUE, LOAD, HOP, FIRST = 0.0009, 0.08, 0.06, 2.0, 3.2, 2.0
+AHEAD, SLACK, ROUNDS, LINE = 3, 0.02, 1, 0.9
+CHUNK = 16
+WHO = [['vvssssssvvssssvv', 'vvsssssvssssssvv'], ['vvsssssssssvvsvv', 'ssssssvvssssssvv'], ['vvssvvvssssvssss', 'vvssvvssvvssvvvv']]
+NUDGE = {('HB', 0): 1, ('Z1', 64): 0.2, ('LU', 160): -0.5, ('PR', 0): -0.2}
+BATCH = (((0, 64), (64, 128), (128, 256)), ((0, 128), (128, 192), (192, 256)))
 
 _F, _B, _I, _U = "float32", "bfloat16", "int32", "uint16"
 
@@ -34,18 +40,18 @@ SCRATCH = {
     "PM": _sb(128, _B), "PL": _sb(1024, _F), "HS0": _sb(128, _F), "HS1": _sb(128, _F), "KR2": _sb(128, _B), "CLSR": _sb(256, _B),
     "ONE": _sb(128, _B), "ZER": _sb(128, _B), "RSTP": _sb(128, _F),
     "DG": _sb(96, _F), "RS96": _sb(96, _F), "OB": _sb(96, _B), "RST": _sb(96, _F), "CODE": _sb(96, _B), "MK": _sb(112, _B),
-    "POW": _sb(6, _F), "H16": _sb(18, _F), "H7": _sb(7, _F), "SM": _sb(64, _F), "SEG4": _sb(192, _B), "SEG7": _sb(64, _B),
+    "POW": _sb(6, _F), "H16": _sb(18, _F), "H7": _sb(7, _F), "SM": _sb(128, _I), "SEG4": _sb(192, _F), "SEG64": _sb(512, _F), "SEG7": _sb(128, _B), "FLX": _sb(128, _B),
     "OBL": _sb(256, _B), "RSL": _sb(256, _F),
-    "S0F": _sb(128, _F), "S0I": _sb(128, _I), "DUP0": _sb(128, _B), "DUP1": _sb(128, _B), "DT": _sb(256, _F),
+    "S0I": _sb(128, _I), "DUP0": _sb(128, _B), "DUP1": _sb(128, _B), "DT": _sb(256, _F),
     "SQ": _sb(128, _F), "TA": _sb(128, _I), "T1": _sb(128, _I), "TR": _sb(384, _I), "LU": _sb(256, _U), "VM": _sb(128, _F),
     "GE": _sb(256, _B), "FL": _sb(128, _B), "INC": _sb(128, _B), "OS": _sb(128, _F), "OL": _sb(16, _U),
     "XF": _sb(256, _F), "XW": _sb(640, _I), "GO": _sb(128, _B), "FR": _sb(128, _B), "NF": _sb(128, _B), "NF32": _sb(128, _F),
     "OC": _sb(16, _B), "OI": _sb(32, _I), "ML": _sb(32, _U), "MG": _sb(256, _B), "PR": _sb(256, _B), "HB": _sb(256, _B),
     "LG": _sb(768, _F), "LGU": _sb(256, _U), "WS": _sb(128, _F), "WI": _sb(128, _I), "WM": _sb(128, _I), "ZS": _sb(128, _I),
     "XR": _sb(384, _I), "VWIN": _sb(16, _B), "DNB": _sb(16, _B),
-    "Y1": _sb(96, _I), "CI": _sb(96, _I), "ZV": _sb(96, _I), "E": _sb(336, _B), "FX": _sb(640, _F), "MS": _sb(512, _I),
+    "Y1": _sb(96, _I), "CI": _sb(96, _I), "ZV": _sb(96, _I), "E": _sb(336, _B), "FX": _sb(640, _F), "MS": _sb(1024, _I),
     "CM": _sb(36, _F), "FD": _sb(12, _F), "SML": _sb(32, _F), "TI": _sb(12, _I), "DLU": _sb(12, _U), "ACOL": _sb(1, _F),
-    "UL": _sb(64, _F), "YQ": _sb(256, _F), "YV": _sb(256, _F), "YO": _sb(256, _F), "YS": _sb(32, _F), "FIN": _sb(48, _F),
+    "UL": _sb(64, _F), "YQ": _sb(256, _F), "YV": _sb(256, _F), "YO": _sb(256, _F), "YS": _sb(64, _F),
 }
 for _k in range(8):
     SCRATCH["PB%d" % _k] = ("psum", [128, 32, 2, 8] if _k in (3, 6) else [128, 512], "float32")
@@ -94,6 +100,98 @@ def _relay_program(g, core, T, topo, c):
         g.wait_ge(T.sem["rl%d" % t], NE)
 
 
+def _plan(ops):
+    n = len(ops)
+    pred, succ = [{} for _ in ops], [[] for _ in ops]
+    acc, bank = {}, {}
+    for i, o in enumerate(ops):
+        for w, regs in ((False, o["r"]), (True, o["w"])):
+            for nm, cols in regs:
+                for j, wj, cj in acc.get(nm, []):
+                    if cj & cols and (w or wj):
+                        pred[i][j] = 0
+        for nm in {nm for nm, _ in o["r"] + o["w"] if nm[:2] == "PB"}:
+            q, now, before = bank.get(nm, (None, [], []))
+            if q == o["q"] and q != "p":
+                now.append(i)
+            else:
+                before, now = now, [i]
+            bank[nm] = (o["q"], now, before)
+            for j in before:
+                pred[i][j] = 0
+        for j in pred[i]:
+            pred[i][j] = 0 if o["q"] == "p" and ops[j]["q"] == "p" else WAKE
+        if o["after"] is not None:
+            pred[i][o["after"]] = 0 if o["q"] in "np" else ISSUE - ops[o["after"]]["cost"]
+        for j in pred[i]:
+            succ[j].append(i)
+        for w, regs in ((False, o["r"]), (True, o["w"])):
+            for nm, cols in regs:
+                acc[nm] = [r for r in acc.get(nm, []) if not w or r[2] & ~cols] + [(i, w, cols)]
+    cost = [o["cost"] for o in ops]
+    hold = [ISSUE if o["sem"] else o["cost"] for o in ops]
+    chain = [0.0] * n
+    nxt = {}
+    for i in reversed(range(n)):
+        chain[i] = cost[i] + max([pred[j][i] + chain[j] for j in succ[i]], default=0.0)
+        if ops[i]["w"]:
+            nm, cols = ops[i]["w"][0]
+            chain[i] += NUDGE.get((nm, (cols & -cols).bit_length() - 1), 0)
+            if nm in ("GT", "G2"):
+                if (nm, ops[i]["q"]) in nxt:
+                    chain[i] = max(chain[i], chain[nxt[nm, ops[i]["q"]]] + LINE * cost[i])
+                nxt[nm, ops[i]["q"]] = i
+
+    def walk(pred, succ, chain):
+        left, ready, done, end = [len(p) for p in pred], [0.0] * n, [False] * n, [0.0] * n
+        free = {q: 0.0 for q in "gvspyn"}
+        avail, order, now = [i for i in range(n) if not left[i]], [], 0.0
+        while avail:
+            soon = {i: ready[i] for i in avail}
+            edge = avail
+            for _ in range(AHEAD):
+                edge = {j for i in edge for j in succ[i] if all(done[k] or k in soon for k in pred[j])}
+                for j in edge:
+                    soon[j] = max([ready[j]] + [max(soon[k], now, min(free[q] for q in ops[k]["q"])) + cost[k] + pred[j][k] for k in pred[j] if not done[k]])
+            took = []
+            for q in "npsgyv":
+                if free[q] > now:
+                    continue
+                mine = [j for j in soon if ops[j]["q"] == q and soon[j] > now]
+                for i in sorted((i for i in avail if q in ops[i]["q"] and ready[i] <= now), key=lambda i: (-chain[i], i)):
+                    if q == "n" or not any(soon[j] < now + hold[i] and max(soon[j] + chain[j], soon[j] + hold[j] + chain[i]) < now + hold[i] + chain[j] - SLACK
+                                           for j in mine if chain[j] > chain[i]):
+                        took.append(i)
+                        order.append((i, q))
+                        avail.remove(i)
+                        if q != "n":
+                            free[q] = now + hold[i]
+                        break
+            for i in took:
+                done[i], end[i] = True, now + cost[i]
+                for j in succ[i]:
+                    left[j] -= 1
+                    ready[j] = max(ready[j], end[i] + pred[j][i])
+                    if not left[j]:
+                        avail.append(j)
+            if not took:
+                now = min([x for x in list(free.values()) + [ready[i] for i in avail] if x > now])
+        return order, end
+
+    back_pred = [{j: pred[j][i] for j in succ[i]} for i in range(n)]
+    back_succ = [list(p) for p in pred]
+    best = walk(pred, succ, chain)
+    now = best
+    for _ in range(ROUNDS):
+        now = walk(pred, succ, walk(back_pred, back_succ, now[1])[1])
+        if max(now[1]) < max(best[1]):
+            best = now
+    return best[0]
+
+
+_PLANS = {}
+
+
 def rank_program(g, core, T, topo):
     rank = T.rank_of(core)
     if rank is None:
@@ -117,7 +215,9 @@ def rank_program(g, core, T, topo):
         return (T[name][:, a:b:st] if st != 1 else T[name][:, a:b], [(name, bits(a, b, st))])
 
     def X4(name, k0, k1, h=None):
-        return (T[name][:, k0:k1] if h is None else T[name][:, k0:k1, h, :], [(name, bits(16 * k0, 16 * k1))])
+        if h is None:
+            return (T[name][:, k0:k1], [(name, bits(16 * k0, 16 * k1))])
+        return (T[name][:, k0:k1, h, :], [(name, sum(255 << (16 * k + 8 * h) for k in range(k0, k1)))])
 
     def IND(win, off):
         return (win[0].indirect(off[0]), win[1], off[1])
@@ -131,7 +231,18 @@ def rank_program(g, core, T, topo):
                 clk[q][k] = n
         clk[q][rec["sem"]] = rec["val"]
 
-    def issue(q, fn, reads, writes, sem=None, val=None, inc=0):
+    ops = []
+
+    def issue(q, fn, reads, writes, cost, sem=None, val=None, inc=0, after=None):
+        ops.append({"q": q, "fn": fn, "r": reads, "w": writes, "cost": cost, "sem": sem, "val": val, "inc": inc, "after": after})
+        return len(ops) - 1
+
+    def emit(q, fn, reads, writes, sem, val, inc):
+        if q == "n":
+            idx[0] += 1
+            for (nm, cols) in writes:
+                acc.setdefault(nm, []).append({"cols": cols, "w": True, "q": "dma", "sem": sem, "val": val, "snap": {}, "idx": idx[0]})
+            return
         lab = q if sem is None else "dma"
         deps = []
         for kind, regs in (("r", reads), ("w", writes)):
@@ -147,7 +258,7 @@ def rank_program(g, core, T, topo):
         deps.sort(key=lambda r: -r["idx"])
         for rec in deps:
             wait(q, rec)
-        ins = fn()
+        ins = fn(q)
         if sem is None:
             CNT[q] += 1
             ins.then_inc(T.sem["q" + q], 1)
@@ -168,9 +279,11 @@ def rank_program(g, core, T, topo):
                 old.append({"cols": cols, "w": w, "q": lab, "sem": s, "val": n, "snap": snap, "idx": idx[0]})
                 acc[nm] = old
 
-    def arrive(name, a, b, sem, val):
-        idx[0] += 1
-        acc.setdefault(name, []).append({"cols": bits(a, b), "w": True, "q": "dma", "sem": sem, "val": val, "snap": {}, "idx": idx[0]})
+    def send(t, hop, out, src, rsem, lsem):
+        return issue("g", lambda q: _send(g, T, topo, core, hop, out, src[0], rsem, lsem), src[1], [], HOP + (FIRST if t == 0 and rsem == "xin0" else 0), lsem, NE)
+
+    def arrive(v, sem, sent, hops):
+        issue("n", None, [], v[1], (hops - 1) * ops[sent]["cost"] + WAKE, sem, NE, after=sent)
 
     def rd(*vs):
         out = []
@@ -187,52 +300,84 @@ def rank_program(g, core, T, topo):
     def outs(o):
         return o[1], (o[2] if len(o) == 3 else [])
 
+    def size(v):
+        return bin(v[1][0][1]).count("1")
+
+    def kind(v):
+        return SCRATCH[v[1][0][0]]
+
+    def cycles(n, sides, rate=None):
+        if any(len(v) == 3 for v in sides):
+            return 0.06 + n * CYCLE * (3.5 if len(sides[0]) == 3 else 1.5)
+        if rate is None:
+            rate = 0.5 if all(kind(v)[2] in (_B, _U) for v in sides) else 1
+        return max(64, n * rate) * CYCLE
+
     def tt(o, a, b, op):
-        issue("v", lambda: g.vector.tensor_tensor(ap(o), ap(a), ap(b), op), rd(a, b), o[1])
+        issue("v", lambda q: g.vector.tensor_tensor(ap(o), ap(a), ap(b), op), rd(a, b), o[1],
+              cycles(size(o), [o, a, b], 1 if "psum" in (kind(a)[0], kind(b)[0]) else 2))
 
     def ts(o, a, s1, op0, s2=None, op1=None):
-        def f():
+        def f(q):
             if op1 is None:
                 return g.vector.tensor_scalar(ap(o), ap(a), ap(s1), None, op0)
             return g.vector.tensor_scalar(ap(o), ap(a), ap(s1), ap(s2), op0, op1)
-        issue("v", f, rd(a, s1, s2), o[1])
+        issue("v", f, rd(a, s1, s2), o[1], cycles(size(o), [o, a]))
 
     def tc(o, a):
         w, r = outs(o)
-        issue("v", lambda: g.vector.tensor_copy(ap(o), ap(a)), rd(a) + r, w)
+        issue("v", lambda q: g.vector.tensor_copy(ap(o), ap(a)), rd(a) + r, w, cycles(size(a if len(o) == 3 else o), [o, a]))
+
+    def pick(o, a, q="vs"):
+        def f(q):
+            if q == "v":
+                return g.vector.tensor_copy(ap(o), ap(a))
+            return g.scalar.activation(ap(o), ap(a), AF.Copy)
+        issue(q, f, rd(a), o[1], cycles(size(o), [o, a]))
+
+    def cuts(who, l0, l1):
+        out = []
+        for a in range(l0, l1, CHUNK):
+            q = who[a // CHUNK]
+            if out and out[-1][2] == q and a % 64:
+                out[-1] = (out[-1][0], a + CHUNK, q)
+            else:
+                out.append((a, a + CHUNK, q))
+        return out
 
     def ms(o, c):
-        issue("v", lambda: g.vector.memset(ap(o), c), [], o[1])
+        issue("v", lambda q: g.vector.memset(ap(o), c), [], o[1], cycles(size(o), [o]))
 
     def scan(o, d0, d1, op0, op1, init=0.0):
-        issue("v", lambda: g.vector.tensor_tensor_scan(ap(o), ap(d0), ap(d1), ap(init), op0, op1), rd(d0, d1, init), o[1])
+        issue("v", lambda q: g.vector.tensor_tensor_scan(ap(o), ap(d0), ap(d1), ap(init), op0, op1), rd(d0, d1, init), o[1], cycles(size(o), [o, d0, d1]))
 
     def red(o, a):
-        issue("v", lambda: g.vector.tensor_reduce(ap(o), ap(a), AxisListType.X, OP.add), rd(a), o[1])
+        issue("v", lambda q: g.vector.tensor_reduce(ap(o), ap(a), AxisListType.X, OP.add), rd(a), o[1], cycles(size(a), [a], 1))
 
     def act(o, a, func=AF.Copy, bias=0.0, scale=1.0):
-        issue("s", lambda: g.scalar.activation(ap(o), ap(a), func, bias=ap(bias), scale=ap(scale)), rd(a, bias, scale), o[1])
+        issue("s", lambda q: g.scalar.activation(ap(o), ap(a), func, bias=ap(bias), scale=ap(scale)), rd(a, bias, scale), o[1], cycles(size(o), [o, a], 1))
 
-    def mm(o, l, r, start, stop):
-        issue("p", lambda: g.tensor.matmul(ap(o), ap(l), ap(r), start, stop), rd(l, r), o[1])
+    def mm(o, l, r, start, stop, after=None):
+        return issue("p", lambda q: g.tensor.matmul(ap(o), ap(l), ap(r), start, stop), rd(l, r), o[1],
+                     cycles(size(r), [r], 1) * (4 if kind(r)[2] == _F else 1), after=after)
 
     def msum(o, pairs):
         for j, (l, r) in enumerate(pairs):
             mm(o, l, r, j == 0, j == len(pairs) - 1)
 
     def iota(o, pat, base=0, cm=0):
-        def f():
-            if SCRATCH[o[1][0][0]][2] == "int32":
+        def f(q):
+            if kind(o)[2] == _I:
                 return g.iota(ap(o), pat, base, cm)
             return g.iota(ap(o), pat, base, cm, allow_small_or_imprecise_dtypes=True)
-        issue("g", f, [], o[1])
+        issue("g", f, [], o[1], 0.13 + 2 * size(o) * CYCLE)
 
-    def dma(q, out, in_, reads, writes, sem, val=16):
-        issue(q, lambda: Q[q].dma_start(out, in_), reads, writes, sem=sem, val=val, inc=16)
+    def dma(q, out, in_, reads, writes, sem, val=16, cost=LOAD, after=None):
+        return issue(q, lambda q: Q[q].dma_start(out, in_), reads, writes, cost, sem, val, 16, after)
 
-    def load(q, name, a, b, src, sem):
+    def load(q, name, a, b, src, sem, after=None):
         v = X(name, a, b)
-        dma(q, v[0], src, [], v[1], sem)
+        return dma(q, v[0], src, [], v[1], sem, cost=LOAD + (b - a) / 1400, after=after)
 
     def col(name, j):
         return X(name, j, j + 1)
@@ -241,8 +386,7 @@ def rank_program(g, core, T, topo):
         act(o, col("GH", 0), AF.Copy, bias=float(c), scale=0.0)
 
     load("s", "Z0", 0, 256, T.sd[:, :], "dsd")
-    load("y", "V0", 0, 16, T.v0[:, :], "dv0")
-    load("y", "xt", 0, 4096, T.x[:, :], "dx")
+    load("y", "xt", 0, 4096, T.x[:, :], "dx", after=load("y", "V0", 0, 16, T.v0[:, :], "dv0"))
     load("s", "THI", 0, 4, T.th[:, :], "dth")
 
     iota(X("PI"), [[0, 1]], 0, 1)
@@ -250,14 +394,13 @@ def rank_program(g, core, T, topo):
     iota(X("C8"), [[0, 16], [1, 8]])
     iota(X("TJ"), [[16, 8], [1, 2], [0, 8]])
     iota(X("CJ"), [[1, 128]])
-    iota(X("SEGM"), [[0, 64], [256, 8]])
     iota(X("GJ"), [[16, 8], [0, 16]])
     iota(X("GM"), [[16, 8], [0, 2], [1, 8]])
+    iota(X("SEGM"), [[0, 64], [256, 8]])
     iota(X("CLSR"), [[1, 4], [0, 64]])
-    iota(X("RSTP"), [[0, 128]])
-    iota(X("RSTP", 0, 128, 8), [[16, 16]], 256, 1)
-    iota(X("D", 0, WIN // 8), [[0, WIN // 8]])
 
+    ms(X("RSTP"), 0.0)
+    ms(X("RST"), 0.0)
     ms(X("xt", 4096, WIN), 0.0)
     ms(X("ZER"), 0.0)
     ms(X("ONE"), 1.0)
@@ -281,47 +424,43 @@ def rank_program(g, core, T, topo):
     ts(col("KC", 5), K2, K2, OP.mult)
     ts(X("NI"), X("CJ"), P, OP.is_equal, -1.0, OP.mult)
     ts(KM, col("KC", 5), -1.0, OP.mult, -0.25, OP.add)
-    for m in range(8):
-        const(col("KROW", 8 + m), 1.0 / REP[m] if m else 0.0)
-        const(col("KROW", 16 + m), REP[m])
+    ts(X("DC", 0, 2), X("GH", 0, 16, 8), I16, OP.is_equal, 256.0, OP.mult)
+    ts(col("DC", 2), H2, -1.0, OP.mult)
 
     tc(X("VHL", 0, 16), X("V0"))
     msum(X("PB0", 0, 128), [(X("WU%d" % h), X("Z0", h, 256, 2)) for h in range(2)])
+    ts(X("OBM"), X("C8"), M8, OP.not_equal, 2048.0, OP.mult)
     tt(X("VHL", 16, 32), X("V0"), X("VHL", 0, 16), OP.subtract)
-    act(X("S0F"), X("PB0", 0, 128), AF.Square, bias=K2, scale=0.25)
+    act(X("WS"), X("PB0", 0, 128), AF.Square, bias=K2, scale=0.25)
     act(X("LG", 512, 640), X("PB0", 0, 128))
+    ts(X("RKA"), X("CJ"), 8.0, OP.add, P, OP.is_equal)
     for e in range(8):
         ts(X("VS", e, 256, 8), X("VHL"), col("MC", e), OP.mult)
     msum(X("PB1", 0, 128), [(X("WP"), X("VS", 128 * j, 128 * j + 128)) for j in range(2)])
-    ts(X("S0I"), X("S0F"), KM, OP.add)
+    ts(X("S0I"), X("WS"), KM, OP.add)
+    ts(X("BO"), X("GJ"), G16, OP.is_equal)
     tt(X("TA"), X("S0I"), X("PB1", 0, 128), OP.add)
     ts(X("VM"), X("PB1", 0, 128), KM, OP.add)
     ts(X("TR", 0, 128), X("TA"), 4095, OP.bitwise_and)
     tc(X("TR", 256, 384), X("PB1", 0, 128))
     tc(X("LU", 0, 128), X("TR", 0, 128))
+    ts(X("RK1"), X("GM"), G16, OP.subtract, M8, OP.is_equal)
+    ts(X("NTH"), X("THI"), -1.0, OP.mult, 0.5, OP.add)
+    act(X("RKA"), X("RKA"), AF.Identity, scale=col("DC", 2))
+    act(X("OBM"), X("OBM"), bias=1024.0)
+    for h in range(2):
+        act(X("HS%d" % h), X("BO"), AF.Identity, scale=col("DC", h))
+    iota(X("RSTP", 0, 128, 8), [[16, 16]], 256, 1)
+    issue("g", lambda q: g.affine_select(T.RKF[:, :], T.RKA[:, :], [[-1, 128]], OP.not_equal, -1024.0, 0, 1), X("RKA")[1], X("RKF")[1], 0.17 + 256 * CYCLE)
+    iota(X("D", 0, WIN // 8), [[0, WIN // 8]])
     for j in range(1, 8):
         a = X("D", j * (WIN // 8), (j + 1) * (WIN // 8))
         z = X("D", 0, WIN // 8)
-        dma("y", a[0], z[0], z[1], a[1], "dz", 7 * 16)
-
-    ts(X("NTH"), X("THI"), -1.0, OP.mult, 0.5, OP.add)
-    ts(X("BO"), X("GJ"), G16, OP.is_equal)
-    ts(X("DC", 0, 2), X("GH", 0, 16, 8), I16, OP.is_equal, 256.0, OP.mult)
-    ts(col("DC", 2), H2, -1.0, OP.mult)
-    ts(X("RK1"), X("GM"), G16, OP.subtract, M8, OP.is_equal)
-    ts(X("RKA"), X("CJ"), 8.0, OP.add, P, OP.is_equal)
-    ts(X("OBM"), X("C8"), M8, OP.not_equal, 2048.0, OP.mult)
-    for h in range(2):
-        act(X("HS%d" % h), X("BO"), AF.Identity, scale=col("DC", h))
-    act(X("RKA"), X("RKA"), AF.Identity, scale=col("DC", 2))
-    act(X("OBM"), X("OBM"), bias=1024.0)
-    act(X("K4"), X("ID"), scale=4096.0)
-    a, b = X("RKF"), X("RKA")
-    issue("g", lambda: g.affine_select(a[0], b[0], [[-1, 128]], OP.not_equal, -1024.0, 0, 1), b[1], a[1])
+        dma("y", a[0], z[0], z[1] + X("xt", 0, 4096)[1], a[1], "dz", 7 * 16)
     iota(X("IS"), [[0, 16], [1, 16]])
-    iota(X("RST"), [[0, 96]])
     iota(X("RST", 0, 96, 16), [[16, 6]], DUMP, 1)
     DMP6 = X("RST", 0, 96, 16)
+    DGP = X("PB5", 416, 512)
 
     def repeats(out, u):
         act(X("DT", 0, 128), u, AF.Identity, bias=MAGIC, scale=RA)
@@ -329,6 +468,10 @@ def rank_program(g, core, T, topo):
         tt(out, X("DT", 128, 256), u, OP.is_equal)
 
     def consts_verdict():
+        for m in range(8):
+            const(col("KROW", 8 + m), 1.0 / REP[m] if m else 0.0)
+            const(col("KROW", 16 + m), REP[m])
+        act(X("K4"), X("ID"), scale=4096.0)
         tt(X("KEQ", 8, 24), X("MK8", 8, 24), X("KROW", 8, 24), OP.mult)
         ts(col("DC", 3), M8, 2.0, OP.mult, G16, OP.add)
         red(RA, X("KEQ", 8, 16))
@@ -350,19 +493,22 @@ def rank_program(g, core, T, topo):
         ms(X("RS96"), 65536.0)
         ms(X("H16"), 16.0)
         ms(X("H7"), 16.0)
-        ms(X("SM"), 0.0)
-        ms(X("SEG4"), 1.0)
+        ms(X("SM"), 0)
+        ms(X("SEG4"), 2.0 ** 25)
+        ms(X("SEG64"), 2.0 ** 25)
+        ms(X("SEG64", 0, 512, 64), NORM[0])
         ms(X("SEG7"), 1.0)
         ms(X("DNB"), 0.0)
         ms(X("RS96", 0, 96, 16), -1.0)
         ms(X("H16", 0, 18, 6), 0.0)
         ms(col("H7", 6), 3.0)
-        ms(X("SM", 6, 14, 7), NORM[0])
-        ms(col("SM", 15), NORM[0])
-        ms(X("SEG4", 0, 192, 4), 0.0)
+        for j in (6, 13, 15):
+            ms(col("SM", 2 * j + 1), int(NORM[0]))
+        ms(X("SEG4", 0, 192, 4), NORM[0])
         for j in (0, 7, 14):
-            ms(X("SEG7", j, 64, 16), 0.0)
+            ms(X("SEG7", 2 * j, 128, 32), 0.0)
         tc(X("FD", 1, 12, 2), DMP6)
+        tc(DGP, X("DG"))
 
     def consts_out():
         for e in range(8):
@@ -371,15 +517,12 @@ def rank_program(g, core, T, topo):
         ms(X("RSL"), 0.0)
         ms(X("RSL", 0, 256, 16), 1.0)
 
-    def gat(q, b, l0, l1):
-        o, i = X("GT", 8 * l0, 8 * l1), IND(X("xt"), X("LU", 128 * b + l0 // 2, 128 * b + l1 // 2))
-        if q == "v":
-            tc(o, i)
-        else:
-            act(o, i)
-
-    def smax(l0, l1):
-        scan(X("HM", 8 * l0, 8 * l1), X("SEGM", 0, 8 * (l1 - l0)), X("GT", 8 * l0, 8 * l1), OP.min, OP.max)
+    def reads(b, l0, l1):
+        for a, e, q in cuts(WHO[0 if first[0] else 1][b], l0, l1):
+            pick(X("GT", 8 * a, 8 * e), IND(X("xt"), X("LU", 128 * b + a // 2, 128 * b + e // 2)), q)
+        for a in range(l0, l1, 64):
+            e = min(a + 64, l1)
+            scan(X("HM", 8 * a, 8 * e), X("SEGM", 0, 8 * (e - a)), X("GT", 8 * a, 8 * e), OP.min, OP.max)
 
     def diff(pb, zin, l0, l1):
         msum(X(pb, 0, l1 - l0), [(X("NI"), X(zin, l0, l1)), (X("ID"), X("HM", 8 * l0 + 7, 8 * l1, 8))])
@@ -416,30 +559,31 @@ def rank_program(g, core, T, topo):
             scan(X("SML", 0, 7), X("H7"), X("DNB", 1, 14, 2), OP.mult, OP.add)
         elif step == 1:
             ts(X("MS", 0, 192), X("PB5", 0, 192), col("SML", 6), OP.add)
-            ts(X("MS", 192, 256), X("PB2", 256, 320), col("SML", 6), OP.add)
+            ts(X("MS", 192, 256), X("PB2", 320, 384), col("SML", 6), OP.add)
         elif step == 2:
             ts(X("MS", 256, 512), X("MS", 0, 256), 0x444444, OP.bitwise_and)
         else:
             ts(X("HB"), X("MS", 256, 512), 0.0, OP.is_gt)
 
-    def back(t):
-        arrive("VWIN", 0, 16, "rin%d" % t, NE)
-        tt(X("PR"), IND(X("VWIN"), X("ML", 16, 32)), X("MG"), OP.mult)
+    def back(l0, l1):
+        tt(X("PR", l0, l1), IND(X("VWIN"), X("ML", 16 + l0 // 16, 16 + l1 // 16)), X("MG", l0, l1), OP.mult)
 
-    def thaw(step):
-        o = X("PB7", 0, 128)
+    BANK = {0: (X("PB7", 0, 64), X("PB2", 0, 64), X("PB4", 128, 192)), 128: (X("PB5", 192, 256), X("PB1", 256, 320), X("PB0", 256, 320))}
+
+    def thaw(step, l0):
+        o, l1, c0, c1 = BANK[l0][0], l0 + 128, l0 // 2, l0 // 2 + 64
         if step == 0:
-            mm(o, X("ID"), X("NF"), True, False)
+            mm(o, X("ID"), X("NF", c0, c1), True, False)
             for h in range(2):
-                mm(o, X("WU%d" % h), X("HB", h, 256, 2), False, False)
+                mm(o, X("WU%d" % h), X("HB", l0 + h, l1, 2), False, False)
         elif step == 1:
             for h in range(2):
-                mm(o, X("WU%d" % h), X("PR", h, 256, 2), False, h == 1)
+                mm(o, X("WU%d" % h), X("PR", l0 + h, l1, 2), False, h == 1)
         else:
-            act(X("FR"), o, AF.Relu, bias=8192.0, scale=-8192.0)
-            act(X("NF"), X("FR"), bias=16384.0, scale=-2.0)
+            act(X("FR", c0, c1), o, AF.Relu, bias=8192.0, scale=-8192.0)
 
-    def word(pb, step, l0, l1):
+    def word(step, l0):
+        pb, l1 = "PB6" if l0 else "PB3", l0 + 128
         k0, k1 = l0 // 16, l1 // 16
         if step == 0:
             mm(X4(pb, k0, k1), X("KR2"), X("CLSR", l0, l1), True, False)
@@ -451,20 +595,28 @@ def rank_program(g, core, T, topo):
         else:
             act(X("XF", l0, l1), X4(pb, k0, k1), bias=256.0 * (4 * KAP[0] ** 2 + 0.25))
 
-    def halt(t, step, l0, l1):
-        c0, c1 = l0 // 2, l1 // 2
+    def sign(t, l0, l1):
+        act(X("GE", l0, l1), X("Z2", l0, l1), AF.Sign, bias=col("NTH", t))
+
+    def halt(t, step, l0):
+        l1, c0, c1 = l0 + 128, l0 // 2, l0 // 2 + 64
+        th, cn, off = BANK[l0]
         if step == 0:
-            act(X("GE", l0, l1), X("Z2", l0, l1), AF.Sign, bias=col("NTH", t))
+            msum(cn, [(X("WU%d" % h), X("GE", l0 + h, l1, 2)) for h in range(2)])
         elif step == 1:
-            msum(X("PB2", c0, c1), [(X("NI"), X("FR", c0, c1))] * (t > 0) + [(X("WU%d" % h), X("GE", l0 + h, l1, 2)) for h in range(2)])
+            if t:
+                ts(X("FLX", c0, c1), cn, 1.0, OP.is_lt, 65536.0, OP.mult)
+            else:
+                ts(X("FL", c0, c1), cn, 1.0, OP.is_ge)
         elif step == 2:
-            ts(X("FL", c0, c1), X("PB2", c0, c1), 1.0, OP.is_ge)
+            if t:
+                tt(X("FL", c0, c1), th, X("FLX", c0, c1), OP.is_gt)
         elif step == 3:
             scan(X("INC", c0, c1), X("FL", c0, c1), X("ZER", c0, c1), OP.add, OP.add, col("INC", c0 - 1) if c0 else -0.5)
         elif step == 4:
-            msum(X("PB4", 128 + c0, 128 + c1), [(X("ID"), X("OBM", c0, c1)), (X("RKF"), X("FL", c0, c1)), (X("RK1"), X("INC", c0, c1))])
+            msum(off, [(X("ID"), X("OBM", c0, c1)), (X("RKF"), X("FL", c0, c1)), (X("RK1"), X("INC", c0, c1))])
         elif step == 5:
-            scan(X("OS", c0, c1), X("RSTP", c0, c1), X("PB4", 128 + c0, 128 + c1), OP.max, OP.min)
+            scan(X("OS", c0, c1), X("RSTP", c0, c1), off, OP.max, OP.min)
         elif step == 6:
             tc(X("OL", l0 // 16, l1 // 16), X("OS", c0 + 7, c1, 8))
         else:
@@ -474,94 +626,48 @@ def rank_program(g, core, T, topo):
     S6 = X("FX", 207, 288, 16)
     DN = X("DNB", 1, 12, 2)
 
+    consts_verdict()
+    consts_out()
+    first = [True]
     for t in range(STAGES):
         last = t == STAGES - 1
         dst = T.cores[_partner(rank, t)]
         hop = dst if topo.may_write(core, dst) else _relay(core, T, topo)
-        gat("s", 0, 0, 64)
-        if t:
-            for j in range(3):
-                list0(j, 128, 256)
-                if j == 0:
-                    hurt(0)
-        gat("v", 0, 64, 128)
-        gat("s", 0, 128, 192)
+        hops = 1 if hop == dst else 2
+        first[0] = t == 0
         if t:
             ts(X("VM"), X("WM"), X("ACOL"), OP.add, KM, OP.add)
-        smax(0, 64)
-        smax(64, 128)
-        diff("PB0", "Z0", 0, 128)
-        gat("s", 0, 192, 224)
-        absz("PB0", "Z1", 0, 128)
-        usum("PB0", 0, 128)
-        gat("s", 0, 224, 256)
-        sq("PB0", 0, 128)
+            for j in range(4):
+                hurt(j)
+            for l0 in (0, 128):
+                thaw(0, l0)
+                back(l0, l0 + 128)
+                thaw(1, l0)
+        for j, (l0, l1) in enumerate(BATCH[0]):
+            pb = "PB%d" % (j % 2)
+            reads(0, l0, l1)
+            diff(pb, "Z0", l0, l1)
+            absz(pb, "Z1", l0, l1)
+            usum(pb, l0, l1)
+            sq(pb, l0, l1)
+            for k in range(3):
+                list1(k, l0, l1)
+        for j, (l0, l1) in enumerate(BATCH[1]):
+            pb = "PB%d" % ((j + len(BATCH[0])) % 2)
+            reads(1, l0, l1)
+            diff(pb, "Z1", l0, l1)
+            absz(pb, "Z2", l0, l1)
+            sign(t, l0, l1)
+        for l0 in (0, 128):
+            for j in range(3):
+                word(j, l0)
+            for j in range(8):
+                halt(t, j, l0)
+        sent = send(t, hop, T.XR[:, 96 * t:96 * t + 96], X("XW", 0, 96), "xin%d" % t, "xl%d" % t)
         if t:
-            hurt(1)
-        smax(128, 192)
-        list1(0, 0, 128)
-        smax(192, 256)
-        diff("PB1", "Z0", 128, 256)
-        list1(1, 0, 128)
-        if t:
-            hurt(2)
-        list1(2, 0, 128)
-        absz("PB1", "Z1", 128, 256)
-        usum("PB1", 128, 256)
-        gat("s", 1, 0, 32)
-        sq("PB1", 128, 256)
-        gat("s", 1, 32, 64)
-        word("PB3", 0, 0, 192)
-        gat("v", 1, 64, 96)
-        list1(0, 128, 256)
-        if t:
-            hurt(3)
-            thaw(0)
-        list1(1, 128, 256)
-        smax(0, 64)
-        list1(2, 128, 256)
-        gat("s", 1, 96, 128)
-        gat("s", 1, 128, 192)
-        word("PB6", 0, 192, 256)
-        if t:
-            back(t - 1)
-            thaw(1)
-            thaw(2)
-        smax(64, 128)
-        diff("PB0", "Z1", 0, 128)
-        absz("PB0", "Z2", 0, 128)
-        gat("s", 1, 192, 232)
-        gat("v", 1, 232, 256)
-        smax(128, 192)
-        diff("PB1", "Z1", 128, 192)
-        absz("PB1", "Z2", 128, 192)
-        halt(t, 0, 0, 192)
-        halt(t, 1, 0, 192)
-        word("PB3", 1, 0, 192)
-        smax(192, 256)
-        diff("PB0", "Z1", 192, 256)
-        absz("PB0", "Z2", 192, 256)
-        halt(t, 0, 192, 256)
-        word("PB3", 2, 0, 192)
-        halt(t, 2, 0, 192)
-        halt(t, 3, 0, 192)
-        halt(t, 4, 0, 192)
-        halt(t, 1, 192, 256)
-        word("PB6", 1, 192, 256)
-        word("PB6", 2, 192, 256)
-        halt(t, 5, 0, 192)
-        halt(t, 2, 192, 256)
-        halt(t, 6, 0, 192)
-        halt(t, 3, 192, 256)
-        halt(t, 4, 192, 256)
-        halt(t, 7, 0, 192)
-        for j in (5, 6, 7):
-            halt(t, j, 192, 256)
-        sv = X("XW", 0, 96)
-        issue("g", lambda: _send(g, T, topo, core, hop, T.XR[:, 96 * t:96 * t + 96], sv[0], "xin%d" % t, "xl%d" % t),
-              sv[1], [], sem="xl%d" % t, val=NE)
-        if t == 0:
-            consts_verdict()
+            thaw(2, 0)
+            thaw(2, 128)
+            act(X("NF"), X("FR"), bias=16384.0, scale=-2.0)
         msum(X("PB2", 128, 256), [(X("RKF"), X("FL")), (X("RK1"), X("INC"))])
         fr = [(X("ID"), X("FR"))] * (t > 0)
         msum(X("PB5", 256, 384), [(X("WU%d" % h), X("Z1", h, 256, 2)) for h in range(2)] + fr)
@@ -591,7 +697,7 @@ def rank_program(g, core, T, topo):
         tc(X("ML", 0, 16), X("PB7", 128, 144))
         tc(X("OI", 0, 16), X("PB7", 128, 144))
         ts(X("LGU"), X("LG", 0, 256), 4096.0, OP.min)
-        act(X("MG"), IND(X("MK"), X("ML", 0, 16)))
+        pick(X("MG"), IND(X("MK"), X("ML", 0, 16)))
         ts(X("OI", 16, 32), X("OI", 0, 16), 4, OP.logical_shift_right)
         ts(X("WI"), X("WS"), 2.0, OP.mult, -2738.25, OP.add)
         ts(X("ML", 16, 32), X("OI", 16, 32), 2.0, OP.mult, 1.0, OP.add)
@@ -602,59 +708,55 @@ def rank_program(g, core, T, topo):
             msum(X("PB7", 256, 320), [(X("PL", 128 * e, 128 * e + 128), X("LG", 256 + e, 768, 8)) for e in range(8)])
         else:
             tt(X("ZS"), X("WI"), X("S0I"), OP.add)
-        if t == 1:
-            consts_out()
-        arrive("XR", 96 * t, 96 * t + 96, "xin%d" % t, NE)
         XR = X("XR", 96 * t, 96 * t + 96)
+        arrive(XR, "xin%d" % t, sent, hops)
         ts(X("Y1"), XR, 8, OP.logical_shift_right, 0x8FFF, OP.bitwise_and)
         ts(X("CI"), XR, 21, OP.logical_shift_right)
-        tt(X("FX", 0, 96), X("Y1"), X("DG"), OP.min)
-        scan(X("FX", 96, 192), X("RS96"), X("FX", 0, 96), OP.min, OP.max)
-        tt(X("FX", 288, 384), X("CI"), X("DG"), OP.min)
+        tt(X("FX", 0, 96), X("Y1"), DGP, OP.min)
+        tt(X("FX", 288, 384), X("CI"), DGP, OP.min)
+        scan(X("PB0", 0, 96), X("RS96"), X("FX", 0, 96), OP.min, OP.max)
+        if not last:
+            ts(X("ZV"), XR, 255, OP.bitwise_and)
         pos = []
         o = 96
         for k in range(5):
             n = 80 - 16 * k
-            ts(X("E", o, o + n), X("Y1", 16 + 16 * k, 96), col("FX", 96 + 16 * k + 15), OP.is_equal)
+            ts(X("E", o, o + n), X("Y1", 16 + 16 * k, 96), col("PB0", 16 * k + 15), OP.is_equal)
             pos.append((o, n))
             o += n
-        tt(X("E", 0, 96), X("Y1"), X("FX", 96, 192), OP.is_equal)
+        tt(X("E", 0, 96), X("Y1"), X("PB0", 0, 96), OP.is_equal)
+        ts(X("FX", 544, 640), X("Y1"), 1.0 / 256, OP.mult)
         mm(X("PB4", 0, 96), X("ID"), X("OB"), True, False)
+        mm(X("PB4", 0, 96), X("HS0"), X("FX", 544, 640), False, False)
         for (o, n) in pos:
             mm(X("PB4", 96 - n, 96), X("BOK"), X("E", o, o + n), False, False)
         mm(X("PB4", 0, 96), X("BOK"), X("E", 0, 96), False, True)
         scan(X("FX", 384, 480), X("RS96"), X("FX", 288, 384), OP.min, OP.max)
-        tt(X("FX", 0, 96), X("PB4", 0, 96), X("Y1"), OP.add)
         ts(X("CM", 0, 6), X("FX", 399, 480, 16), 1.0, OP.is_ge, 7.0, OP.mult)
-        scan(X("FX", 192, 288), X("RST"), X("FX", 0, 96), OP.max, OP.min)
+        scan(X("FX", 192, 288), X("RST"), X("PB4", 0, 96), OP.max, OP.min)
         ts(X("CM", 6, 12), X("FX", 399, 480, 16), 2.0, OP.is_ge, 7.0, OP.mult)
         tc(X("DLU", 0, 6), S6)
         ts(X("CM", 12, 18), X("FX", 399, 480, 16), 3.0, OP.is_ge, 7.0, OP.mult)
         tc(IND(X("D"), X("DLU", 0, 6)), X("CODE"))
 
-        def piece(q, cl, b, l0=0, l1=64):
-            a, c = 1024 * cl + 512 * b, 128 * b + 32 * cl
-            o, i = X("G2", a + 8 * l0, a + 8 * l1), IND(X("D"), X("LGU", c + l0 // 2, c + l1 // 2))
-            if q == "v":
-                tc(o, i)
-            else:
-                act(o, i)
+        def piece(cl, b):
+            for l0, l1, q in cuts(WHO[2][b], 64 * cl, 64 * cl + 64):
+                a = 512 * (cl + b)
+                pick(X("G2", a + 8 * l0, a + 8 * l1), IND(X("D"), X("LGU", 128 * b + l0 // 2, 128 * b + l1 // 2)), q)
 
-        def sums(cl, b):
-            o = X("PB2", 256, 320) if cl == 3 else X("PB5", 64 * cl, 64 * cl + 64)
-            a = 1024 * cl + 512 * b
-            for m in range(8):
-                mm(o, X("ID"), X("G2", a + m, a + 512, 8), b == 0 and m == 0, b == 1 and m == 7)
+        def sums(o, cl, steps):
+            for b in steps:
+                a = 1024 * cl + 512 * b
+                for m in range(8):
+                    prev[0] = mm(o, X("ID"), X("G2", a + m, a + 512, 8), b == steps[0] and m == 0, b == steps[-1] and m == 7, prev[0])
 
-        for cl, b in ((0, 0), (0, 1), (1, 0), (1, 1)):
-            piece("v", cl, b, 0, 32)
-            piece("s", cl, b, 32, 64)
-            sums(cl, b)
-        for cl in (2, 3):
-            piece("v", cl, 0)
-            piece("s", cl, 1)
-            sums(cl, 0)
-            sums(cl, 1)
+        prev = [None]
+        for cl in range(4):
+            for b in range(2):
+                piece(cl, b)
+        for cl in range(3):
+            sums(X("PB5", 64 * cl, 64 * cl + 64), cl, (0, 1))
+        sums(X("PB2", 256, 320), 3, (0,))
         if last:
             act(X("UL"), X("PB7", 256, 320))
             for e in range(16):
@@ -664,37 +766,34 @@ def rank_program(g, core, T, topo):
         scan(X("CM", 18, 36), X("H16"), X("CM", 0, 18), OP.mult, OP.add)
         ts(X("SML", 8, 14), S6, 4096.0, OP.is_lt, 10.0, OP.mult)
         for j in (6, 13, 15):
-            tc(X("SM", 16 + j, 64, 16), X("CM", 23, 36, 6))
+            tc(X("SM", 32 + 2 * j + 1, 128, 32), X("CM", 23, 36, 6))
         if not last:
             tt(X("FD", 0, 12, 2), S6, DMP6, OP.subtract)
-            ts(X("ZV"), XR, 255, OP.bitwise_and)
-        scan(X("FX", 288, 480), X("SEG4"), X("PB5", 0, 192), OP.mult, OP.add)
         if not last:
             ms(X("XW", 0, 96), SENT)
-        ts(X("MS", 0, 48), X("FX", 291, 480, 4), NORM[0], OP.add)
-        scan(X("FX", 480, 544), X("SEG4", 0, 64), X("PB2", 256, 320), OP.mult, OP.add)
-        ts(X("MS", 48, 64), X("FX", 483, 544, 4), NORM[0], OP.add)
-        ts(X("MS", 64, 128), X("MS", 0, 64), NORM[1], OP.bitwise_and, 3, OP.logical_shift_right)
-        scan(X("FX", 0, 64), X("SEG7"), X("MS", 64, 128), OP.mult, OP.add)
-        tt(X("MS", 128, 192), X("FX", 0, 64), X("SM"), OP.add)
-        ts(X("MS", 192, 256), X("MS", 128, 192), NORM[1], OP.bitwise_and, 3, OP.logical_shift_right)
+        for (o, a, n, seg, src) in ((0, 256, 4, X("SEG4"), X("PB5", 0, 192)), (96, 448, 8, X("SEG64", 0, 512, 8), X("PB2", 256, 320)),
+                                    (112, 512, 64, X("SEG64"), X("G2", 3584, 4096))):
+            scan(X("MS", a, a + size(src)), seg, src, OP.min, OP.add, NORM[0])
+            ts(X("SM", o, o + 2 * size(src) // n, 2), X("MS", a + n - 1, a + size(src), n), NORM[1], OP.bitwise_and, 3, OP.logical_shift_right)
+        sums(X("PB2", 320, 384), 3, (0, 1))
+        scan(X("MS", 64, 192), X("SEG7"), X("SM"), OP.mult, OP.add)
+        ts(X("MS", 192, 256), X("MS", 65, 192, 2), NORM[1], OP.bitwise_and, 3, OP.logical_shift_right)
         scan(X("FX", 64, 128), X("MS", 192, 256), X("ZER", 0, 64), OP.add, OP.add, -float(0x666666))
         ts(X("TI", 0, 6), X("POW"), col("FX", 127), OP.mult)
         ts(X("TI", 6, 12), X("TI", 0, 6), 15, OP.bitwise_and)
         tt(DN, X("TI", 6, 12), X("SML", 8, 14), OP.is_equal)
         out = T.VWIN[:, 0:16] if hop in T.cores else T.G2[:, 16 * t:16 * t + 16]
-        dv = X("DNB")
-        issue("g", lambda: _send(g, T, topo, core, hop, out, dv[0], "rin%d" % t, "rl%d" % t), dv[1], [], sem="rl%d" % t, val=NE)
+        arrive(X("VWIN"), "rin%d" % t, send(t, hop, out, X("DNB"), "rin%d" % t, "rl%d" % t), hops)
         mm(X("PB4", 256, 262), X("ONE"), DN, True, True)
         if not last:
             scan(X("SML", 16, 28), X("DNB", 0, 12), X("FD"), OP.mult, OP.add)
             tc(X("DLU", 6, 12), X("SML", 17, 28, 2))
         red(X("ACOL"), X("PB4", 256, 262))
         if not last:
-            list0(0, 0, 128)
             tc(IND(X("xt"), X("DLU", 6, 12)), X("ZV"))
-            list0(1, 0, 128)
-            list0(2, 0, 128)
+            for l0 in (0, 128):
+                for j in range(3):
+                    list0(j, l0, l0 + 128)
 
     hurt(0)
     tt(X("TR", 0, 256), X("YQ"), X("YV"), OP.add)
@@ -707,20 +806,27 @@ def rank_program(g, core, T, topo):
     tc(X("YO"), X("MS", 0, 256))
     v = X("YO")
     dma("y", T.yt[:, :], v[0], v[1], [], "dyt")
-    tt(X("FIN", 0, 16), X("UL", 0, 16), X("OI", 0, 16), OP.subtract)
+    tt(X("YS", 32, 48), X("OI", 0, 16), X("UL", 0, 16), OP.subtract)
     o = X("PB2", 0, 256)
     mm(o, X("ID"), X("OBL"), True, False)
     mm(o, X("BO"), X("HB"), False, False)
     for h in range(2):
         mm(X("PB2", h, 256, 2), X("HS%d" % h), X("NF32"), False, False)
-    back(STAGES - 1)
+    back(0, 256)
     mm(o, X("BO"), X("PR"), False, True)
     scan(X("FX", 0, 256), X("RSL"), o, OP.max, OP.min)
+    tt(X("YS", 48, 64), X("YS", 32, 48), X("FX", 15, 256, 16), OP.mult)
     ts(X("YS", 16, 32), X("FX", 15, 256, 16), 0.0, OP.is_equal)
-    tt(X("FIN", 16, 32), X("FIN", 0, 16), X("YS", 16, 32), OP.mult)
-    tt(X("YS", 0, 16), X("FIN", 16, 32), X("OI", 0, 16), OP.add)
-    v = X("YS")
+    tt(X("YS", 0, 16), X("YS", 48, 64), X("UL", 0, 16), OP.add)
+    v = X("YS", 0, 32)
     dma("y", T.ys[:, :], v[0], v[1], [], "dys")
+
+    key = tuple(o["cost"] for o in ops if o["q"] == "n")
+    if key not in _PLANS:
+        _PLANS[key] = _plan(ops)
+    for i, q in _PLANS[key]:
+        o = ops[i]
+        emit(q, o["fn"], o["r"], o["w"], o["sem"], o["val"], o["inc"])
 
     for n, v in [("dx", 16), ("dsd", 16), ("dv0", 16), ("dth", 16), ("dz", 7 * 16), ("dyt", 16), ("dys", 16)]:
         g.wait_ge(T.sem[n], v)

from concourse.mybir import AluOpType as OP, AxisListType, ActivationFunctionType as AF

KAP = (3, 29, 71, 113, 151, 197, 233, 277)
STAGES, CAP = 4, 96
NE = 8
DUMP = 4112
WIN = 4352
SENT = 1 << 23
MAGIC = 1.5 * 2 ** 23
NORM = (float(0x777777), 0x888888)
CYCLE, WAKE, ISSUE, LOAD, HOP, FIRST = 0.0009, 0.08, 0.06, 2.0, 3.2, 2.0
AHEAD, SLACK, ROUNDS, LINE = 3, 0.02, 1, 0.9
CHUNK = 16
WHO = [['vvssssssvvssssvv', 'vvsssssvssssssvv'], ['vvsssssssssvvsvv', 'ssssssvvssssssvv'], ['vvssvvvssssvssss', 'vvssvvssvvssvvvv']]
NUDGE = {('HB', 0): 1, ('Z1', 64): 0.2, ('LU', 160): -0.5, ('PR', 0): -0.2}
BATCH = (((0, 64), (64, 128), (128, 256)), ((0, 128), (128, 192), (192, 256)))

_F, _B, _I, _U = "float32", "bfloat16", "int32", "uint16"


def _sb(n, d):
    return ("sbuf", [128, n], d)


def _twos(n):
    return 0 if n % 2 else 1 + _twos(n // 2)


REP = [0] + [4096 >> max(_twos(KAP[m] - KAP[j]) for j in range(m)) for m in range(1, 8)]

SCRATCH = {
    "xt": _sb(WIN, _B), "D": _sb(WIN, _B), "Z0": _sb(256, _B), "Z1": _sb(256, _B), "Z2": _sb(256, _B),
    "V0": _sb(16, _I), "THI": _sb(4, _I), "NTH": _sb(4, _F),
    "GT": _sb(2048, _B), "HM": _sb(2048, _B), "SEGM": _sb(512, _B), "G2": _sb(4096, _B),
    "PI": _sb(1, _I), "PT": _sb(7, _I), "PC": _sb(7, _F), "DC": _sb(8, _F), "KC": _sb(8, _F), "KROW": _sb(24, _F), "KEQ": _sb(24, _F),
    "GH": _sb(128, _F), "C8": _sb(128, _F), "TJ": _sb(128, _F), "CJ": _sb(128, _F), "GM": _sb(128, _F), "GJ": _sb(128, _F),
    "IS": _sb(256, _F), "MK8": _sb(24, _F), "MC": _sb(8, _F), "VHL": _sb(32, _B), "VS": _sb(256, _B),
    "WU0": _sb(128, _B), "WU1": _sb(128, _B), "WP": _sb(128, _B), "ID": _sb(128, _B), "NI": _sb(128, _B), "K4": _sb(128, _B),
    "BO": _sb(128, _B), "BOK": _sb(128, _B), "RK1": _sb(128, _B), "RKA": _sb(128, _B), "RKF": _sb(128, _B), "OBM": _sb(128, _B),
    "PM": _sb(128, _B), "PL": _sb(1024, _F), "HS0": _sb(128, _F), "HS1": _sb(128, _F), "KR2": _sb(128, _B), "CLSR": _sb(256, _B),
    "ONE": _sb(128, _B), "ZER": _sb(128, _B), "RSTP": _sb(128, _F),
    "DG": _sb(96, _F), "RS96": _sb(96, _F), "OB": _sb(96, _B), "RST": _sb(96, _F), "CODE": _sb(96, _B), "MK": _sb(112, _B),
    "POW": _sb(6, _F), "H16": _sb(18, _F), "H7": _sb(7, _F), "SM": _sb(128, _I), "SEG4": _sb(192, _F), "SEG64": _sb(512, _F), "SEG7": _sb(128, _B), "FLX": _sb(128, _B),
    "OBL": _sb(256, _B), "RSL": _sb(256, _F),
    "S0I": _sb(128, _I), "DUP0": _sb(128, _B), "DUP1": _sb(128, _B), "DT": _sb(256, _F),
    "SQ": _sb(128, _F), "TA": _sb(128, _I), "T1": _sb(128, _I), "TR": _sb(384, _I), "LU": _sb(256, _U), "VM": _sb(128, _F),
    "GE": _sb(256, _B), "FL": _sb(128, _B), "INC": _sb(128, _B), "OS": _sb(128, _F), "OL": _sb(16, _U),
    "XF": _sb(256, _F), "XW": _sb(640, _I), "GO": _sb(128, _B), "FR": _sb(128, _B), "NF": _sb(128, _B), "NF32": _sb(128, _F),
    "OC": _sb(16, _B), "OI": _sb(32, _I), "ML": _sb(32, _U), "MG": _sb(256, _B), "PR": _sb(256, _B), "HB": _sb(256, _B),
    "LG": _sb(768, _F), "LGU": _sb(256, _U), "WS": _sb(128, _F), "WI": _sb(128, _I), "WM": _sb(128, _I), "ZS": _sb(128, _I),
    "XR": _sb(384, _I), "VWIN": _sb(16, _B), "DNB": _sb(16, _B),
    "Y1": _sb(96, _I), "CI": _sb(96, _I), "ZV": _sb(96, _I), "E": _sb(336, _B), "FX": _sb(640, _F), "MS": _sb(1024, _I),
    "CM": _sb(36, _F), "FD": _sb(12, _F), "SML": _sb(32, _F), "TI": _sb(12, _I), "DLU": _sb(12, _U), "ACOL": _sb(1, _F),
    "UL": _sb(64, _F), "YQ": _sb(256, _F), "YV": _sb(256, _F), "YO": _sb(256, _F), "YS": _sb(64, _F),
}
for _k in range(8):
    SCRATCH["PB%d" % _k] = ("psum", [128, 32, 2, 8] if _k in (3, 6) else [128, 512], "float32")

SEMAPHORES = ["qv", "qs", "qp", "qg", "dx", "dsd", "dv0", "dth", "dz", "dyt", "dys"] + [n + str(t) for t in range(STAGES) for n in ("xin", "rin", "xl", "rl")]


def _partner(r, t):
    return r ^ (1 + t % 3)


def _relay(c, T, topo):
    r = T.rank_of(c)
    far = [T.cores[_partner(r, t)] for t in range(STAGES)]
    far = [d for d in far if not topo.may_write(c, d)]
    if not far:
        return None
    ks = [k for k in topo.cores_of(c) if k not in T.cores and topo.may_write(c, k) and all(topo.may_write(k, d) for d in far)]
    ks.sort(key=lambda k: (topo.die(k) != topo.die(c), k))
    return ks[0]


def _send(g, T, topo, src, dst, out, in_, rsem, lsem):
    eng = [e for e in topo.engines(src, dst)][:NE]
    m = 0
    for e in eng:
        m |= 1 << e
    rid, pid = topo.addr(dst, src)
    g.remote_dma(out, in_, remote_sem=T.sem[rsem], local_sem=T.sem[lsem], pid=pid, routing_id=rid, dma_engine_mask=m)


def _relay_program(g, core, T, topo, c):
    r = T.rank_of(c)
    used = []
    for t in range(STAGES):
        d = T.cores[_partner(r, t)]
        if topo.may_write(c, d):
            continue
        g.wait_ge(T.sem["xin%d" % t], NE)
        _send(g, T, topo, core, d, T.XR[:, 96 * t:96 * t + 96], T.XR[:, 96 * t:96 * t + 96], "xin%d" % t, "xl%d" % t)
        g.wait_ge(T.sem["rin%d" % t], NE)
        _send(g, T, topo, core, d, T.VWIN[:, 0:16], T.G2[:, 16 * t:16 * t + 16], "rin%d" % t, "rl%d" % t)
        used.append(t)
    for t in used:
        g.wait_ge(T.sem["xl%d" % t], NE)
        g.wait_ge(T.sem["rl%d" % t], NE)


def _plan(ops):
    n = len(ops)
    pred, succ = [{} for _ in ops], [[] for _ in ops]
    acc, bank = {}, {}
    for i, o in enumerate(ops):
        for w, regs in ((False, o["r"]), (True, o["w"])):
            for nm, cols in regs:
                for j, wj, cj in acc.get(nm, []):
                    if cj & cols and (w or wj):
                        pred[i][j] = 0
        for nm in {nm for nm, _ in o["r"] + o["w"] if nm[:2] == "PB"}:
            q, now, before = bank.get(nm, (None, [], []))
            if q == o["q"] and q != "p":
                now.append(i)
            else:
                before, now = now, [i]
            bank[nm] = (o["q"], now, before)
            for j in before:
                pred[i][j] = 0
        for j in pred[i]:
            pred[i][j] = 0 if o["q"] == "p" and ops[j]["q"] == "p" else WAKE
        if o["after"] is not None:
            pred[i][o["after"]] = 0 if o["q"] in "np" else ISSUE - ops[o["after"]]["cost"]
        for j in pred[i]:
            succ[j].append(i)
        for w, regs in ((False, o["r"]), (True, o["w"])):
            for nm, cols in regs:
                acc[nm] = [r for r in acc.get(nm, []) if not w or r[2] & ~cols] + [(i, w, cols)]
    cost = [o["cost"] for o in ops]
    hold = [ISSUE if o["sem"] else o["cost"] for o in ops]
    chain = [0.0] * n
    nxt = {}
    for i in reversed(range(n)):
        chain[i] = cost[i] + max([pred[j][i] + chain[j] for j in succ[i]], default=0.0)
        if ops[i]["w"]:
            nm, cols = ops[i]["w"][0]
            chain[i] += NUDGE.get((nm, (cols & -cols).bit_length() - 1), 0)
            if nm in ("GT", "G2"):
                if (nm, ops[i]["q"]) in nxt:
                    chain[i] = max(chain[i], chain[nxt[nm, ops[i]["q"]]] + LINE * cost[i])
                nxt[nm, ops[i]["q"]] = i

    def walk(pred, succ, chain):
        left, ready, done, end = [len(p) for p in pred], [0.0] * n, [False] * n, [0.0] * n
        free = {q: 0.0 for q in "gvspyn"}
        avail, order, now = [i for i in range(n) if not left[i]], [], 0.0
        while avail:
            soon = {i: ready[i] for i in avail}
            edge = avail
            for _ in range(AHEAD):
                edge = {j for i in edge for j in succ[i] if all(done[k] or k in soon for k in pred[j])}
                for j in edge:
                    soon[j] = max([ready[j]] + [max(soon[k], now, min(free[q] for q in ops[k]["q"])) + cost[k] + pred[j][k] for k in pred[j] if not done[k]])
            took = []
            for q in "npsgyv":
                if free[q] > now:
                    continue
                mine = [j for j in soon if ops[j]["q"] == q and soon[j] > now]
                for i in sorted((i for i in avail if q in ops[i]["q"] and ready[i] <= now), key=lambda i: (-chain[i], i)):
                    if q == "n" or not any(soon[j] < now + hold[i] and max(soon[j] + chain[j], soon[j] + hold[j] + chain[i]) < now + hold[i] + chain[j] - SLACK
                                           for j in mine if chain[j] > chain[i]):
                        took.append(i)
                        order.append((i, q))
                        avail.remove(i)
                        if q != "n":
                            free[q] = now + hold[i]
                        break
            for i in took:
                done[i], end[i] = True, now + cost[i]
                for j in succ[i]:
                    left[j] -= 1
                    ready[j] = max(ready[j], end[i] + pred[j][i])
                    if not left[j]:
                        avail.append(j)
            if not took:
                now = min([x for x in list(free.values()) + [ready[i] for i in avail] if x > now])
        return order, end

    back_pred = [{j: pred[j][i] for j in succ[i]} for i in range(n)]
    back_succ = [list(p) for p in pred]
    best = walk(pred, succ, chain)
    now = best
    for _ in range(ROUNDS):
        now = walk(pred, succ, walk(back_pred, back_succ, now[1])[1])
        if max(now[1]) < max(best[1]):
            best = now
    return best[0]


_PLANS = {}


def rank_program(g, core, T, topo):
    rank = T.rank_of(core)
    if rank is None:
        for c in T.cores:
            if core in topo.cores_of(c) and _relay(c, T, topo) == core:
                _relay_program(g, core, T, topo, c)
        return

    Q = {"v": g.vector, "s": g.scalar, "p": g.tensor, "g": g, "y": g.sync}
    CNT = {"v": 0, "s": 0, "p": 0, "g": 0}
    clk = {q: {} for q in Q}
    acc = {}
    idx = [0]

    def bits(a, b, st=1):
        return (1 << b) - (1 << a) if st == 1 else sum(1 << j for j in range(a, b, st))

    def X(name, a=0, b=None, st=1):
        n = SCRATCH[name][1][1]
        b = n if b is None else b
        return (T[name][:, a:b:st] if st != 1 else T[name][:, a:b], [(name, bits(a, b, st))])

    def X4(name, k0, k1, h=None):
        if h is None:
            return (T[name][:, k0:k1], [(name, bits(16 * k0, 16 * k1))])
        return (T[name][:, k0:k1, h, :], [(name, sum(255 << (16 * k + 8 * h) for k in range(k0, k1)))])

    def IND(win, off):
        return (win[0].indirect(off[0]), win[1], off[1])

    def wait(q, rec):
        if clk[q].get(rec["sem"], 0) >= rec["val"]:
            return
        Q[q].wait_ge(T.sem[rec["sem"]], rec["val"])
        for k, n in rec["snap"].items():
            if clk[q].get(k, 0) < n:
                clk[q][k] = n
        clk[q][rec["sem"]] = rec["val"]

    ops = []

    def issue(q, fn, reads, writes, cost, sem=None, val=None, inc=0, after=None):
        ops.append({"q": q, "fn": fn, "r": reads, "w": writes, "cost": cost, "sem": sem, "val": val, "inc": inc, "after": after})
        return len(ops) - 1

    def emit(q, fn, reads, writes, sem, val, inc):
        if q == "n":
            idx[0] += 1
            for (nm, cols) in writes:
                acc.setdefault(nm, []).append({"cols": cols, "w": True, "q": "dma", "sem": sem, "val": val, "snap": {}, "idx": idx[0]})
            return
        lab = q if sem is None else "dma"
        deps = []
        for kind, regs in (("r", reads), ("w", writes)):
            for (nm, cols) in regs:
                ps = nm[:2] == "PB"
                for rec in acc.get(nm, []):
                    clash = rec["cols"] & cols and (rec["w"] or kind == "w")
                    if rec["q"] == lab and lab != "dma":
                        if clash and not (ps and q == "p"):
                            deps.append(rec)
                    elif ps or clash:
                        deps.append(rec)
        deps.sort(key=lambda r: -r["idx"])
        for rec in deps:
            wait(q, rec)
        ins = fn(q)
        if sem is None:
            CNT[q] += 1
            ins.then_inc(T.sem["q" + q], 1)
            s, n = "q" + q, CNT[q]
        else:
            s, n = sem, val
            if inc:
                ins.then_inc(T.sem[sem], inc)
        snap = dict(clk[q])
        idx[0] += 1
        for w, regs in ((False, reads), (True, writes)):
            for (nm, cols) in regs:
                old = acc.get(nm, [])
                if w:
                    old = [r for r in old if r["cols"] & ~cols]
                else:
                    old = [r for r in old if r["w"] or r["q"] != lab or lab == "dma" or r["cols"] & ~cols]
                old.append({"cols": cols, "w": w, "q": lab, "sem": s, "val": n, "snap": snap, "idx": idx[0]})
                acc[nm] = old

    def send(t, hop, out, src, rsem, lsem):
        return issue("g", lambda q: _send(g, T, topo, core, hop, out, src[0], rsem, lsem), src[1], [], HOP + (FIRST if t == 0 and rsem == "xin0" else 0), lsem, NE)

    def arrive(v, sem, sent, hops):
        issue("n", None, [], v[1], (hops - 1) * ops[sent]["cost"] + WAKE, sem, NE, after=sent)

    def rd(*vs):
        out = []
        for v in vs:
            if isinstance(v, tuple):
                out += v[1]
                if len(v) == 3:
                    out += v[2]
        return out

    def ap(v):
        return v[0] if isinstance(v, tuple) else v

    def outs(o):
        return o[1], (o[2] if len(o) == 3 else [])

    def size(v):
        return bin(v[1][0][1]).count("1")

    def kind(v):
        return SCRATCH[v[1][0][0]]

    def cycles(n, sides, rate=None):
        if any(len(v) == 3 for v in sides):
            return 0.06 + n * CYCLE * (3.5 if len(sides[0]) == 3 else 1.5)
        if rate is None:
            rate = 0.5 if all(kind(v)[2] in (_B, _U) for v in sides) else 1
        return max(64, n * rate) * CYCLE

    def tt(o, a, b, op):
        issue("v", lambda q: g.vector.tensor_tensor(ap(o), ap(a), ap(b), op), rd(a, b), o[1],
              cycles(size(o), [o, a, b], 1 if "psum" in (kind(a)[0], kind(b)[0]) else 2))

    def ts(o, a, s1, op0, s2=None, op1=None):
        def f(q):
            if op1 is None:
                return g.vector.tensor_scalar(ap(o), ap(a), ap(s1), None, op0)
            return g.vector.tensor_scalar(ap(o), ap(a), ap(s1), ap(s2), op0, op1)
        issue("v", f, rd(a, s1, s2), o[1], cycles(size(o), [o, a]))

    def tc(o, a):
        w, r = outs(o)
        issue("v", lambda q: g.vector.tensor_copy(ap(o), ap(a)), rd(a) + r, w, cycles(size(a if len(o) == 3 else o), [o, a]))

    def pick(o, a, q="vs"):
        def f(q):
            if q == "v":
                return g.vector.tensor_copy(ap(o), ap(a))
            return g.scalar.activation(ap(o), ap(a), AF.Copy)
        issue(q, f, rd(a), o[1], cycles(size(o), [o, a]))

    def cuts(who, l0, l1):
        out = []
        for a in range(l0, l1, CHUNK):
            q = who[a // CHUNK]
            if out and out[-1][2] == q and a % 64:
                out[-1] = (out[-1][0], a + CHUNK, q)
            else:
                out.append((a, a + CHUNK, q))
        return out

    def ms(o, c):
        issue("v", lambda q: g.vector.memset(ap(o), c), [], o[1], cycles(size(o), [o]))

    def scan(o, d0, d1, op0, op1, init=0.0):
        issue("v", lambda q: g.vector.tensor_tensor_scan(ap(o), ap(d0), ap(d1), ap(init), op0, op1), rd(d0, d1, init), o[1], cycles(size(o), [o, d0, d1]))

    def red(o, a):
        issue("v", lambda q: g.vector.tensor_reduce(ap(o), ap(a), AxisListType.X, OP.add), rd(a), o[1], cycles(size(a), [a], 1))

    def act(o, a, func=AF.Copy, bias=0.0, scale=1.0):
        issue("s", lambda q: g.scalar.activation(ap(o), ap(a), func, bias=ap(bias), scale=ap(scale)), rd(a, bias, scale), o[1], cycles(size(o), [o, a], 1))

    def mm(o, l, r, start, stop, after=None):
        return issue("p", lambda q: g.tensor.matmul(ap(o), ap(l), ap(r), start, stop), rd(l, r), o[1],
                     cycles(size(r), [r], 1) * (4 if kind(r)[2] == _F else 1), after=after)

    def msum(o, pairs):
        for j, (l, r) in enumerate(pairs):
            mm(o, l, r, j == 0, j == len(pairs) - 1)

    def iota(o, pat, base=0, cm=0):
        def f(q):
            if kind(o)[2] == _I:
                return g.iota(ap(o), pat, base, cm)
            return g.iota(ap(o), pat, base, cm, allow_small_or_imprecise_dtypes=True)
        issue("g", f, [], o[1], 0.13 + 2 * size(o) * CYCLE)

    def dma(q, out, in_, reads, writes, sem, val=16, cost=LOAD, after=None):
        return issue(q, lambda q: Q[q].dma_start(out, in_), reads, writes, cost, sem, val, 16, after)

    def load(q, name, a, b, src, sem, after=None):
        v = X(name, a, b)
        return dma(q, v[0], src, [], v[1], sem, cost=LOAD + (b - a) / 1400, after=after)

    def col(name, j):
        return X(name, j, j + 1)

    def const(o, c):
        act(o, col("GH", 0), AF.Copy, bias=float(c), scale=0.0)

    load("s", "Z0", 0, 256, T.sd[:, :], "dsd")
    load("y", "xt", 0, 4096, T.x[:, :], "dx", after=load("y", "V0", 0, 16, T.v0[:, :], "dv0"))
    load("s", "THI", 0, 4, T.th[:, :], "dth")

    iota(X("PI"), [[0, 1]], 0, 1)
    iota(X("GH"), [[8, 16], [0, 8]])
    iota(X("C8"), [[0, 16], [1, 8]])
    iota(X("TJ"), [[16, 8], [1, 2], [0, 8]])
    iota(X("CJ"), [[1, 128]])
    iota(X("GJ"), [[16, 8], [0, 16]])
    iota(X("GM"), [[16, 8], [0, 2], [1, 8]])
    iota(X("SEGM"), [[0, 64], [256, 8]])
    iota(X("CLSR"), [[1, 4], [0, 64]])

    ms(X("RSTP"), 0.0)
    ms(X("RST"), 0.0)
    ms(X("xt", 4096, WIN), 0.0)
    ms(X("ZER"), 0.0)
    ms(X("ONE"), 1.0)
    ms(X("KR2"), 16384.0)
    ms(X("XW", 0, 96), SENT)
    P, I16, M8, H2, G16, IH, IO = [col("PC", j) for j in range(7)]
    for j, (sh, mk) in enumerate(((0, 127), (0, 15), (0, 7), (3, 1), (0, 112), (1, 7), (0, 1))):
        ts(col("PT", j), X("PI"), sh, OP.logical_shift_right, mk, OP.bitwise_and)
    tc(X("PC"), X("PT"))
    for m in range(8):
        const(col("KROW", m), 2 * KAP[m])
    ts(X("WU0"), X("GH"), G16, OP.is_equal)
    ts(X("WU1"), X("GH"), G16, OP.subtract, 8.0, OP.is_equal)
    ts(X("MK8"), X("C8", 0, 24), M8, OP.is_equal)
    ts(X("MC"), X("C8", 0, 8), IH, OP.is_equal)
    tt(X("KEQ", 0, 8), X("MK8", 0, 8), X("KROW", 0, 8), OP.mult)
    ts(X("WP"), X("TJ"), G16, OP.subtract, IO, OP.is_equal)
    K2, KM, RA, RB, RC = [col("KC", j) for j in range(5)]
    red(K2, X("KEQ", 0, 8))
    ts(X("ID"), X("CJ"), P, OP.is_equal)
    ts(col("KC", 5), K2, K2, OP.mult)
    ts(X("NI"), X("CJ"), P, OP.is_equal, -1.0, OP.mult)
    ts(KM, col("KC", 5), -1.0, OP.mult, -0.25, OP.add)
    ts(X("DC", 0, 2), X("GH", 0, 16, 8), I16, OP.is_equal, 256.0, OP.mult)
    ts(col("DC", 2), H2, -1.0, OP.mult)

    tc(X("VHL", 0, 16), X("V0"))
    msum(X("PB0", 0, 128), [(X("WU%d" % h), X("Z0", h, 256, 2)) for h in range(2)])
    ts(X("OBM"), X("C8"), M8, OP.not_equal, 2048.0, OP.mult)
    tt(X("VHL", 16, 32), X("V0"), X("VHL", 0, 16), OP.subtract)
    act(X("WS"), X("PB0", 0, 128), AF.Square, bias=K2, scale=0.25)
    act(X("LG", 512, 640), X("PB0", 0, 128))
    ts(X("RKA"), X("CJ"), 8.0, OP.add, P, OP.is_equal)
    for e in range(8):
        ts(X("VS", e, 256, 8), X("VHL"), col("MC", e), OP.mult)
    msum(X("PB1", 0, 128), [(X("WP"), X("VS", 128 * j, 128 * j + 128)) for j in range(2)])
    ts(X("S0I"), X("WS"), KM, OP.add)
    ts(X("BO"), X("GJ"), G16, OP.is_equal)
    tt(X("TA"), X("S0I"), X("PB1", 0, 128), OP.add)
    ts(X("VM"), X("PB1", 0, 128), KM, OP.add)
    ts(X("TR", 0, 128), X("TA"), 4095, OP.bitwise_and)
    tc(X("TR", 256, 384), X("PB1", 0, 128))
    tc(X("LU", 0, 128), X("TR", 0, 128))
    ts(X("RK1"), X("GM"), G16, OP.subtract, M8, OP.is_equal)
    ts(X("NTH"), X("THI"), -1.0, OP.mult, 0.5, OP.add)
    act(X("RKA"), X("RKA"), AF.Identity, scale=col("DC", 2))
    act(X("OBM"), X("OBM"), bias=1024.0)
    for h in range(2):
        act(X("HS%d" % h), X("BO"), AF.Identity, scale=col("DC", h))
    iota(X("RSTP", 0, 128, 8), [[16, 16]], 256, 1)
    issue("g", lambda q: g.affine_select(T.RKF[:, :], T.RKA[:, :], [[-1, 128]], OP.not_equal, -1024.0, 0, 1), X("RKA")[1], X("RKF")[1], 0.17 + 256 * CYCLE)
    iota(X("D", 0, WIN // 8), [[0, WIN // 8]])
    for j in range(1, 8):
        a = X("D", j * (WIN // 8), (j + 1) * (WIN // 8))
        z = X("D", 0, WIN // 8)
        dma("y", a[0], z[0], z[1] + X("xt", 0, 4096)[1], a[1], "dz", 7 * 16)
    iota(X("IS"), [[0, 16], [1, 16]])
    iota(X("RST", 0, 96, 16), [[16, 6]], DUMP, 1)
    DMP6 = X("RST", 0, 96, 16)
    DGP = X("PB5", 416, 512)

    def repeats(out, u):
        act(X("DT", 0, 128), u, AF.Identity, bias=MAGIC, scale=RA)
        act(X("DT", 128, 256), X("DT", 0, 128), AF.Identity, bias=RC, scale=RB)
        tt(out, X("DT", 128, 256), u, OP.is_equal)

    def consts_verdict():
        for m in range(8):
            const(col("KROW", 8 + m), 1.0 / REP[m] if m else 0.0)
            const(col("KROW", 16 + m), REP[m])
        act(X("K4"), X("ID"), scale=4096.0)
        tt(X("KEQ", 8, 24), X("MK8", 8, 24), X("KROW", 8, 24), OP.mult)
        ts(col("DC", 3), M8, 2.0, OP.mult, G16, OP.add)
        red(RA, X("KEQ", 8, 16))
        red(RB, X("KEQ", 16, 24))
        ts(X("PM"), X("CJ"), col("DC", 3), OP.subtract, H2, OP.is_equal)
        ts(RC, RB, -MAGIC, OP.mult, col("MK8", 0), OP.subtract)
        ts(X("DG"), X("IS", 0, 96), I16, OP.is_equal, 65536.0, OP.mult)
        repeats(X("DUP0"), X("LG", 512, 640))
        act(X("DG"), X("DG"), bias=-1.0)
        act(X("OB"), X("DG"), bias=57343.0, scale=-1.0)
        act(X("BOK"), X("BO"), scale=8192.0)
        act(X("MK", 0, 96), X("DG"), bias=-0.25, scale=-0.25)
        for k in range(6):
            s = 16.0 ** (5 - k) / 65536
            act(X("CODE", 16 * k, 16 * k + 16), X("DG", 16 * k, 16 * k + 16), bias=s, scale=s)
            const(col("POW", k), 16.0 ** (k - 5))
        ms(X("NF"), 16384.0)
        ms(X("MK", 96, 112), 0.0)
        ms(X("RS96"), 65536.0)
        ms(X("H16"), 16.0)
        ms(X("H7"), 16.0)
        ms(X("SM"), 0)
        ms(X("SEG4"), 2.0 ** 25)
        ms(X("SEG64"), 2.0 ** 25)
        ms(X("SEG64", 0, 512, 64), NORM[0])
        ms(X("SEG7"), 1.0)
        ms(X("DNB"), 0.0)
        ms(X("RS96", 0, 96, 16), -1.0)
        ms(X("H16", 0, 18, 6), 0.0)
        ms(col("H7", 6), 3.0)
        for j in (6, 13, 15):
            ms(col("SM", 2 * j + 1), int(NORM[0]))
        ms(X("SEG4", 0, 192, 4), NORM[0])
        for j in (0, 7, 14):
            ms(X("SEG7", 2 * j, 128, 32), 0.0)
        tc(X("FD", 1, 12, 2), DMP6)
        tc(DGP, X("DG"))

    def consts_out():
        for e in range(8):
            act(X("PL", 128 * e, 128 * e + 128), X("PM"), AF.Identity, scale=col("MK8", e))
        ts(X("OBL"), X("IS"), I16, OP.not_equal)
        ms(X("RSL"), 0.0)
        ms(X("RSL", 0, 256, 16), 1.0)

    def reads(b, l0, l1):
        for a, e, q in cuts(WHO[0 if first[0] else 1][b], l0, l1):
            pick(X("GT", 8 * a, 8 * e), IND(X("xt"), X("LU", 128 * b + a // 2, 128 * b + e // 2)), q)
        for a in range(l0, l1, 64):
            e = min(a + 64, l1)
            scan(X("HM", 8 * a, 8 * e), X("SEGM", 0, 8 * (e - a)), X("GT", 8 * a, 8 * e), OP.min, OP.max)

    def diff(pb, zin, l0, l1):
        msum(X(pb, 0, l1 - l0), [(X("NI"), X(zin, l0, l1)), (X("ID"), X("HM", 8 * l0 + 7, 8 * l1, 8))])

    def absz(pb, zout, l0, l1):
        act(X(zout, l0, l1), X(pb, 0, l1 - l0), AF.Abs)

    def usum(pb, l0, l1):
        msum(X(pb, 128, 128 + (l1 - l0) // 2), [(X("WU%d" % h), X("Z1", l0 + h, l1, 2)) for h in range(2)])

    def sq(pb, l0, l1):
        act(X("SQ", l0 // 2, l1 // 2), X(pb, 128, 128 + (l1 - l0) // 2), AF.Square, bias=K2, scale=0.25)

    def list0(step, l0, l1):
        c0, c1 = l0 // 2, l1 // 2
        if step == 0:
            ts(X("TA", c0, c1), X("ZS", c0, c1), X("ACOL"), OP.add)
        elif step == 1:
            ts(X("TR", c0, c1), X("TA", c0, c1), 4095, OP.bitwise_and)
        else:
            tc(X("LU", c0, c1), X("TR", c0, c1))

    def list1(step, l0, l1):
        c0, c1 = l0 // 2, l1 // 2
        if step == 0:
            tt(X("T1", c0, c1), X("SQ", c0, c1), X("VM", c0, c1), OP.add)
        elif step == 1:
            ts(X("TR", 128 + c0, 128 + c1), X("T1", c0, c1), 4095, OP.bitwise_and)
        else:
            tc(X("LU", 128 + c0, 128 + c1), X("TR", 128 + c0, 128 + c1))

    def hurt(step):
        if step == 0:
            scan(X("SML", 0, 7), X("H7"), X("DNB", 1, 14, 2), OP.mult, OP.add)
        elif step == 1:
            ts(X("MS", 0, 192), X("PB5", 0, 192), col("SML", 6), OP.add)
            ts(X("MS", 192, 256), X("PB2", 320, 384), col("SML", 6), OP.add)
        elif step == 2:
            ts(X("MS", 256, 512), X("MS", 0, 256), 0x444444, OP.bitwise_and)
        else:
            ts(X("HB"), X("MS", 256, 512), 0.0, OP.is_gt)

    def back(l0, l1):
        tt(X("PR", l0, l1), IND(X("VWIN"), X("ML", 16 + l0 // 16, 16 + l1 // 16)), X("MG", l0, l1), OP.mult)

    BANK = {0: (X("PB7", 0, 64), X("PB2", 0, 64), X("PB4", 128, 192)), 128: (X("PB5", 192, 256), X("PB1", 256, 320), X("PB0", 256, 320))}

    def thaw(step, l0):
        o, l1, c0, c1 = BANK[l0][0], l0 + 128, l0 // 2, l0 // 2 + 64
        if step == 0:
            mm(o, X("ID"), X("NF", c0, c1), True, False)
            for h in range(2):
                mm(o, X("WU%d" % h), X("HB", l0 + h, l1, 2), False, False)
        elif step == 1:
            for h in range(2):
                mm(o, X("WU%d" % h), X("PR", l0 + h, l1, 2), False, h == 1)
        else:
            act(X("FR", c0, c1), o, AF.Relu, bias=8192.0, scale=-8192.0)

    def word(step, l0):
        pb, l1 = "PB6" if l0 else "PB3", l0 + 128
        k0, k1 = l0 // 16, l1 // 16
        if step == 0:
            mm(X4(pb, k0, k1), X("KR2"), X("CLSR", l0, l1), True, False)
            for h in range(2):
                mm(X4(pb, k0, k1, h), X("HS%d" % h), X("VM", l0 // 2, l1 // 2), False, False)
        elif step == 1:
            for h in range(2):
                mm(X4(pb, k0, k1, h), X("ID"), X("Z2", l0 + h, l1, 2), False, h == 1)
        else:
            act(X("XF", l0, l1), X4(pb, k0, k1), bias=256.0 * (4 * KAP[0] ** 2 + 0.25))

    def sign(t, l0, l1):
        act(X("GE", l0, l1), X("Z2", l0, l1), AF.Sign, bias=col("NTH", t))

    def halt(t, step, l0):
        l1, c0, c1 = l0 + 128, l0 // 2, l0 // 2 + 64
        th, cn, off = BANK[l0]
        if step == 0:
            msum(cn, [(X("WU%d" % h), X("GE", l0 + h, l1, 2)) for h in range(2)])
        elif step == 1:
            if t:
                ts(X("FLX", c0, c1), cn, 1.0, OP.is_lt, 65536.0, OP.mult)
            else:
                ts(X("FL", c0, c1), cn, 1.0, OP.is_ge)
        elif step == 2:
            if t:
                tt(X("FL", c0, c1), th, X("FLX", c0, c1), OP.is_gt)
        elif step == 3:
            scan(X("INC", c0, c1), X("FL", c0, c1), X("ZER", c0, c1), OP.add, OP.add, col("INC", c0 - 1) if c0 else -0.5)
        elif step == 4:
            msum(off, [(X("ID"), X("OBM", c0, c1)), (X("RKF"), X("FL", c0, c1)), (X("RK1"), X("INC", c0, c1))])
        elif step == 5:
            scan(X("OS", c0, c1), X("RSTP", c0, c1), off, OP.max, OP.min)
        elif step == 6:
            tc(X("OL", l0 // 16, l1 // 16), X("OS", c0 + 7, c1, 8))
        else:
            tc(IND(X("XW"), X("OL", l0 // 16, l1 // 16)), X("XF", l0, l1))

    V = X("LG", 256, 384)
    S6 = X("FX", 207, 288, 16)
    DN = X("DNB", 1, 12, 2)

    consts_verdict()
    consts_out()
    first = [True]
    for t in range(STAGES):
        last = t == STAGES - 1
        dst = T.cores[_partner(rank, t)]
        hop = dst if topo.may_write(core, dst) else _relay(core, T, topo)
        hops = 1 if hop == dst else 2
        first[0] = t == 0
        if t:
            ts(X("VM"), X("WM"), X("ACOL"), OP.add, KM, OP.add)
            for j in range(4):
                hurt(j)
            for l0 in (0, 128):
                thaw(0, l0)
                back(l0, l0 + 128)
                thaw(1, l0)
        for j, (l0, l1) in enumerate(BATCH[0]):
            pb = "PB%d" % (j % 2)
            reads(0, l0, l1)
            diff(pb, "Z0", l0, l1)
            absz(pb, "Z1", l0, l1)
            usum(pb, l0, l1)
            sq(pb, l0, l1)
            for k in range(3):
                list1(k, l0, l1)
        for j, (l0, l1) in enumerate(BATCH[1]):
            pb = "PB%d" % ((j + len(BATCH[0])) % 2)
            reads(1, l0, l1)
            diff(pb, "Z1", l0, l1)
            absz(pb, "Z2", l0, l1)
            sign(t, l0, l1)
        for l0 in (0, 128):
            for j in range(3):
                word(j, l0)
            for j in range(8):
                halt(t, j, l0)
        sent = send(t, hop, T.XR[:, 96 * t:96 * t + 96], X("XW", 0, 96), "xin%d" % t, "xl%d" % t)
        if t:
            thaw(2, 0)
            thaw(2, 128)
            act(X("NF"), X("FR"), bias=16384.0, scale=-2.0)
        msum(X("PB2", 128, 256), [(X("RKF"), X("FL")), (X("RK1"), X("INC"))])
        fr = [(X("ID"), X("FR"))] * (t > 0)
        msum(X("PB5", 256, 384), [(X("WU%d" % h), X("Z1", h, 256, 2)) for h in range(2)] + fr)
        ts(X("OC"), X("OS", 7, 128, 8), 96.0, OP.min)
        ts(X("GO"), X("PB2", 128, 256), -928.5, OP.is_ge, 8192.0, OP.mult)
        if t:
            for j in range(4):
                mm(X("PB1", 128 * j, 128 * j + 128), X("ID"), X("NF"), True, True)
            ts(X("TA"), X("WM"), X("ACOL"), OP.add)
        repeats(X("DUP1"), X("PB5", 256, 384))
        mm(X("PB7", 128, 144), X("PM"), X("OC"), True, True)
        for b in range(2):
            msum(X("PB0", 128 * b, 128 * b + 128), [(X("ID"), X("GO")), (X("K4"), X("DUP%d" % b))])
        if t:
            mm(X("PB0", 256, 384), X("ID"), X("FR"), True, True)
            ts(X("TR", 256, 384), X("TA"), 4095, OP.bitwise_and)
            tt(X("LG", 0, 512), X("LG", 0, 512), X("PB1"), OP.add)
            tc(IND(X("D"), X("DLU", 0, 6)), X("ZER", 0, 96))
            tt(X("PB0", 0, 384), X("TR"), X("PB0", 0, 384), OP.add)
            tt(X("LG", 384, 512), X("LG", 384, 512), X("PB5", 256, 384), OP.min)
            tt(X("LG", 0, 384), X("LG", 0, 384), X("PB0", 0, 384), OP.min)
        else:
            tc(V, X("TR", 256, 384))
            act(X("LG", 384, 512), X("PB5", 256, 384))
            tt(X("LG", 0, 256), X("TR", 0, 256), X("PB0", 0, 256), OP.add)
        act(X("WS"), V, AF.Square, bias=37.0, scale=0.25)
        tc(X("ML", 0, 16), X("PB7", 128, 144))
        tc(X("OI", 0, 16), X("PB7", 128, 144))
        ts(X("LGU"), X("LG", 0, 256), 4096.0, OP.min)
        pick(X("MG"), IND(X("MK"), X("ML", 0, 16)))
        ts(X("OI", 16, 32), X("OI", 0, 16), 4, OP.logical_shift_right)
        ts(X("WI"), X("WS"), 2.0, OP.mult, -2738.25, OP.add)
        ts(X("ML", 16, 32), X("OI", 16, 32), 2.0, OP.mult, 1.0, OP.add)
        ts(X("WM"), X("WI"), 4095, OP.bitwise_and)
        if last:
            act(X("NF32"), X("NF"), scale=1.0 / 256)
            tc(X("LG", 640, 768), X("WM"))
            msum(X("PB7", 256, 320), [(X("PL", 128 * e, 128 * e + 128), X("LG", 256 + e, 768, 8)) for e in range(8)])
        else:
            tt(X("ZS"), X("WI"), X("S0I"), OP.add)
        XR = X("XR", 96 * t, 96 * t + 96)
        arrive(XR, "xin%d" % t, sent, hops)
        ts(X("Y1"), XR, 8, OP.logical_shift_right, 0x8FFF, OP.bitwise_and)
        ts(X("CI"), XR, 21, OP.logical_shift_right)
        tt(X("FX", 0, 96), X("Y1"), DGP, OP.min)
        tt(X("FX", 288, 384), X("CI"), DGP, OP.min)
        scan(X("PB0", 0, 96), X("RS96"), X("FX", 0, 96), OP.min, OP.max)
        if not last:
            ts(X("ZV"), XR, 255, OP.bitwise_and)
        pos = []
        o = 96
        for k in range(5):
            n = 80 - 16 * k
            ts(X("E", o, o + n), X("Y1", 16 + 16 * k, 96), col("PB0", 16 * k + 15), OP.is_equal)
            pos.append((o, n))
            o += n
        tt(X("E", 0, 96), X("Y1"), X("PB0", 0, 96), OP.is_equal)
        ts(X("FX", 544, 640), X("Y1"), 1.0 / 256, OP.mult)
        mm(X("PB4", 0, 96), X("ID"), X("OB"), True, False)
        mm(X("PB4", 0, 96), X("HS0"), X("FX", 544, 640), False, False)
        for (o, n) in pos:
            mm(X("PB4", 96 - n, 96), X("BOK"), X("E", o, o + n), False, False)
        mm(X("PB4", 0, 96), X("BOK"), X("E", 0, 96), False, True)
        scan(X("FX", 384, 480), X("RS96"), X("FX", 288, 384), OP.min, OP.max)
        ts(X("CM", 0, 6), X("FX", 399, 480, 16), 1.0, OP.is_ge, 7.0, OP.mult)
        scan(X("FX", 192, 288), X("RST"), X("PB4", 0, 96), OP.max, OP.min)
        ts(X("CM", 6, 12), X("FX", 399, 480, 16), 2.0, OP.is_ge, 7.0, OP.mult)
        tc(X("DLU", 0, 6), S6)
        ts(X("CM", 12, 18), X("FX", 399, 480, 16), 3.0, OP.is_ge, 7.0, OP.mult)
        tc(IND(X("D"), X("DLU", 0, 6)), X("CODE"))

        def piece(cl, b):
            for l0, l1, q in cuts(WHO[2][b], 64 * cl, 64 * cl + 64):
                a = 512 * (cl + b)
                pick(X("G2", a + 8 * l0, a + 8 * l1), IND(X("D"), X("LGU", 128 * b + l0 // 2, 128 * b + l1 // 2)), q)

        def sums(o, cl, steps):
            for b in steps:
                a = 1024 * cl + 512 * b
                for m in range(8):
                    prev[0] = mm(o, X("ID"), X("G2", a + m, a + 512, 8), b == steps[0] and m == 0, b == steps[-1] and m == 7, prev[0])

        prev = [None]
        for cl in range(4):
            for b in range(2):
                piece(cl, b)
        for cl in range(3):
            sums(X("PB5", 64 * cl, 64 * cl + 64), cl, (0, 1))
        sums(X("PB2", 256, 320), 3, (0,))
        if last:
            act(X("UL"), X("PB7", 256, 320))
            for e in range(16):
                k = KAP[e % 8]
                act(X("YQ", 16 * e, 16 * e + 16), X("UL", 32 - 16 * (e // 8), 48 - 16 * (e // 8)), AF.Square, bias=2.0 * k, scale=0.25)
                act(X("YV", 16 * e, 16 * e + 16), X("UL", 0, 16), bias=-4.0 * k * k - 0.25)
        scan(X("CM", 18, 36), X("H16"), X("CM", 0, 18), OP.mult, OP.add)
        ts(X("SML", 8, 14), S6, 4096.0, OP.is_lt, 10.0, OP.mult)
        for j in (6, 13, 15):
            tc(X("SM", 32 + 2 * j + 1, 128, 32), X("CM", 23, 36, 6))
        if not last:
            tt(X("FD", 0, 12, 2), S6, DMP6, OP.subtract)
        if not last:
            ms(X("XW", 0, 96), SENT)
        for (o, a, n, seg, src) in ((0, 256, 4, X("SEG4"), X("PB5", 0, 192)), (96, 448, 8, X("SEG64", 0, 512, 8), X("PB2", 256, 320)),
                                    (112, 512, 64, X("SEG64"), X("G2", 3584, 4096))):
            scan(X("MS", a, a + size(src)), seg, src, OP.min, OP.add, NORM[0])
            ts(X("SM", o, o + 2 * size(src) // n, 2), X("MS", a + n - 1, a + size(src), n), NORM[1], OP.bitwise_and, 3, OP.logical_shift_right)
        sums(X("PB2", 320, 384), 3, (0, 1))
        scan(X("MS", 64, 192), X("SEG7"), X("SM"), OP.mult, OP.add)
        ts(X("MS", 192, 256), X("MS", 65, 192, 2), NORM[1], OP.bitwise_and, 3, OP.logical_shift_right)
        scan(X("FX", 64, 128), X("MS", 192, 256), X("ZER", 0, 64), OP.add, OP.add, -float(0x666666))
        ts(X("TI", 0, 6), X("POW"), col("FX", 127), OP.mult)
        ts(X("TI", 6, 12), X("TI", 0, 6), 15, OP.bitwise_and)
        tt(DN, X("TI", 6, 12), X("SML", 8, 14), OP.is_equal)
        out = T.VWIN[:, 0:16] if hop in T.cores else T.G2[:, 16 * t:16 * t + 16]
        arrive(X("VWIN"), "rin%d" % t, send(t, hop, out, X("DNB"), "rin%d" % t, "rl%d" % t), hops)
        mm(X("PB4", 256, 262), X("ONE"), DN, True, True)
        if not last:
            scan(X("SML", 16, 28), X("DNB", 0, 12), X("FD"), OP.mult, OP.add)
            tc(X("DLU", 6, 12), X("SML", 17, 28, 2))
        red(X("ACOL"), X("PB4", 256, 262))
        if not last:
            tc(IND(X("xt"), X("DLU", 6, 12)), X("ZV"))
            for l0 in (0, 128):
                for j in range(3):
                    list0(j, l0, l0 + 128)

    hurt(0)
    tt(X("TR", 0, 256), X("YQ"), X("YV"), OP.add)
    hurt(1)
    ts(X("OI", 16, 32), X("UL", 48, 64), X("ACOL"), OP.add)
    hurt(2)
    hurt(3)
    ts(X("MS", 0, 256), X("TR", 0, 256), 4095, OP.bitwise_and)
    ts(X("OI", 0, 16), X("OI", 16, 32), 4095, OP.bitwise_and)
    tc(X("YO"), X("MS", 0, 256))
    v = X("YO")
    dma("y", T.yt[:, :], v[0], v[1], [], "dyt")
    tt(X("YS", 32, 48), X("OI", 0, 16), X("UL", 0, 16), OP.subtract)
    o = X("PB2", 0, 256)
    mm(o, X("ID"), X("OBL"), True, False)
    mm(o, X("BO"), X("HB"), False, False)
    for h in range(2):
        mm(X("PB2", h, 256, 2), X("HS%d" % h), X("NF32"), False, False)
    back(0, 256)
    mm(o, X("BO"), X("PR"), False, True)
    scan(X("FX", 0, 256), X("RSL"), o, OP.max, OP.min)
    tt(X("YS", 48, 64), X("YS", 32, 48), X("FX", 15, 256, 16), OP.mult)
    ts(X("YS", 16, 32), X("FX", 15, 256, 16), 0.0, OP.is_equal)
    tt(X("YS", 0, 16), X("YS", 48, 64), X("UL", 0, 16), OP.add)
    v = X("YS", 0, 32)
    dma("y", T.ys[:, :], v[0], v[1], [], "dys")

    key = tuple(o["cost"] for o in ops if o["q"] == "n")
    if key not in _PLANS:
        _PLANS[key] = _plan(ops)
    for i, q in _PLANS[key]:
        o = ops[i]
        emit(q, o["fn"], o["r"], o["w"], o["sem"], o["val"], o["inc"])

    for n, v in [("dx", 16), ("dsd", 16), ("dv0", 16), ("dth", 16), ("dz", 7 * 16), ("dyt", 16), ("dys", 16)]:
        g.wait_ge(T.sem[n], v)
    for q in "vspg":
        g.wait_ge(T.sem["q" + q], CNT[q])
    for t in range(STAGES):
        for n in ("xin", "rin", "xl", "rl"):
            g.wait_ge(T.sem[n + str(t)], NE)
